import numpy as np, ml_dtypes
CORES = [2,6,10,14,18,22,26,30]
N = 8
BF = ml_dtypes.bfloat16
def gentries(a):
    return np.ascontiguousarray(a.reshape(8, 16, -1).transpose(0, 2, 1)).reshape(8, -1)
def gtable(e):
    e = np.asarray(e); return np.ascontiguousarray(e.reshape(8, -1, 16).transpose(0, 2, 1)).reshape(128, -1).astype(np.int32)
W, F, C, K, TV, R = 4096, 2048, 256, 6, 2, 16
def num(l, b, t):
    return ((l * b >> 5) + l + 37 * b + 77 * t) & (F - 1)
def parts(rng):
    x = rng.integers(0, 16, (N, 8, 16, W)); fa = rng.integers(0, W, (N, 8, 16, F))
    l = rng.integers(0, W, (N, 8, K, C)); u = np.stack([rng.integers(-1, k, (N, 8, C)) for k in range(K)], axis=2)
    return x, fa, l, u, rng.integers(0, W, (N, 8, C)), rng.integers(36, 76, (N, 8, K)), rng.integers(0, 16, (N, 8, 16))
def pack(x, fa, l, u, e, th, w):
    return {"xs": np.ascontiguousarray(x.reshape(N, 128, W)).astype(np.float32).astype(BF), "fa": np.ascontiguousarray(fa.reshape(N, 128, F)).astype(np.int32),
            "lc": np.stack([gtable(a.reshape(8, -1)) for a in l]), "up": np.stack([gtable(a.reshape(8, -1)) for a in u]), "ex": np.stack([gtable(a) for a in e]),
            "th": np.ascontiguousarray(th).astype(np.int32), "wt": np.ascontiguousarray(w.reshape(N, 128, 1)).astype(np.int32)}
def setup_inputs(rng):
    return pack(*parts(rng))
def setup_inputs_spread(rng):
    x, fa, l, u, e, th, w = parts(rng)
    x = np.minimum((np.exp2(4 * rng.random((N, 8, 1, W))) * rng.random((N, 8, 16, W))).astype(np.int64), 15)
    a = rng.choice(np.array([1, 2, 4]), (N, 8, 1, 1))
    fa = np.minimum((W * rng.random(fa.shape) ** a).astype(np.int64), W - 1); l = np.minimum((W * rng.random(l.shape) ** a).astype(np.int64), W - 1)
    e = np.minimum((W * rng.random(e.shape) ** a[..., 0]).astype(np.int64), W - 1)
    th = np.minimum(np.exp2(8 * rng.random(th.shape)).astype(np.int64) - 1, 255); w = np.minimum(np.exp2(4 * rng.random(w.shape)).astype(np.int64) - 1, 15)
    return pack(x, fa, l, u, e, th, w)
def setup_inputs_ends(rng):
    x, fa, l, u, e, th, w = parts(rng)
    kind = rng.integers(0, 4, (N, 8, 1, W)); x = np.where(kind == 0, 0, np.where(kind == 1, 15, 15 * rng.integers(0, 2, x.shape)))
    x[..., 0] = 0; x[..., W - 1] = 15
    kind = rng.integers(0, 4, (N, 8, 1, F)); end = (W - 1) * rng.integers(0, 2, fa.shape)
    fa = np.where(kind == 0, 0, np.where(kind == 1, W - 1, np.where((kind == 2) | (rng.random(fa.shape) < 0.5), end, fa)))
    l = np.where(rng.random(l.shape) < 0.85, (W - 1) * rng.integers(0, 2, l.shape), l)
    e = np.where(rng.random(e.shape) < 0.85, (W - 1) * rng.integers(0, 2, e.shape), e)
    u = np.where(rng.random(u.shape) < 0.6, -1, np.arange(K)[:, None] - 1)
    th = 255 * rng.integers(0, 2, th.shape); th[:, 0, 0] = 0; th[:, 7] = 255
    w = 15 * rng.integers(0, 2, w.shape); w[:, 0] = 0; w[:, 7] = 15
    e[:, :, C - 1] = W - 1; l[:, :, 0, C - 1] = W - 1; l[:, :, 1, C - 1] = 0; u[:, :, 1, C - 1] = -1; u[:, :, K - 1, 0] = K - 2
    n0, n1 = num(W - 1, W - 1, 0), num(0, W - 1, 0)
    for g in (3, 7):
        x[:, g, :, 1:4] = 0; fa[:, g, :, n0] = rng.integers(0, 4, (N, 16)); fa[:, g, 0, n0] = 3; fa[:, g, 1, n0] = 0; fa[:, g, :, n1] = W - 1
    return pack(x, fa, l, u, e, th, w)
def setup_inputs_corners(rng):
    x, fa, l, u, e, th, w = parts(rng); k = np.arange(K)[:, None]
    for s in range(N):
        for g in range(8):
            m = (g + s) % 8
            if m == 0: u[s, g] = k - 1; th[s, g] = 255; th[s, g, 0] = 0
            if m == 1: u[s, g] = k - 1; th[s, g] = 255
            if m == 2: u[s, g] = -1; th[s, g] = rng.choice(np.array([0, 255]), K); w[s, g] = 0
            if m == 3: u[s, g] = k - 1; th[s, g] = 255; th[s, g, K - 1] = 0; w[s, g] = 15
            if m == 4: u[s, g] = np.minimum(k - 1, 0)
            if m == 5: x[s, g] = rng.integers(0, 16, W); th[s, g] = rng.choice(np.array([0, 1, 16, 17, 32]), K)
            if m == 6: x[s, g] = x[s, g][:, rng.integers(0, 8, W)]
            if m == 7:
                fa[s, g] = fa[s, g, :1].copy(); fa[s, g, :, ::4] = rng.choice(np.array([0, W - 1, W // 2, W // 2 + 1]), (16, F // 4))
                e[s, g] = rng.choice(np.array([0, W - 1, W // 2, 1]), C); l[s, g, ::2] = e[s, g]; th[s, g] = rng.integers(60, 110, K)
    return pack(x, fa, l, u, e, th, w)
def setup_inputs_crowd(rng):
    x, fa, l, u, e, th, w = parts(rng)
    for s in (0, 2):
        for g in range(8):
            x[s, g, :, :8] = 0; o = np.argsort(np.sum(x[s, g], axis=0)); e[s, g] = rng.choice(o[W // 2:], C); one = s == 2 and g == 7
            if one: l[s, g, K - 1, C - 1] = e[s, g, C - 1]; u[s, g, K - 1, C - 1] = -1; th[s, g] = 1
            n = num(l[s, g], e[s, g], 0)
            fa[s, g][:, n.reshape(-1)] = rng.integers(0, 8, (16, K * C))
            if one: fa[s, g, int(rng.integers(0, 16)), n[K - 1, C - 1]] = e[s, g, C - 1]
    for s in range(1, N, 2):
        for g in (0, 4):
            e[s, g] = int(e[s, g, 0]); l[s, g] = l[s, g, :, :1].copy(); u[s, g] = u[s, g, :, :1].copy()
        l[s, 4, :, C - 1] = rng.integers(0, W, K)
    if N > 5: th[5] = 255
    return pack(x, fa, l, u, e, th, w)
def setup_inputs_brink(rng):
    x, fa, l, u, e, th, w = parts(rng); al = np.arange(W); odd = np.arange(1, C, 2)
    pq = np.array([[3, 21], [21, 3], [5, 19], [19, 5], [7, 9], [9, 7]])
    for s in range(N):
        for g in range(8):
            m = (g + s) % 8
            if m < 3: u[s, g] = np.arange(K)[:, None] - 1; th[s, g] = 255
            if m == 0:
                used = np.zeros(F, bool)
                for i in range(C):
                    n = num(al, int(e[s, g, i]), 0); room = np.flatnonzero(~used[n])
                    if len(room) == 0: e[s, g, i] = 0; n = num(al, 0, 0); room = np.flatnonzero(~used[n])
                    v = int(room[int(rng.integers(0, len(room)))]); l[s, g, 0, i] = v; used[n[v]] = True
            if m == 1:
                lo = 512 * int(rng.integers(0, W // 512)); d = int(rng.integers(0, 512)); v = lo + d
                fa[s, g] = lo + rng.integers(0, 512, (16, F)); x[s, g, :, v] = 15
                e[s, g, C - 1] = v; l[s, g, 0, C - 1] = v; n = num(v, v, 0)
                fa[s, g, :15, n] = lo + ((d + rng.integers(1, 512, 15)) & 511); fa[s, g, 15, n] = v
            if m == 2:
                j = pq[rng.integers(0, 6, len(odd))]; l[s, g, 0, odd] = W - j[:, 0]; e[s, g, odd] = W - j[:, 1]
            if m == 3 or m == 4:
                o = rng.permutation(W)[:192]; x[s, g][:, o[:128]] = 0; x[s, g][rng.integers(0, 16, 64), o[64:128]] = 1; x[s, g][:, o[128:]] = 15
                e[s, g, odd] = rng.choice(o[128:], len(odd)); u[s, g][:, odd] = -1
                n = num(l[s, g][:, odd], e[s, g, odd], 0).reshape(-1); c = rng.choice(o[:64], (16, F))
                if m == 4:
                    hit = rng.random((16, F)) < 0.25; hit[0] = False; hit[15] = True
                    c = np.where(hit, rng.choice(o[64:128], (16, F)), c)
                fa[s, g][:, n] = c[:, n]
                th[s, g] = np.resize(np.array([240, 241, 239]) if m == 3 else np.array([240, 239, 241]), K)
    return pack(x, fa, l, u, e, th, w)
def check_inputs(d):
    bad = []
    for k, lo, hi in (("xs", 0, 15), ("fa", 0, W - 1), ("lc", 0, W - 1), ("up", -1, K - 2), ("ex", 0, W - 1), ("th", 0, 255), ("wt", 0, 15)):
        v = np.asarray(d[k]).astype(np.float32)
        if not (np.min(v) >= lo and np.max(v) <= hi): bad.append("range of " + k)
        if k == "xs" and np.any(v != np.floor(v)): bad.append("whole numbers in xs")
    u = np.stack([gentries(a) for a in np.asarray(d["up"])]).reshape(N, 8, K, C)
    if np.any(u > np.arange(K)[:, None] - 1): bad.append("inputs in up that are not rows before")
    return bad
def reference(xs, fa, lc, up, ex, th, wt):
    X = xs.astype(np.float32).astype(np.int32).reshape(N, 8, 16, W); FC = fa.astype(np.int64).reshape(N, 8, 16, F)
    L = np.stack([gentries(a) for a in lc]).astype(np.int64).reshape(N, 8, K, C); U = np.stack([gentries(a) for a in up]).astype(np.int64).reshape(N, 8, K, C)
    E = np.stack([gentries(a) for a in ex]).astype(np.int64); H = th.astype(np.int64); V = wt.astype(np.int64).reshape(N, 8, 16, 1)
    A = np.zeros(N, np.int64)
    for t in range(TV):
        deaths = np.zeros(N, np.int64)
        for s in range(N):
            r = (s - t) % N; l, u, x = L[r], U[r], X[s]
            beta = np.zeros((8, K + 1, C), np.int64); beta[:, 0] = E[s]
            live = np.ones((8, K + 1, C), bool); y = np.zeros((8, 16, C), np.int32)
            for k in range(K):
                j = u[:, k:k + 1] + 1
                b = np.take_along_axis(beta, j, 1)[:, 0]; ok = np.take_along_axis(live, j, 1)[:, 0]
                c = np.take_along_axis(FC[s], num(l[:, k], b, t)[:, None, :], 2)
                q = np.maximum(np.take_along_axis(x, l[:, k:k + 1], 2), np.take_along_axis(x, b[:, None, :], 2))
                v = np.take_along_axis(x, np.ascontiguousarray(c.transpose(0, 2, 1)).reshape(8, 1, 16 * C), 2).reshape(8, 16, C, 16)
                dist = np.add.reduce(np.abs(v - q[..., None]), axis=1)
                m = np.argmin(dist, axis=2)
                ok = ok & (np.min(dist, axis=2) < H[s][:, k:k + 1] + A[s])
                beta[:, k + 1] = np.take_along_axis(c, m[:, None, :], 1)[:, 0]; live[:, k + 1] = ok
                y = np.maximum(y, np.where(ok[:, None, :], np.take_along_axis(x, beta[:, k + 1:k + 2], 2), 0))
            place = R * np.arange(C) + (np.add.reduce(V[s] * y, axis=1) & (R - 1))
            np.put_along_axis(x, np.repeat(place[:, None, :], 16, axis=1), y, 2)
            last = np.zeros((8, C), np.int64)
            for k in range(K):
                p = np.take_along_axis(beta, last[:, None, :], 1)[:, 0]; dead = ~live[:, k + 1]
                l[:, k] = np.where(dead, ((l[:, k] * p >> 5) + 37 * p + k) & (W - 1), l[:, k])
                u[:, k] = np.where(dead, last - 1, u[:, k])
                last = np.where(dead, last, k + 1)
            deaths[s] = np.count_nonzero(~live)
        A = deaths & 31
    return {"yl": np.stack([gtable(a.reshape(8, -1)) for a in L]).astype(np.float32), "yi": np.stack([gtable(a.reshape(8, -1)) for a in U]).astype(np.float32),
            "yx": X.reshape(N, 128, W).astype(np.float32).astype(BF)}

@@ -1,0 +1,556 @@
+from concourse.bass import DstId, RemoteDMATransfer
+from concourse.mybir import AluOpType as ALU, AxisListType, ActivationFunctionType as ACT
+
+CFG = {"cuts": [("dve", 0, 44), ("act", 44, 64), ("dve", 64, 80), ("act", 80, 128)], "nu": 2, "nm": 8, "win": 0.0,
+       "cutk": {}, "seed": 1, "n1": 800, "n2": 2500}
+XO = 16
+XW = XO + 4096
+KSUB = 65536 * 166
+DW = 131072.0
+
+SCRATCH = {
+    "xa": ("sbuf", [128, XW], "bfloat16"), "xb": ("sbuf", [128, XW], "bfloat16"),
+    "fi": ("sbuf", [128, 2048], "int32"),
+    "l0": ("sbuf", [128, 96], "int32"), "i0": ("sbuf", [128, 96], "int32"),
+    "l1": ("sbuf", [128, 96], "float32"), "i1": ("sbuf", [128, 96], "float32"),
+    "l2": ("sbuf", [128, 80], "float32"), "i2": ("sbuf", [128, 80], "float32"), "r5": ("sbuf", [128, 32], "float32"),
+    "sl0": ("sbuf", [128, 80], "float32"), "si0": ("sbuf", [128, 80], "float32"), "f50": ("sbuf", [128, 32], "float32"),
+    "sl1": ("sbuf", [128, 80], "float32"), "si1": ("sbuf", [128, 80], "float32"), "f51": ("sbuf", [128, 32], "float32"),
+    "exi": ("sbuf", [128, 16], "int32"), "th8": ("sbuf", [128, 8], "int32"), "th8b": ("sbuf", [128, 8], "bfloat16"),
+    "wti": ("sbuf", [128, 4], "int32"), "wtf": ("sbuf", [128, 4], "float32"),
+    "thf": ("sbuf", [128, 8], "float32"), "thr0": ("sbuf", [128, 8], "float32"), "thr1": ("sbuf", [128, 8], "float32"),
+    "mm": ("sbuf", [128, 768], "float32"), "d0": ("sbuf", [128, 768], "float32"), "bz": ("sbuf", [128, 128], "int32"),
+    "b5": ("sbuf", [128, 16], "int32"), "yu": ("sbuf", [128, 96], "uint16"), "lu": ("sbuf", [128, 96], "uint16"),
+    "xl": ("sbuf", [128, 1536], "bfloat16"), "yy": ("sbuf", [128, 256], "bfloat16"),
+    "onb": ("sbuf", [128, 128], "bfloat16"), "idb": ("sbuf", [128, 128], "bfloat16"), "idf": ("sbuf", [128, 128], "float32"),
+    "sel": ("sbuf", [128, 128], "bfloat16"), "g8": ("sbuf", [128, 8], "bfloat16"), "bm": ("sbuf", [128, 8], "float32"),
+    "pi": ("sbuf", [128, 4], "int32"), "pa": ("sbuf", [128, 4], "int32"), "pb": ("sbuf", [128, 4], "int32"),
+    "pf": ("sbuf", [128, 8], "float32"), "ia": ("sbuf", [128, 128], "float32"), "ma": ("sbuf", [128, 128], "float32"),
+    "ix": ("sbuf", [128, 144], "float32"), "uw": ("sbuf", [128, 144], "bfloat16"), "rs": ("sbuf", [128, 128], "float32"),
+    "ic": ("sbuf", [128, 8], "float32"), "eo": ("sbuf", [128, 8], "uint16"), "po": ("sbuf", [128, 8], "uint16"),
+    "base": ("sbuf", [128, 8], "int32"), "kt": ("sbuf", [128, 96], "float32"), "ki": ("sbuf", [128, 96], "float32"),
+    "ds": ("sbuf", [128, 128], "float32"), "bf": ("sbuf", [128, 128], "float32"), "sb": ("sbuf", [128, 128], "float32"),
+    "sr": ("sbuf", [128, 128], "float32"), "bp": ("sbuf", [128, 96], "float32"), "w2": ("sbuf", [128, 96], "float32"),
+    "zr": ("sbuf", [128, 96], "int32"), "nl": ("sbuf", [128, 96], "int32"), "dl": ("sbuf", [128, 96], "float32"),
+    "aa": ("sbuf", [128, 96], "float32"), "di": ("sbuf", [128, 96], "float32"), "dead": ("sbuf", [128, 96], "bfloat16"),
+    "tl": ("sbuf", [128, 96], "float32"), "ti": ("sbuf", [128, 96], "float32"),
+    "cn": ("sbuf", [128, 4], "float32"), "ci": ("sbuf", [128, 4], "int32"), "cj": ("sbuf", [128, 4], "int32"),
+    "cf": ("sbuf", [128, 4], "float32"),
+    "pd0": ("psum", [128, 1024], "float32"), "pd1": ("psum", [128, 1024], "float32"), "pd2": ("psum", [128, 1024], "float32"),
+    "pk0": ("psum", [128, 512], "float32"), "pk1": ("psum", [128, 512], "float32"),
+}
+for _h in (0, 1):
+    for _n, _w, _t in (("pr", 64, "float32"), ("ss", 64, "float32"), ("bu", 8, "uint16"), ("zi", 8, "int32"),
+                       ("ni", 8, "int32"), ("nu", 8, "uint16"), ("cu", 128, "uint16"), ("fg", 128, "float32"),
+                       ("q", 128, "bfloat16"), ("v", 2048, "bfloat16"), ("sc", 128, "float32"),
+                       ("rx", 128, "float32"), ("kc", 8, "int32"), ("s1", 8, "int32"), ("s2", 8, "int32"),
+                       ("s3", 8, "int32"), ("pu", 8, "uint16")):
+        SCRATCH["%s_%d" % (_n, _h)] = ("sbuf", [128, _w], _t)
+    SCRATCH["a_%d" % _h] = ("sbuf", [128, 16, 128], "bfloat16")
+
+NDMA = 24
+NFIRST = 6
+SEMAPHORES = ["pe", "dve", "act", "pool"] + ["m%d" % _i for _i in range(NDMA)] + \
+             ["arr%d" % _i for _i in range(4)] + ["out%d" % _i for _i in range(4)]
+
+CY, GA, FIX, HOP, PC = 1.04, 1.56, 25.0, 80.0, 0.55
+COSTS = [(1.56, 15.0, 70.0, 0.55), (1.15, 15.0, 100.0, 0.5), (1.95, 30.0, 60.0, 0.55), (1.56, 50.0, 120.0, 0.65)]
+
+
+def build(g, core, T, topo):
+    rank = T.rank_of(core)
+    n_ranks = len(T.cores)
+    ops = []
+    ndma = [0]
+
+    def op(eng, fn, r, w, cost, kind="c", sem=None, val=0, lat=0.0, n=0, per=0):
+        ops.append({"eng": eng, "fn": fn, "r": r, "w": w, "cost": cost, "kind": kind, "sem": sem, "val": val, "lat": lat,
+                    "n": n, "per": per})
+
+    V, S, P = g.vector, g.scalar, g.tensor
+
+    def dve(fn, r, w, n, per=1.0):
+        op("dve", fn, r, w, FIX + max(64.0, n * per) * CY, n=n, per=per)
+
+    def act(fn, r, w, n, per=1.0):
+        op("act", fn, r, w, FIX + max(64.0, n * per) * CY, n=n, per=per)
+
+    def pool(fn, r, w, n):
+        op("pool", fn, r, w, 200 + 2 * n * CY)
+
+    def pe(fn, r, w, cyc):
+        op("pe", fn, r, w, cyc * PC, n=cyc)
+
+    def dma(eng, out, in_, r, w, lat, slow=False):
+        name = "m%d" % ndma[0]
+        ndma[0] += 1
+        q = {"sp": g.sync, "act": g.scalar, "pool": g}[eng]
+        if slow:
+            fn = lambda: q.dma_start(out, in_, allow_slow_non_contiguous=True)
+        else:
+            fn = lambda: q.dma_start(out, in_)
+        op(eng, fn, r, w, 60.0, "dma", name, 16, 2000.0, n=lat)
+
+    def ts(out, in0, s1, o1, s2=None, o2=None):
+        if o2 is None:
+            return lambda: V.tensor_scalar(out, in0, s1, None, o1)
+        return lambda: V.tensor_scalar(out, in0, s1, s2, o1, o2)
+
+    def tt(out, a, b, o):
+        return lambda: V.tensor_tensor(out, a, b, o)
+
+    def cp(out, a):
+        return lambda: V.tensor_copy(out, a)
+
+    def send(idx, dst, pairs, r, w):
+        eng = topo.engines(core, dst)[:8]
+        rid, pid = topo.addr(dst)[:2]
+        share = len(eng) // len(pairs)
+
+        def fn():
+            trs = []
+            for i, (src, land) in enumerate(pairs):
+                m = sum(1 << e for e in eng[i * share:(i + 1) * share])
+                trs.append(RemoteDMATransfer(dst_ids=[DstId(rid=rid, pnc=pid)], dma_engine_mask=m,
+                                             remote_sem=T.sem["arr%d" % idx], src=src, dst=land))
+            return g.remote_dma_fused(trs, local_sem=T.sem["out%d" % idx])
+        op("pool", fn, r, ["sent%d" % idx], 300.0, "send", "out%d" % idx, share * len(pairs), 2500.0)
+        op(None, None, ["sent%d" % idx], w, 0.0, "recv", "arr%d" % idx, share * len(pairs), 500.0)
+
+    dma("act", T.l0[:], T.lc[:], [], ["l0"], 150)
+    dma("act", T.exi[:], T.ex[:], [], ["exi"], 100)
+    dma("sp", T.fi[:], T.fa[:], [], ["fi0", "fi1"], 3200)
+    dma("sp", T.xa[:, XO:XW], T.xs[:], [], ["xa0", "xa1"], 3200)
+    dma("act", T.i0[:], T.up[:], [], ["i0"], 0)
+    dma("act", T.th8[0:8, 0:6], T.th[:], [], ["th8"], 0)
+
+    pool(lambda: g.iota(T.pi[:, 0:1], [[1, 1]], 0, 1), [], ["pi"], 1)
+    pool(lambda: g.iota(T.ic[:], [[1, 8]], 0, 0, allow_small_or_imprecise_dtypes=True), [], ["ic"], 8)
+    pool(lambda: g.iota(T.ia[:], [[0, 8], [1, 16]], 0, 0, allow_small_or_imprecise_dtypes=True), [], ["ia"], 128)
+    dve(lambda: V.memset(T.onb[:], 1.0), [], ["onb"], 128, 0.5)
+    dve(lambda: V.memset(T.bz[:], 1), [], ["bz0", "bz1"], 128)
+    dve(lambda: V.memset(T.mm[:], 0.0), [], ["mm0", "mm1"], 768)
+    dve(lambda: V.memset(T.d0[:], 1.0), [], ["d00", "d01"], 768)
+    dve(lambda: V.memset(T.mm[:, 6::8], -2048.0 - XO), [], ["mm0", "mm1"], 96)
+    dve(lambda: V.memset(T.mm[:, 0:128:8], 1.0), [], ["mm0"], 16)
+    dve(lambda: V.memset(T.d0[:, 0::8], 0.0), [], ["d00", "d01"], 96)
+    for name in ("xa", "xb"):
+        dve(lambda name=name: V.memset(T[name][:, 0:XO], 0.0), [], [name + "s"], 16)
+        dve(lambda name=name: V.memset(T[name][:, 1:2], 64.0), [], [name + "s"], 1)
+    dve(lambda: V.memset(T.rs[:], 0.0), [], ["rs"], 128)
+    dve(lambda: V.memset(T.rs[:, 0::16], 1.0e9), [], ["rs"], 8)
+    pool(lambda: g.affine_select(T.idb[:], T.onb[:], [[-1, 128]], ALU.is_equal, 0.0, 0, 1), ["onb"], ["idb"], 128)
+    pool(lambda: g.affine_select(T.sel[0:8, :], T.onb[0:8, :], [[1, 8], [0, 16]], ALU.is_equal, 0.0, 0, -1), ["onb"], ["sel"], 128)
+    pool(lambda: g.iota(T.ix[:], [[1, 144]], -15, 0, allow_small_or_imprecise_dtypes=True), [], ["ix"], 144)
+    pool(lambda: g.iota(T.kt[:], [[32, 6], [0, 16]], 2048 * 1184 - KSUB, 0, allow_small_or_imprecise_dtypes=True), [], ["kt"], 96)
+    pool(lambda: g.iota(T.ki[:], [[1, 6], [0, 16]], -1, 0, allow_small_or_imprecise_dtypes=True), [], ["ki"], 96)
+    dma("pool", T.wti[:, 0:1], T.wt[:], [], ["wti"], 0, slow=True)
+    dve(ts(T.pa[:, 0:1], T.pi[:, 0:1], 15, ALU.bitwise_and), ["pi"], ["pa"], 1)
+    dve(ts(T.pb[:, 0:1], T.pi[:, 0:1], 4, ALU.arith_shift_right), ["pi"], ["pb"], 1)
+    dve(cp(T.pf[:, 0:1], T.pa[:, 0:1]), ["pa"], ["pf0"], 1)
+    dve(cp(T.pf[:, 1:2], T.pb[:, 0:1]), ["pb"], ["pf1"], 1)
+    dve(ts(T.pf[:, 2:3], T.pa[:, 0:1], 8192.0, ALU.mult, XO - 16777216.0, ALU.add), ["pa"], ["pf2"], 1)
+    dve(ts(T.pf[:, 3:4], T.pb[:, 0:1], 16.0, ALU.mult), ["pb"], ["pf3"], 1)
+    dve(ts(T.pf[:, 4:5], T.pa[:, 0:1], 16.0, ALU.mult), ["pa"], ["pf4"], 1)
+    dve(ts(T.pf[:, 5:6], T.pa[:, 0:1], 8.0, ALU.mult), ["pa"], ["pf5"], 1)
+    dve(cp(T.idf[:], T.idb[:]), ["idb"], ["idf"], 128)
+    dve(ts(T.g8[:], T.ic[:], T.pf[:, 1:2], ALU.is_equal, DW, ALU.mult), ["ic", "pf1"], ["g8"], 8)
+    dve(ts(T.bm[:], T.ic[:], T.pf[:, 1:2], ALU.is_equal), ["ic", "pf1"], ["bm"], 8)
+    dve(ts(T.ma[:], T.ia[:], T.pf[:, 0:1], ALU.is_equal), ["ia", "pf0"], ["ma"], 128)
+    dve(ts(T.eo[:], T.ic[:], 16.0, ALU.mult, 15.0, ALU.add), ["ic"], ["eo"], 8)
+    dve(ts(T.po[:], T.ic[:], T.pf[:, 5:6], ALU.add), ["ic", "pf5"], ["po"], 8)
+    dve(ts(T.base[:], T.ic[:], 256.0, ALU.mult, T.pf[:, 4:5], ALU.add), ["ic", "pf4"], ["base"], 8)
+    dve(ts(T.bz[:, 0::8], T.exi[:], float(XO), ALU.add), ["exi"], ["bz0", "bz1"], 16)
+    dve(cp(T.th8b[0:8, 0:6], T.th8[0:8, 0:6]), ["th8"], ["th8b"], 6)
+    pe(lambda: P.matmul(T.pk1[:, 0:6], T.sel[0:8, :], T.th8b[0:8, 0:6], True, True), ["sel", "th8b"], ["pk1"], 64)
+    dve(ts(T.thf[:, 0:6], T.pk1[:, 0:6], -128.0, ALU.add), [], ["pk1", "thf"], 6)
+    dve(ts(T.thr0[:, 0:6], T.thf[:, 0:6], DW, ALU.mult), ["thf"], ["thr0"], 6)
+    dve(cp(T.wtf[:, 0:1], T.wti[:, 0:1]), ["wti"], ["wtf"], 1)
+    dve(ts(T.uw[:], T.ix[:], T.pf[:, 3:4], ALU.is_equal, T.wtf[:, 0:1], ALU.mult), ["ix", "pf3", "wtf"], ["uw"], 144)
+    dma("sp", T.xb[:, XO:XW], T.xs[:], ["xa0"], ["xb0", "xb1"], 3200)
+
+    ring = [0]
+    for t in (0, 1):
+        X = T.xa if t == 0 else T.xb
+        xn = "xa" if t == 0 else "xb"
+        xk = [xn + "0", xn + "1"]
+        xks = xk + [xn + "s"]
+        L, I = (T.l0, T.i0) if t == 0 else (T.l1, T.i1)
+        ka, kb = (["l0"], ["l0", "i0"]) if t == 0 else (["st1a"], ["st1a", "st1b"])
+        thr = T.thr0 if t == 0 else T.thr1
+        wadd = float(32 * 64 * 1184 + 32 * 77 * t - KSUB)
+
+        def prep(c0, c1, part, keys):
+            dve(ts(T.d0[:, 8 * c0 + 7:8 * c1:8], L[:, c0:c1], 1184.0, ALU.add), keys, ["d0%d" % part], c1 - c0)
+            dve(ts(T.mm[:, 8 * c0 + 7:8 * c1:8], L[:, c0:c1], 2080.0, ALU.mult, wadd, ALU.add), keys, ["mm%d" % part], c1 - c0)
+            dve(cp(T.lu[:, c0:c1], L[:, c0:c1]), keys, ["lu%d" % part], c1 - c0)
+
+        def xl(k0, k1, X=X, xk=xk):
+            act(lambda: S.activation(T.xl[:, 256 * k0:256 * k1], X[:, XO:XW].indirect(T.lu[:, 16 * k0:16 * k1]), ACT.Copy),
+                xk + ["lu%d" % min(k0, 1)], ["xl%d" % k for k in range(k0, k1)], 256 * (k1 - k0), GA)
+
+        prep(0, 16, 0, ka)
+        xl(0, 1)
+        if t == 1:
+            dma("sp", T.xa[:, XO:XO + 2048], T.xb[:, XO:XO + 2048], ["xb0", "sent1"], ["xa0"], 1600)
+
+        def ymax(k, c0, c1, src, keys, X=X, xks=xks):
+            hs = [h for h in (0, 1) if c0 <= 8 * h < c1]
+            uk = ["yu%d_%d" % (k, h) for h in hs]
+            yk = ["yy%d" % h for h in hs]
+            off = T.yu[:, 16 * k + c0:16 * k + c1]
+            dve(cp(off, src), keys, uk, c1 - c0)
+            o = T.yy[:, 16 * c0:16 * c1]
+            if k == 0:
+                dve(lambda: V.tensor_copy(o, X[:, 0:XW].indirect(off)), xks + uk, yk, 16 * (c1 - c0), GA)
+            else:
+                dve(lambda: V.tensor_tensor(o, X[:, 0:XW].indirect(off), o, ALU.max), xks + uk, yk, 16 * (c1 - c0), GA)
+
+        def settle(c0, c1, ol, oi, okeys, L=L, I=I, kb=kb):
+            p = "a" if c0 == 0 else "b"
+            uk = ["yu%d_%d" % (k, h) for k in range(c0 // 16, c1 // 16) for h in (0, 1)]
+            dve(ts(T.dead[:, c0:c1], T.yu[:, c0:c1], 0.0, ALU.is_equal), uk, ["dead" + p], c1 - c0)
+            dve(tt(T.tl[:, c0:c1], T.dl[:, c0:c1], T.dead[:, c0:c1], ALU.mult), ["dl", "dead" + p], ["tl" + p], c1 - c0, 2)
+            dve(tt(T.ti[:, c0:c1], T.di[:, c0:c1], T.dead[:, c0:c1], ALU.mult), ["di", "dead" + p], ["ti" + p], c1 - c0, 2)
+            dve(tt(ol, L[:, c0:c1], T.tl[:, c0:c1], ALU.add), kb + ["tl" + p], [okeys[0]], c1 - c0, 2)
+            dve(tt(oi, I[:, c0:c1], T.ti[:, c0:c1], ALU.subtract), kb + ["ti" + p], [okeys[1]], c1 - c0, 2)
+
+        for k in range(6):
+            part = min(k, 1)
+            if k == 1:
+                prep(16, 96, 1, kb)
+                for s in range(6):
+                    k0 = max(s, 1)
+                    dve(ts(T.mm[:, 128 * k0 + s::8], I[:, 16 * k0:96], float(s - 1), ALU.is_equal), kb, ["mm1"], 96 - 16 * k0)
+            if k in (1, 3):
+                xl(k, k + 2)
+            if k == 5:
+                xl(5, 6)
+            for h in (0, 1):
+                def B(n, h=h):
+                    return T["%s_%d" % (n, h)]
+
+                def K(n, h=h):
+                    return "%s_%d" % (n, h)
+                pk = T["pk%d" % h]
+                pkk = "pk%d" % h
+                c0 = 128 * k + 64 * h
+                dve(tt(B("pr")[:], T.mm[:, c0:c0 + 64], T.bz[:, 64 * h:64 * h + 64], ALU.mult),
+                    ["mm%d" % part, "bz%d" % h], [K("pr")], 64, 2)
+                dve(lambda B=B, c0=c0: V.tensor_tensor_scan(B("ss")[:], T.d0[:, c0:c0 + 64], B("pr")[:], 0.0, ALU.mult, ALU.add),
+                    ["d0%d" % part, K("pr")], [K("ss")], 64)
+                dve(cp(B("zi")[:], B("ss")[:, 7::8]), [K("ss")], [K("zi")], 8)
+                dve(ts(B("ni")[:], B("zi")[:], 5, ALU.arith_shift_right, 2047, ALU.bitwise_and), [K("zi")], [K("ni")], 8)
+                dve(cp(B("nu")[:], B("ni")[:]), [K("ni")], [K("nu")], 8)
+                dve(lambda B=B: V.tensor_copy(B("cu")[:], T.fi[:].indirect(B("nu")[:])), ["fi0", "fi1", K("nu")], [K("cu")], 128, GA)
+                dve(ts(B("bu")[:], B("ss")[:, 6::8], 2048.0 + XO, ALU.add, 1.0, ALU.max), [K("ss")], [K("bu")], 8)
+                x0 = 256 * k + 128 * h
+                dve(lambda B=B, X=X, x0=x0: V.tensor_tensor(B("q")[:], X[:, 0:XW].indirect(B("bu")[:]), T.xl[:, x0:x0 + 128], ALU.max),
+                    xks + [K("bu"), "xl%d" % k], [K("q")], 128, GA)
+                dve(ts(B("fg")[:], B("cu")[:], T.pf[:, 2:3], ALU.add), [K("cu"), "pf2"], [K("fg")], 128)
+                pe(lambda B=B, pk=pk: P.matmul(pk[:, 0:128], B("fg")[:], T.idf[:], True, False), [K("fg"), "idf"], [pkk], 512)
+                nu, nm = CFG["nu"], CFG["nm"]
+                cw = 128 // nu
+                vk = [[] for u in range(nu)]
+                for i, (eng, a, b) in enumerate(CFG["cutk"].get((k, h), CFG["cuts"])):
+                    key = K("v%d" % i)
+                    for u in range(nu):
+                        if a < cw * u + cw and b > cw * u:
+                            vk[u].append(key)
+                    o, w = B("v")[:, 16 * a:16 * b], X[:, XO:XW].indirect(B("cu")[:, a:b])
+                    if eng == "dve":
+                        dve(ts(o, w, -1.0, ALU.mult), xk + [K("cu")], [key], 16 * (b - a), GA)
+                    else:
+                        act(lambda o=o, w=w: S.activation(o, w, ACT.Copy, scale=-1.0), xk + [K("cu")], [key], 16 * (b - a), GA)
+                nb = nm * cw // 512
+                for u in range(nu):
+                    for m0 in range(0, 16, nm):
+                        slot = ring[0] % (6 // nb)
+                        ring[0] += 1
+                        pd = T["pd%d" % (slot * nb // 2)]
+                        p0 = 512 * (slot * nb % 2)
+                        pdk = "pd%d" % slot
+
+                        def fill(B=B, pd=pd, p0=p0, u=u, m0=m0):
+                            for j in range(nm):
+                                o = pd[:, p0 + cw * j:p0 + cw * j + cw]
+                                P.matmul(o, T.idb[:], B("q")[:, cw * u:cw * u + cw], True, False)
+                                ins = P.matmul(o, T.idb[:], B("v")[:, 16 * cw * u + m0 + j:16 * cw * (u + 1):16], False, True)
+                            return ins
+                        pe(fill, vk[u] + [K("q"), "idb"], [pdk], 2 * cw * nm)
+                        act(lambda B=B, pd=pd, p0=p0, u=u, m0=m0: S.activation(
+                            B("a")[:, m0:m0 + nm, cw * u:cw * u + cw], pd[:, p0:p0 + cw * nm], ACT.Abs),
+                            [], [pdk, K("a%d_%d" % (u, m0))], cw * nm)
+                for m0 in range(0, 16, nm):
+                    def lanes(B=B, pk=pk, m0=m0):
+                        for m in range(m0, m0 + nm):
+                            ins = P.matmul(pk[:, m:128:16], B("a")[:, m, :], T.g8[:], False, m == 15)
+                        return ins
+                    pe(lanes, [K("a%d_%d" % (u, m0)) for u in range(nu)] + ["g8"], [pkk], 64 * nm)
+                dve(lambda B=B, pk=pk: V.tensor_tensor_scan(B("sc")[:], T.rs[:], pk[:, 0:128], 0.0, ALU.add, ALU.min),
+                    ["rs"], [pkk, K("sc")], 128)
+                dve(lambda B=B: V.tensor_tensor(B("rx")[:], B("sc")[:].indirect(T.eo[:]), T.ma[:], ALU.mult),
+                    [K("sc"), "eo", "ma"], [K("rx")], 128, GA)
+                pe(lambda B=B, pk=pk: P.matmul(pk[:, 128:136], B("rx")[:], T.bm[:], True, True), [K("rx"), "bm"], [pkk], 256)
+                dve(ts(B("kc")[:], pk[:, 128:136], thr[:, k:k + 1], ALU.min), ["thr%d" % t], [pkk, K("kc")], 8)
+                if k < 5:
+                    dve(ts(T.bz[:, 64 * h + k + 1:64 * h + 64:8], B("kc")[:], 8191, ALU.bitwise_and), [K("kc")], ["bz%d" % h], 8)
+                    continue
+                dve(ts(T.b5[:, 8 * h:8 * h + 8], B("kc")[:], 8191, ALU.bitwise_and), [K("kc")], ["b5%d" % h], 8)
+                ymax(5, 8 * h, 8 * h + 8, T.b5[:, 8 * h:8 * h + 8], ["b5%d" % h])
+
+                def wsum(pk=pk, h=h):
+                    for a in range(16):
+                        ins = P.matmul(pk[:, 136:144], T.uw[:, 15 - a:143 - a], T.yy[:, 128 * h + a:128 * h + 128:16], a == 0, a == 15)
+                    return ins
+                pe(wsum, ["uw", "yy%d" % h], [pkk], 1024)
+                dve(cp(B("s1")[:], pk[:, 136:144]), [], [pkk, K("s1")], 8)
+                dve(ts(B("s2")[:], B("s1")[:], 15, ALU.bitwise_and), [K("s1")], [K("s2")], 8)
+                dve(tt(B("s3")[:], B("s2")[:], T.base[:], ALU.add), [K("s2"), "base"], [K("s3")], 8, 2)
+                dve(cp(B("pu")[:], B("s3")[:]), [K("s3")], [K("pu")], 8)
+                on = "xa" if (t == 1 and h == 0) else "xb"
+                w0 = XO + 2048 * h
+                dve(lambda B=B, on=on, w0=w0, h=h: V.tensor_copy(T[on][:, w0:w0 + 2048].indirect(B("pu")[:]), T.yy[:, 128 * h:128 * h + 128]),
+                    [K("pu"), "yy%d" % h], ["%s%d" % (on, h)], 128, 3.8)
+                if t == 1:
+                    if h == 0:
+                        dma("sp", T.yx[:, 0:2048], T.xa[:, w0:w0 + 2048], ["xa0"], ["yx0"], 1600)
+                    else:
+                        dma("sp", T.yx[:, 2048:4096], T.xb[:, w0:w0 + 2048], ["xb1"], ["yx1"], 1600)
+            if k < 5:
+                ymax(k, 0, 16, T.bz[:, k + 1::8], ["bz0", "bz1"])
+            if k == 4:
+                bzk = ["bz0", "bz1"]
+                dve(ts(T.ds[:], T.bz[:], 0.0, ALU.is_equal), bzk, ["ds"], 128)
+                dve(cp(T.bf[:], T.bz[:]), bzk, ["bf"], 128)
+                dve(lambda: V.tensor_tensor_scan(T.sb[:], T.ds[:], T.bf[:], 0.0, ALU.mult, ALU.add), ["ds", "bf"], ["sb"], 128)
+                dve(lambda: V.tensor_tensor_scan(T.sr[:], T.ds[:], T.ds[:], 0.0, ALU.mult, ALU.add), ["ds"], ["sr"], 128)
+                dve(lambda: V.tensor_scalar(T.bp[:], T.sb[:].indirect(T.po[:, 0:6]), -2048.0 - XO, None, ALU.add), ["sb", "po"], ["bp"], 96, GA)
+                dve(tt(T.bp[:], T.bp[:], T.d0[:, 7::8], ALU.mult), ["d00", "d01"], ["bp"], 96, 2)
+                dve(ts(T.w2[:], L[:], 2048.0, ALU.mult), kb, ["w2"], 96)
+                dve(tt(T.w2[:], T.w2[:], T.kt[:], ALU.add), ["kt"], ["w2"], 96, 2)
+                dve(tt(T.zr[:], T.bp[:], T.w2[:], ALU.add), ["bp", "w2"], ["zr"], 96, 2)
+                dve(ts(T.nl[:], T.zr[:], 5, ALU.arith_shift_right, 4095, ALU.bitwise_and), ["zr"], ["nl"], 96)
+                dve(tt(T.dl[:], T.nl[:], L[:], ALU.subtract), kb + ["nl"], ["dl"], 96, 2)
+                dve(tt(T.aa[:], T.ki[:], I[:], ALU.subtract), kb + ["ki"], ["aa"], 96, 2)
+                dve(lambda: V.tensor_tensor(T.di[:], T.sr[:].indirect(T.po[:, 0:6]), T.aa[:], ALU.subtract), ["sr", "po", "aa"], ["di"], 96, GA)
+                sl, si = T["sl%d" % t], T["si%d" % t]
+                settle(0, 80, sl[:], si[:], ["sl%d" % t, "si%d" % t])
+                if t == 0:
+                    send(0, T.cores[(rank + 1) % n_ranks], [(sl[:], T.l1[:, 0:80]), (si[:], T.i1[:, 0:80])], ["sl0", "si0"], ["st1a"])
+                else:
+                    send(2, T.cores[(rank - 1) % n_ranks], [(sl[:], T.l2[:]), (si[:], T.i2[:])], ["sl1", "si1"], ["st2a"])
+        f5 = T["f5%d" % t]
+        settle(80, 96, f5[:, 0:16], f5[:, 16:32], ["f5l%d" % t, "f5i%d" % t])
+        if t == 0:
+            send(1, T.cores[(rank + 1) % n_ranks], [(f5[:, 0:16], T.l1[:, 80:96]), (f5[:, 16:32], T.i1[:, 80:96])],
+                 ["f5l0", "f5i0"], ["st1b"])
+            pe(lambda: P.matmul(T.pk0[:, 256:352], T.onb[:], T.dead[:], True, True), ["onb", "deada", "deadb"], ["pk0"], 96)
+            dve(lambda: V.tensor_reduce(T.cn[:, 0:1], T.pk0[:, 256:352], AxisListType.X, ALU.add), [], ["pk0", "cn"], 96)
+            dve(cp(T.ci[:, 0:1], T.cn[:, 0:1]), ["cn"], ["ci"], 1)
+            dve(ts(T.cj[:, 0:1], T.ci[:, 0:1], 31, ALU.bitwise_and), ["ci"], ["cj"], 1)
+            dve(cp(T.cf[:, 0:1], T.cj[:, 0:1]), ["cj"], ["cf"], 1)
+            dve(ts(T.thr1[:, 0:6], T.thf[:, 0:6], T.cf[:, 0:1], ALU.add, DW, ALU.mult), ["cf", "thf"], ["thr1"], 6)
+        else:
+            send(3, T.cores[(rank - 1) % n_ranks], [(f5[:], T.r5[:])], ["f5l1", "f5i1"], ["st2b"])
+            dma("act", T.yl[:, 0:80], T.l2[:], ["st2a", "sc_0", "sc_1"], ["yla"], 150)
+            dma("act", T.yi[:, 0:80], T.i2[:], ["st2a", "sc_0", "sc_1"], ["yia"], 150)
+            dma("act", T.yl[:, 80:96], T.r5[:, 0:16], ["st2b"], ["ylb"], 100)
+            dma("act", T.yi[:, 80:96], T.r5[:, 16:32], ["st2b"], ["yib"], 100)
+    return ops
+
+
+def depend(ops):
+    last_w, readers, deps = {}, {}, []
+    for i, o in enumerate(ops):
+        d = set()
+        for k in o["r"]:
+            if k in last_w:
+                d.add(last_w[k])
+        for k in o["w"]:
+            if k in last_w:
+                d.add(last_w[k])
+            d.update(readers.get(k, []))
+        for k in o["r"]:
+            readers.setdefault(k, []).append(i)
+        for k in o["w"]:
+            last_w[k] = i
+            readers[k] = []
+        d.discard(i)
+        deps.append(sorted(d))
+    return deps
+
+
+def tag(o):
+    w = o["w"][-1]
+    if w[:2] in ("pd", "pk", "yu", "xl", "bz"):
+        w = w[:2]
+    elif w[-2:] in ("_0", "_1"):
+        w = w[:-2]
+    return "%s.%s" % (w, o["r"][0][:2] if o["eng"] == "pe" else "")
+
+
+def arrange(ops, deps, shift):
+    n = len(ops)
+    succ = [[] for _ in range(n)]
+    for i, d in enumerate(deps):
+        for j in d:
+            succ[j].append(i)
+    level = [0.0] * n
+    for i in range(n - 1, -1, -1):
+        level[i] = ops[i]["cost"] + ops[i]["lat"] + (ops[i]["n"] if ops[i]["kind"] == "dma" else 0.0) + max([level[j] + HOP for j in succ[i]] or [0.0])
+    level = [level[i] + shift[i] if i >= NFIRST else 1.0e9 - i for i in range(n)]
+    bus = 0.0
+    left = [len(d) for d in deps]
+    ready = [i for i in range(n) if left[i] == 0]
+    rt, end, free, order, start = [0.0] * n, [0.0] * n, {}, [], [0.0] * n
+    while ready:
+        st = {i: max(rt[i], free.get(ops[i]["eng"], 0.0)) for i in ready}
+        first = min(ready, key=lambda i: (st[i], -level[i]))
+        near = [i for i in ready if ops[i]["eng"] == ops[first]["eng"] and st[i] <= st[first] + CFG["win"]]
+        best = max(near, key=lambda i: level[i])
+        bs = st[best]
+        ready.remove(best)
+        o = ops[best]
+        start[best] = bs
+        if o["eng"]:
+            free[o["eng"]] = bs + o["cost"]
+        end[best] = bs + o["cost"] + o["lat"]
+        if o["kind"] == "dma" and o["n"]:
+            bus = end[best] = max(end[best], bus) + o["n"]
+        order.append(best)
+        for j in succ[best]:
+            same = o["eng"] == "pe" and ops[j]["eng"] == "pe"
+            rt[j] = max(rt[j], end[best] + (0.0 if same else HOP))
+            left[j] -= 1
+            if left[j] == 0:
+                ready.append(j)
+    return order, start, end
+
+
+def replay(ops, deps, order, ga, fix, hop, pc):
+    end, free = {}, {}
+    for i in order:
+        o = ops[i]
+        e, c = o["eng"], o["cost"]
+        if o["kind"] == "c" and e in ("dve", "act"):
+            c = 60.0 + o["n"] * ga * CY if o["per"] == GA else fix + max(64.0, o["n"] * o["per"]) * CY
+        elif e == "pe":
+            c = o["n"] * pc
+        s = free.get(e, 0.0) if e else 0.0
+        for j in deps[i]:
+            x = end[j] + (0.0 if e == "pe" and ops[j]["eng"] == "pe" else hop)
+            if x > s:
+                s = x
+        free[e] = s + c
+        end[i] = s + c + o["lat"]
+        if o["kind"] == "dma" and o["n"]:
+            free["bus"] = end[i] = max(end[i], free.get("bus", 0.0)) + o["n"]
+    return max(end.values())
+
+
+def search(ops, deps):
+    seed = [CFG["seed"]]
+
+    def rnd(k):
+        seed[0] = (seed[0] * 1103515245 + 12345) % 2147483648
+        return (seed[0] >> 8) % k
+
+    def score(p):
+        order = arrange(ops, deps, p)[0]
+        return sum(replay(ops, deps, order, *m) for m in COSTS) / len(COSTS)
+    kinds = {}
+    for i, o in enumerate(ops):
+        kinds.setdefault(tag(o), []).append(i)
+    names = sorted(k for k in kinds if len(kinds[k]) >= 10)
+    steps = [-8000.0, -4000.0, -2000.0, 0.0, 2000.0, 4000.0, 8000.0, 12000.0]
+    p = [0.0] * len(ops)
+    best = score(p)
+    for it in range(CFG["n1"] + CFG["n2"]):
+        q = list(p)
+        for _ in range(1 + rnd(3)):
+            v = steps[rnd(8)]
+            if it < CFG["n1"]:
+                for i in kinds[names[rnd(len(names))]]:
+                    q[i] = v
+            else:
+                q[rnd(len(ops))] = 2 * v
+        s = score(q)
+        if s <= best:
+            best, p = s, q
+    return p, best
+
+
+def plan(ops):
+    deps = depend(ops)
+    order, start, end = arrange(ops, deps, search(ops, deps)[0])
+    pos, cnt = {}, {}
+    for i in order:
+        o = ops[i]
+        if o["kind"] == "c":
+            cnt[o["eng"]] = cnt.get(o["eng"], 0) + 1
+            pos[i] = (o["eng"], cnt[o["eng"]])
+        else:
+            pos[i] = (o["sem"], o["val"])
+    known, clock, waits, marked = {}, {}, {}, set()
+    for i in order:
+        o = ops[i]
+        if o["kind"] == "recv":
+            clock[i] = {}
+            continue
+        kn = known.setdefault(o["eng"], {})
+        ws = []
+        for j in sorted(deps[i], key=lambda j: -end[j]):
+            if o["eng"] == "pe" and ops[j]["eng"] == "pe":
+                continue
+            s, v = pos[j]
+            if kn.get(s, 0) >= v:
+                continue
+            ws.append(j)
+            marked.add(j)
+            kn[s] = v
+            for a, b in clock[j].items():
+                if kn.get(a, 0) < b:
+                    kn[a] = b
+        waits[i] = ws
+        clock[i] = dict(kn)
+    value, cnt = {}, {}
+    for i in order:
+        o = ops[i]
+        if o["kind"] == "c":
+            if i in marked:
+                cnt[o["eng"]] = cnt.get(o["eng"], 0) + 1
+                value[i] = (o["eng"], cnt[o["eng"]])
+        else:
+            value[i] = (o["sem"], o["val"])
+    return order, waits, marked, value, start, end
+
+
+PLAN = {}
+
+
+def rank_program(g, core, T, topo):
+    if T.rank_of(core) is None:
+        return
+    ops = build(g, core, T, topo)
+    if "p" not in PLAN:
+        PLAN["p"] = plan(ops)
+    order, waits, marked, value = PLAN["p"][:4]
+    queue = {"pe": g.tensor, "dve": g.vector, "act": g.scalar, "pool": g, "sp": g.sync}
+    for i in order:
+        o = ops[i]
+        if o["kind"] == "recv":
+            continue
+        q = queue[o["eng"]]
+        for j in waits[i]:
+            s, v = value[j]
+            q.wait_ge(T.sem[s], v)
+        ins = o["fn"]()
+        if o["kind"] == "dma":
+            ins.then_inc(T.sem[o["sem"]], 16)
+        elif o["kind"] == "c" and i in marked:
+            ins.then_inc(T.sem[o["eng"]], 1)
+    for i in order:
+        o = ops[i]
+        if o["kind"] != "c" and i not in marked:
+            g.wait_ge(T.sem[o["sem"]], o["val"])

@@ -1,60 +1,75 @@
 from concourse.bass import DstId, RemoteDMATransfer
 from concourse.mybir import AluOpType as ALU, AxisListType, ActivationFunctionType as ACT
 
-CFG = {"cuts": [("dve", 0, 44), ("act", 44, 64), ("dve", 64, 80), ("act", 80, 128)], "nu": 2, "nm": 8, "win": 0.0,
-       "cutk": {}, "seed": 1, "n1": 800, "n2": 2500}
-XO = 16
+CFG = {"cuts": [("act", 64, 128), ("act", 0, 32), ("act", 32, 64)], "runs": [(64, 128), (0, 32), (32, 64)],
+       "relu": [(2, 4, 64)], "at": {}, "seed": 1, "rounds": 900}
+for _t in (0, 1):
+    CFG["at"][_t, 0, 0] = {"cuts": [("act", 64, 128), ("dve", 0, 32), ("dve", 32, 64)]}
+    CFG["at"][_t, 5, 0] = CFG["at"][_t, 5, 1] = {"relu": [(2, 4, 64), (0, 2, 64)], "runs": [(0, 32), (32, 64)]}
+XO = 32
 XW = XO + 4096
+FW = 2048 + 8
 KSUB = 65536 * 166
 DW = 131072.0
+MID = 2048.0
+DEAD = -2080.0
+LIFT = 1056.0
+KS, NS = 20, 9
+RKEY = 1.5 * 2.0 ** 36
+RIDX = 1.5 * 2.0 ** 39
+YROWS = {1: (0, 1), 3: (2, 3), 4: (4,)}
+BZ, BK, SP, Z0, Z1, Z2 = 0, 80, 136, 160, 256, 352
 
 SCRATCH = {
     "xa": ("sbuf", [128, XW], "bfloat16"), "xb": ("sbuf", [128, XW], "bfloat16"),
-    "fi": ("sbuf", [128, 2048], "int32"),
+    "fi": ("sbuf", [128, FW], "int32"),
     "l0": ("sbuf", [128, 96], "int32"), "i0": ("sbuf", [128, 96], "int32"),
     "l1": ("sbuf", [128, 96], "float32"), "i1": ("sbuf", [128, 96], "float32"),
     "l2": ("sbuf", [128, 80], "float32"), "i2": ("sbuf", [128, 80], "float32"), "r5": ("sbuf", [128, 32], "float32"),
     "sl0": ("sbuf", [128, 80], "float32"), "si0": ("sbuf", [128, 80], "float32"), "f50": ("sbuf", [128, 32], "float32"),
     "sl1": ("sbuf", [128, 80], "float32"), "si1": ("sbuf", [128, 80], "float32"), "f51": ("sbuf", [128, 32], "float32"),
-    "exi": ("sbuf", [128, 16], "int32"), "th8": ("sbuf", [128, 8], "int32"), "th8b": ("sbuf", [128, 8], "bfloat16"),
-    "wti": ("sbuf", [128, 4], "int32"), "wtf": ("sbuf", [128, 4], "float32"),
-    "thf": ("sbuf", [128, 8], "float32"), "thr0": ("sbuf", [128, 8], "float32"), "thr1": ("sbuf", [128, 8], "float32"),
-    "mm": ("sbuf", [128, 768], "float32"), "d0": ("sbuf", [128, 768], "float32"), "bz": ("sbuf", [128, 128], "int32"),
-    "b5": ("sbuf", [128, 16], "int32"), "yu": ("sbuf", [128, 96], "uint16"), "lu": ("sbuf", [128, 96], "uint16"),
+    "exi": ("sbuf", [128, 16], "int32"), "th8": ("sbuf", [128, 8], "int32"), "thf": ("sbuf", [128, 8], "float32"),
+    "thm": ("sbuf", [128, 48], "bfloat16"), "wti": ("sbuf", [128, 4], "int32"), "wtf": ("sbuf", [128, 4], "float32"),
+    "mm": ("sbuf", [128, 96 * NS], "float32"), "d0": ("sbuf", [128, 96 * NS], "float32"),
+    "yu": ("sbuf", [128, 6, 16], "uint16"), "lu": ("sbuf", [128, 96], "uint16"),
     "xl": ("sbuf", [128, 1536], "bfloat16"), "yy": ("sbuf", [128, 256], "bfloat16"),
-    "onb": ("sbuf", [128, 128], "bfloat16"), "idb": ("sbuf", [128, 128], "bfloat16"), "idf": ("sbuf", [128, 128], "float32"),
-    "sel": ("sbuf", [128, 128], "bfloat16"), "g8": ("sbuf", [128, 8], "bfloat16"), "bm": ("sbuf", [128, 8], "float32"),
+    "onb": ("sbuf", [128, 128], "bfloat16"), "idb": ("sbuf", [128, 128], "bfloat16"), "nid": ("sbuf", [128, 128], "bfloat16"),
+    "idk": ("sbuf", [128, 8 * KS], "float16"), "iv": ("sbuf", [128, 8 * KS], "float32"), "cr": ("sbuf", [128, 8 * KS], "bfloat16"),
+    "gq": ("sbuf", [128, 8 * KS], "bfloat16"), "gr24": ("sbuf", [128, 8 * KS], "bfloat16"), "gr34": ("sbuf", [128, 8 * KS], "bfloat16"),
+    "gr02": ("sbuf", [128, 8 * KS], "bfloat16"), "gr23": ("sbuf", [128, 8 * KS], "bfloat16"), "gr14": ("sbuf", [128, 8 * KS], "bfloat16"),
+    "ig": ("sbuf", [128, 8 * KS], "float32"), "im": ("sbuf", [128, 8 * KS], "float32"),
+    "g8": ("sbuf", [128, 8], "bfloat16"), "gv": ("sbuf", [128, 8], "bfloat16"), "up8": ("sbuf", [128, 8], "bfloat16"),
+    "bm": ("sbuf", [128, 8], "float16"), "bm32": ("sbuf", [128, 8], "float16"),
     "pi": ("sbuf", [128, 4], "int32"), "pa": ("sbuf", [128, 4], "int32"), "pb": ("sbuf", [128, 4], "int32"),
-    "pf": ("sbuf", [128, 8], "float32"), "ia": ("sbuf", [128, 128], "float32"), "ma": ("sbuf", [128, 128], "float32"),
-    "ix": ("sbuf", [128, 144], "float32"), "uw": ("sbuf", [128, 144], "bfloat16"), "rs": ("sbuf", [128, 128], "float32"),
+    "pf": ("sbuf", [128, 12], "float32"), "ia": ("sbuf", [128, 128], "float32"), "ma": ("sbuf", [128, 128], "float32"),
+    "ix": ("sbuf", [128, 144], "float32"), "uw": ("sbuf", [128, 144], "bfloat16"), "rs": ("sbuf", [128, 8 * KS], "float32"),
     "ic": ("sbuf", [128, 8], "float32"), "eo": ("sbuf", [128, 8], "uint16"), "po": ("sbuf", [128, 8], "uint16"),
     "base": ("sbuf", [128, 8], "int32"), "kt": ("sbuf", [128, 96], "float32"), "ki": ("sbuf", [128, 96], "float32"),
-    "ds": ("sbuf", [128, 128], "float32"), "bf": ("sbuf", [128, 128], "float32"), "sb": ("sbuf", [128, 128], "float32"),
-    "sr": ("sbuf", [128, 128], "float32"), "bp": ("sbuf", [128, 96], "float32"), "w2": ("sbuf", [128, 96], "float32"),
+    "dx": ("sbuf", [128, 16 * NS], "float32"), "ds": ("sbuf", [128, 16 * NS], "float32"), "sb": ("sbuf", [128, 16 * NS], "float32"),
+    "sr": ("sbuf", [128, 16 * NS], "float32"), "bp": ("sbuf", [128, 96], "float32"), "w2": ("sbuf", [128, 96], "float32"),
     "zr": ("sbuf", [128, 96], "int32"), "nl": ("sbuf", [128, 96], "int32"), "dl": ("sbuf", [128, 96], "float32"),
     "aa": ("sbuf", [128, 96], "float32"), "di": ("sbuf", [128, 96], "float32"), "dead": ("sbuf", [128, 96], "bfloat16"),
     "tl": ("sbuf", [128, 96], "float32"), "ti": ("sbuf", [128, 96], "float32"),
     "cn": ("sbuf", [128, 4], "float32"), "ci": ("sbuf", [128, 4], "int32"), "cj": ("sbuf", [128, 4], "int32"),
     "cf": ("sbuf", [128, 4], "float32"),
-    "pd0": ("psum", [128, 1024], "float32"), "pd1": ("psum", [128, 1024], "float32"), "pd2": ("psum", [128, 1024], "float32"),
-    "pk0": ("psum", [128, 512], "float32"), "pk1": ("psum", [128, 512], "float32"),
 }
 for _h in (0, 1):
-    for _n, _w, _t in (("pr", 64, "float32"), ("ss", 64, "float32"), ("bu", 8, "uint16"), ("zi", 8, "int32"),
-                       ("ni", 8, "int32"), ("nu", 8, "uint16"), ("cu", 128, "uint16"), ("fg", 128, "float32"),
-                       ("q", 128, "bfloat16"), ("v", 2048, "bfloat16"), ("sc", 128, "float32"),
-                       ("rx", 128, "float32"), ("kc", 8, "int32"), ("s1", 8, "int32"), ("s2", 8, "int32"),
-                       ("s3", 8, "int32"), ("pu", 8, "uint16")):
+    for _n in ("pk", "pz", "pq", "pd"):
+        SCRATCH["%s%d" % (_n, _h)] = ("psum", [128, 512], "float32")
+    for _n, _w, _t in (("pr", 8 * NS, "float32"), ("ss", 16 * NS, "float32"), ("nb", 16, "uint16"), ("cu", 128, "uint16"),
+                       ("fg", 128, "float16"), ("q", 128, "bfloat16"), ("sc", 8 * KS, "float32"), ("lo", 8, "float32"),
+                       ("rx", 128, "float16"), ("s1", 8, "int32"), ("s2", 8, "int32"), ("s3", 8, "int32"), ("pu", 8, "uint16")):
         SCRATCH["%s_%d" % (_n, _h)] = ("sbuf", [128, _w], _t)
-    SCRATCH["a_%d" % _h] = ("sbuf", [128, 16, 128], "bfloat16")
+    SCRATCH["a_%d" % _h] = ("sbuf", [128, 4, 512], "bfloat16")
+    SCRATCH["v_%d" % _h] = ("sbuf", [128, 2048], "bfloat16")
 
 NDMA = 24
-NFIRST = 6
 SEMAPHORES = ["pe", "dve", "act", "pool"] + ["m%d" % _i for _i in range(NDMA)] + \
              ["arr%d" % _i for _i in range(4)] + ["out%d" % _i for _i in range(4)]
 
-CY, GA, FIX, HOP, PC = 1.04, 1.56, 25.0, 80.0, 0.55
-COSTS = [(1.56, 15.0, 70.0, 0.55), (1.15, 15.0, 100.0, 0.5), (1.95, 30.0, 60.0, 0.55), (1.56, 50.0, 120.0, 0.65)]
+QUEUES = ("pe", "dve", "act", "pool", "sp", None)
+COSTS = [(1.04, 1.56, 3.8, 30.0, 100.0, 0.52, 5.0), (0.9, 1.56, 3.8, 20.0, 160.0, 0.52, 5.0),
+         (0.95, 1.3, 3.8, 20.0, 70.0, 0.75, 0.0), (1.1, 1.9, 4.5, 30.0, 100.0, 0.55, 10.0)]
 
 
 def build(g, core, T, topo):
@@ -62,26 +77,27 @@ def build(g, core, T, topo):
     n_ranks = len(T.cores)
     ops = []
     ndma = [0]
+    phase = [-1]
 
-    def op(eng, fn, r, w, cost, kind="c", sem=None, val=0, lat=0.0, n=0, per=0):
-        ops.append({"eng": eng, "fn": fn, "r": r, "w": w, "cost": cost, "kind": kind, "sem": sem, "val": val, "lat": lat,
-                    "n": n, "per": per})
+    def op(eng, fn, r, w, form, n, m=0, kind="c", sem=None, val=0, lat=0.0):
+        ops.append({"eng": eng, "fn": fn, "r": r, "w": w, "form": form, "n": n, "m": m, "kind": kind, "sem": sem,
+                    "val": val, "lat": lat, "ph": phase[0], "first": not r})
 
     V, S, P = g.vector, g.scalar, g.tensor
 
-    def dve(fn, r, w, n, per=1.0):
-        op("dve", fn, r, w, FIX + max(64.0, n * per) * CY, n=n, per=per)
+    def dve(fn, r, w, n, form="e"):
+        op("dve", fn, r, w, form, n)
 
-    def act(fn, r, w, n, per=1.0):
-        op("act", fn, r, w, FIX + max(64.0, n * per) * CY, n=n, per=per)
+    def act(fn, r, w, n, form="e"):
+        op("act", fn, r, w, form, n)
 
     def pool(fn, r, w, n):
-        op("pool", fn, r, w, 200 + 2 * n * CY)
+        op("pool", fn, r, w, "ns", 150 + 2.1 * n)
 
-    def pe(fn, r, w, cyc):
-        op("pe", fn, r, w, cyc * PC, n=cyc)
+    def pe(fn, r, w, cyc, calls=1):
+        op("pe", fn, r, w, "pe", cyc, calls)
 
-    def dma(eng, out, in_, r, w, lat, slow=False):
+    def dma(eng, out, in_, r, w, bus, slow=False):
         name = "m%d" % ndma[0]
         ndma[0] += 1
         q = {"sp": g.sync, "act": g.scalar, "pool": g}[eng]
@@ -89,7 +105,7 @@ def build(g, core, T, topo):
             fn = lambda: q.dma_start(out, in_, allow_slow_non_contiguous=True)
         else:
             fn = lambda: q.dma_start(out, in_)
-        op(eng, fn, r, w, 60.0, "dma", name, 16, 2000.0, n=lat)
+        op(eng, fn, r, w, "ns", 60.0, bus, "dma", name, 16, 1500.0)
 
     def ts(out, in0, s1, o1, s2=None, o2=None):
         if o2 is None:
@@ -101,6 +117,23 @@ def build(g, core, T, topo):
 
     def cp(out, a):
         return lambda: V.tensor_copy(out, a)
+
+    def ms(out, c):
+        return lambda: V.memset(out, c)
+
+    def scan(out, a, b, o0, o1):
+        return lambda: V.tensor_tensor_scan(out, a, b, 0.0, o0, o1)
+
+    def lin(out, in_, scale, bias=None):
+        if bias is None:
+            return lambda: S.activation(out, in_, ACT.Copy, scale=scale)
+        return lambda: S.activation(out, in_, ACT.Identity, bias=bias, scale=scale)
+
+    def mat(out, lhs, rhs, start, stop):
+        return lambda: P.matmul(out, lhs, rhs, start, stop)
+
+    def iota(out, pattern, base, cm=0):
+        return lambda: g.iota(out, pattern, base, cm, allow_small_or_imprecise_dtypes=True)
 
     def send(idx, dst, pairs, r, w):
         eng = topo.engines(core, dst)[:8]
@@ -114,245 +147,320 @@ def build(g, core, T, topo):
                 trs.append(RemoteDMATransfer(dst_ids=[DstId(rid=rid, pnc=pid)], dma_engine_mask=m,
                                              remote_sem=T.sem["arr%d" % idx], src=src, dst=land))
             return g.remote_dma_fused(trs, local_sem=T.sem["out%d" % idx])
-        op("pool", fn, r, ["sent%d" % idx], 300.0, "send", "out%d" % idx, share * len(pairs), 2500.0)
-        op(None, None, ["sent%d" % idx], w, 0.0, "recv", "arr%d" % idx, share * len(pairs), 500.0)
+        op("pool", fn, r, ["sent%d" % idx], "ns", 300.0, 0, "send", "out%d" % idx, share * len(pairs), 2500.0)
+        op(None, None, ["sent%d" % idx], w, "ns", 0.0, 0, "recv", "arr%d" % idx, share * len(pairs), 500.0)
 
-    dma("act", T.l0[:], T.lc[:], [], ["l0"], 150)
+    phase[0] = -9
+    dma("sp", T.l0[:], T.lc[:], [], ["l0"], 150)
+    dma("act", T.i0[:], T.up[:], [], ["i0"], 150)
     dma("act", T.exi[:], T.ex[:], [], ["exi"], 100)
-    dma("sp", T.fi[:], T.fa[:], [], ["fi0", "fi1"], 3200)
     dma("sp", T.xa[:, XO:XW], T.xs[:], [], ["xa0", "xa1"], 3200)
-    dma("act", T.i0[:], T.up[:], [], ["i0"], 0)
+    dma("sp", T.fi[:, 0:2048], T.fa[:], [], ["fi"], 3200)
     dma("act", T.th8[0:8, 0:6], T.th[:], [], ["th8"], 0)
+    dma("act", T.fi[:, 2048:FW], T.fa[:, 0:8], [], ["fie"], 0)
 
+    mmk, d0k = ["mm7", "mm8"], ["d0z"]
     pool(lambda: g.iota(T.pi[:, 0:1], [[1, 1]], 0, 1), [], ["pi"], 1)
-    pool(lambda: g.iota(T.ic[:], [[1, 8]], 0, 0, allow_small_or_imprecise_dtypes=True), [], ["ic"], 8)
-    pool(lambda: g.iota(T.ia[:], [[0, 8], [1, 16]], 0, 0, allow_small_or_imprecise_dtypes=True), [], ["ia"], 128)
-    dve(lambda: V.memset(T.onb[:], 1.0), [], ["onb"], 128, 0.5)
-    dve(lambda: V.memset(T.bz[:], 1), [], ["bz0", "bz1"], 128)
-    dve(lambda: V.memset(T.mm[:], 0.0), [], ["mm0", "mm1"], 768)
-    dve(lambda: V.memset(T.d0[:], 1.0), [], ["d00", "d01"], 768)
-    dve(lambda: V.memset(T.mm[:, 6::8], -2048.0 - XO), [], ["mm0", "mm1"], 96)
-    dve(lambda: V.memset(T.mm[:, 0:128:8], 1.0), [], ["mm0"], 16)
-    dve(lambda: V.memset(T.d0[:, 0::8], 0.0), [], ["d00", "d01"], 96)
-    for name in ("xa", "xb"):
-        dve(lambda name=name: V.memset(T[name][:, 0:XO], 0.0), [], [name + "s"], 16)
-        dve(lambda name=name: V.memset(T[name][:, 1:2], 64.0), [], [name + "s"], 1)
-    dve(lambda: V.memset(T.rs[:], 0.0), [], ["rs"], 128)
-    dve(lambda: V.memset(T.rs[:, 0::16], 1.0e9), [], ["rs"], 8)
+    pool(iota(T.ic[:], [[1, 8]], 0), [], ["ic"], 8)
+    dve(ms(T.onb[:], 1.0), [], ["onb"], 64)
+    pool(iota(T.ig[:], [[1, 8], [0, KS]], 0), [], ["ig"], 160)
+    pool(iota(T.d0[:], [[0, 96 * NS]], 1), [], ["d0z"], 864)
     pool(lambda: g.affine_select(T.idb[:], T.onb[:], [[-1, 128]], ALU.is_equal, 0.0, 0, 1), ["onb"], ["idb"], 128)
-    pool(lambda: g.affine_select(T.sel[0:8, :], T.onb[0:8, :], [[1, 8], [0, 16]], ALU.is_equal, 0.0, 0, -1), ["onb"], ["sel"], 128)
-    pool(lambda: g.iota(T.ix[:], [[1, 144]], -15, 0, allow_small_or_imprecise_dtypes=True), [], ["ix"], 144)
-    pool(lambda: g.iota(T.kt[:], [[32, 6], [0, 16]], 2048 * 1184 - KSUB, 0, allow_small_or_imprecise_dtypes=True), [], ["kt"], 96)
-    pool(lambda: g.iota(T.ki[:], [[1, 6], [0, 16]], -1, 0, allow_small_or_imprecise_dtypes=True), [], ["ki"], 96)
+    pool(iota(T.im[:], [[0, 8], [1, KS]], 0), [], ["im"], 160)
+    pool(iota(T.iv[:], [[32, 8], [1, KS]], 0), [], ["iv"], 160)
+    pool(iota(T.ia[:], [[0, 8], [1, 16]], 0), [], ["ia"], 128)
     dma("pool", T.wti[:, 0:1], T.wt[:], [], ["wti"], 0, slow=True)
+    pool(iota(T.ix[:], [[1, 144]], -15), [], ["ix"], 144)
+    pool(iota(T.kt[:], [[32, 6], [0, 16]], 992 * 1184 - KSUB), [], ["kt"], 96)
+    pool(iota(T.ki[:], [[1, 6], [0, 16]], -1), [], ["ki"], 96)
+    dve(ms(T.mm[:, 7::NS], RIDX), [], ["mm7"], 96)
+    dve(ms(T.mm[:, 8::NS], -RIDX), [], ["mm8"], 96)
+    for h in (0, 1):
+        dve(ms(T["pz%d" % h][:, BZ:BZ + 8 * NS], 1.0), [], ["pz%d" % h], 72)
+    for name in ("xa", "xb"):
+        dve(ms(T[name][:, 0:16], 64.0), [], [name + "s"], 8)
+        dve(ms(T[name][:, 16:XO], 0.0), [], [name + "z"], 8)
+    dve(ms(T.rs[:], 0.0), [], ["rs0", "rs1", "rs2"], 160)
+    dve(ms(T.cr[:], 0.0), [], ["cr0", "cr1", "cr2", "cr3"], 80)
+    dve(ms(T.up8[:], 32 * LIFT), [], ["up8"], 8)
     dve(ts(T.pa[:, 0:1], T.pi[:, 0:1], 15, ALU.bitwise_and), ["pi"], ["pa"], 1)
     dve(ts(T.pb[:, 0:1], T.pi[:, 0:1], 4, ALU.arith_shift_right), ["pi"], ["pb"], 1)
+    dve(ms(T.rs[:, 0::KS], 1.0e9), [], ["rs0"], 8)
+    dve(ms(T.rs[:, 17::KS], RKEY), [], ["rs1"], 8)
+    dve(ms(T.rs[:, 18::KS], -RKEY), [], ["rs2"], 8)
+    dve(ms(T.cr[32:33, :], -120 * DW), [], ["cr1"], 80)
     dve(cp(T.pf[:, 0:1], T.pa[:, 0:1]), ["pa"], ["pf0"], 1)
     dve(cp(T.pf[:, 1:2], T.pb[:, 0:1]), ["pb"], ["pf1"], 1)
-    dve(ts(T.pf[:, 2:3], T.pa[:, 0:1], 8192.0, ALU.mult, XO - 16777216.0, ALU.add), ["pa"], ["pf2"], 1)
-    dve(ts(T.pf[:, 3:4], T.pb[:, 0:1], 16.0, ALU.mult), ["pb"], ["pf3"], 1)
-    dve(ts(T.pf[:, 4:5], T.pa[:, 0:1], 16.0, ALU.mult), ["pa"], ["pf4"], 1)
-    dve(ts(T.pf[:, 5:6], T.pa[:, 0:1], 8.0, ALU.mult), ["pa"], ["pf5"], 1)
-    dve(cp(T.idf[:], T.idb[:]), ["idb"], ["idf"], 128)
-    dve(ts(T.g8[:], T.ic[:], T.pf[:, 1:2], ALU.is_equal, DW, ALU.mult), ["ic", "pf1"], ["g8"], 8)
+    act(lin(T.pf[:, 2:3], T.pf[:, 1:2], 32.0, T.pf[:, 0:1]), ["pf0", "pf1"], ["pf2"], 1)
+    act(lin(T.pf[:, 3:4], T.pf[:, 1:2], 16.0), ["pf1"], ["pf3"], 1)
+    act(lin(T.pf[:, 4:5], T.pf[:, 0:1], 16.0), ["pf0"], ["pf4"], 1)
+    act(lin(T.pf[:, 5:6], T.pf[:, 0:1], float(NS)), ["pf0"], ["pf5"], 1)
+    phase[0] = -7
+    for h in (0, 1):
+        dve(ts(T["pz%d" % h][:, BZ:BZ + 8 * NS:NS], T.exi[:, 8 * h:8 * h + 8], 32.0, ALU.mult, 32 * (LIFT - MID), ALU.add),
+            ["exi"], ["pz%d" % h], 8)
+    dve(ts(T.thf[0:8, 0:6], T.th8[0:8, 0:6], DW, ALU.mult), ["th8"], ["thf"], 6)
+    phase[0] = -6
+    dve(ms(T.d0[:, 0::NS], 0.0), [], ["d0z"], 96)
+    act(lin(T.nid[:], T.idb[:], -1.0), ["idb"], ["nid"], 128)
+    for k in range(6):
+        act(lin(T.thm[0:8, 8 * k:8 * k + 8], T.idb[0:8, 0:8], T.thf[0:8, k:k + 1]), ["idb", "thf"], ["thm%d" % k], 8)
+    phase[0] = -8.5
+    dve(ts(T.g8[:], T.ic[:], T.pf[:, 1:2], ALU.is_equal, 2 * DW, ALU.mult), ["ic", "pf1"], ["g8"], 8)
+    act(lin(T.gv[:], T.g8[:], -0.5), ["g8"], ["gv"], 8)
     dve(ts(T.bm[:], T.ic[:], T.pf[:, 1:2], ALU.is_equal), ["ic", "pf1"], ["bm"], 8)
-    dve(ts(T.ma[:], T.ia[:], T.pf[:, 0:1], ALU.is_equal), ["ia", "pf0"], ["ma"], 128)
-    dve(ts(T.eo[:], T.ic[:], 16.0, ALU.mult, 15.0, ALU.add), ["ic"], ["eo"], 8)
+    dve(ts(T.bm32[:], T.ic[:], T.pf[:, 1:2], ALU.is_equal, 32.0, ALU.mult), ["ic", "pf1"], ["bm32"], 8)
+    dve(cp(T.eo[:], T.ic[:]), ["ic"], ["eo"], 8)
     dve(ts(T.po[:], T.ic[:], T.pf[:, 5:6], ALU.add), ["ic", "pf5"], ["po"], 8)
     dve(ts(T.base[:], T.ic[:], 256.0, ALU.mult, T.pf[:, 4:5], ALU.add), ["ic", "pf4"], ["base"], 8)
-    dve(ts(T.bz[:, 0::8], T.exi[:], float(XO), ALU.add), ["exi"], ["bz0", "bz1"], 16)
-    dve(cp(T.th8b[0:8, 0:6], T.th8[0:8, 0:6]), ["th8"], ["th8b"], 6)
-    pe(lambda: P.matmul(T.pk1[:, 0:6], T.sel[0:8, :], T.th8b[0:8, 0:6], True, True), ["sel", "th8b"], ["pk1"], 64)
-    dve(ts(T.thf[:, 0:6], T.pk1[:, 0:6], -128.0, ALU.add), [], ["pk1", "thf"], 6)
-    dve(ts(T.thr0[:, 0:6], T.thf[:, 0:6], DW, ALU.mult), ["thf"], ["thr0"], 6)
+    dve(ts(T.gq[:], T.ig[:], T.pf[:, 1:2], ALU.is_equal, -DW, ALU.mult), ["ig", "pf1"], ["gq"], 160)
+    dve(ms(T.gq[:, 16::KS], 0.0), [], ["gq"], 8)
+    for j0, j1 in sorted({r[:2] for c in [CFG] + list(CFG["at"].values()) for r in c.get("relu", ())}):
+        gr = T["gr%d%d" % (j0, j1)]
+        dve(ms(gr[:], 0.0), [], ["gr%d%d" % (j0, j1)], 80)
+        for j in range(j0, j1):
+            act(lin(gr[:, j::4], T.gq[:, j::4], -2.0), ["gq"], ["gr%d%d" % (j0, j1)], 40)
+    phase[0] = -5
+    act(lin(T.cr[0:1, :], T.im[0:1, :], 8192.0), ["im"], ["cr0"], 160)
+    dve(ts(T.cr[96:97, :], T.im[96:97, :], 16.0, ALU.is_gt, 2.0 ** 40, ALU.mult), ["im"], ["cr3"], 160)
+    dve(ms(T.cr[0:1, 16::KS], DEAD), [], ["cr0"], 8)
+    dve(ts(T.idk[:], T.iv[:], T.pf[:, 2:3], ALU.is_equal), ["iv", "pf2"], ["idk"], 160)
+    dve(ts(T.ma[:], T.ia[:], T.pf[:, 0:1], ALU.is_equal), ["ia", "pf0"], ["ma"], 128)
+    phase[0] = -2
     dve(cp(T.wtf[:, 0:1], T.wti[:, 0:1]), ["wti"], ["wtf"], 1)
     dve(ts(T.uw[:], T.ix[:], T.pf[:, 3:4], ALU.is_equal, T.wtf[:, 0:1], ALU.mult), ["ix", "pf3", "wtf"], ["uw"], 144)
-    dma("sp", T.xb[:, XO:XW], T.xs[:], ["xa0"], ["xb0", "xb1"], 3200)
+    dma("sp", T.xb[:, XO:XW], T.xs[:], ["fi"], ["xb0", "xb1"], 3200)
 
     ring = [0]
     for t in (0, 1):
         X = T.xa if t == 0 else T.xb
         xn = "xa" if t == 0 else "xb"
         xk = [xn + "0", xn + "1"]
-        xks = xk + [xn + "s"]
         L, I = (T.l0, T.i0) if t == 0 else (T.l1, T.i1)
         ka, kb = (["l0"], ["l0", "i0"]) if t == 0 else (["st1a"], ["st1a", "st1b"])
-        thr = T.thr0 if t == 0 else T.thr1
-        wadd = float(32 * 64 * 1184 + 32 * 77 * t - KSUB)
+        wadd = float(992 * 1184 + 32 * 77 * t - 32768 - KSUB)
 
-        def prep(c0, c1, part, keys):
-            dve(ts(T.d0[:, 8 * c0 + 7:8 * c1:8], L[:, c0:c1], 1184.0, ALU.add), keys, ["d0%d" % part], c1 - c0)
-            dve(ts(T.mm[:, 8 * c0 + 7:8 * c1:8], L[:, c0:c1], 2080.0, ALU.mult, wadd, ALU.add), keys, ["mm%d" % part], c1 - c0)
-            dve(cp(T.lu[:, c0:c1], L[:, c0:c1]), keys, ["lu%d" % part], c1 - c0)
+        def prep(c0, c1, part, keys, t=t, L=L):
+            a, b = T.d0[:, NS * c0 + 6:NS * c1:NS], T.mm[:, NS * c0 + 6:NS * c1:NS]
+            dve(cp(T.lu[:, c0:c1], L[:, c0:c1]), keys, ["lu%d" % p for p in part], c1 - c0)
+            if t == 0:
+                dve(ts(a, L[:, c0:c1], 1184.0, ALU.add, 1.0 / 32, ALU.mult), keys + d0k, ["d0%d" % p for p in part], c1 - c0)
+                dve(ts(b, L[:, c0:c1], 1024.0, ALU.mult, wadd, ALU.add), keys, ["mw%d" % p for p in part], c1 - c0)
+            else:
+                act(lin(a, L[:, c0:c1], 1.0 / 32, 37.0), keys, ["d0%d" % p for p in part], c1 - c0)
+                act(lin(b, L[:, c0:c1], 1024.0, wadd), keys, ["mw%d" % p for p in part] + ["mk5"] * part[0], c1 - c0)
+
+        def masks(keys, t=t, I=I):
+            for s in range(6):
+                k0 = max(s, 1) if t else 0
+                dve(ts(T.mm[:, 16 * NS * k0 + s::NS], I[:, 16 * k0:96], float(s - 1), ALU.is_equal), keys, ["mk%d" % s], 96 - 16 * k0)
 
         def xl(k0, k1, X=X, xk=xk):
             act(lambda: S.activation(T.xl[:, 256 * k0:256 * k1], X[:, XO:XW].indirect(T.lu[:, 16 * k0:16 * k1]), ACT.Copy),
-                xk + ["lu%d" % min(k0, 1)], ["xl%d" % k for k in range(k0, k1)], 256 * (k1 - k0), GA)
+                xk + ["lu%d" % min(k0, 1)], ["xl%d" % k for k in range(k0, k1)], 256 * (k1 - k0), "g")
 
-        prep(0, 16, 0, ka)
-        xl(0, 1)
-        if t == 1:
+        if t == 0:
+            phase[0] = -8
+            prep(0, 96, (0, 1), ka)
+            masks(kb)
+            phase[0] = -4
+            xl(0, 1)
+            xl(1, 6)
+            phase[0] = 0
+        else:
+            phase[0] = 12
+            prep(0, 16, (0,), ka)
+            xl(0, 1)
             dma("sp", T.xa[:, XO:XO + 2048], T.xb[:, XO:XO + 2048], ["xb0", "sent1"], ["xa0"], 1600)
 
-        def ymax(k, c0, c1, src, keys, X=X, xks=xks):
-            hs = [h for h in (0, 1) if c0 <= 8 * h < c1]
+        def ylist(k0, k1, h):
+            dve(ts(T.yu[:, k0:k1, 8 * h:8 * h + 8], T["pz%d" % h][:, BK + 8 * k0:BK + 8 * k1], MID + 16, ALU.add, 0.0, ALU.max),
+                ["pz%d" % h], ["yu%d_%d" % (k, h) for k in range(k0, k1)], 8 * (k1 - k0))
+
+        def ymax(k, hs, X=X, xk=xk, xn=xn):
             uk = ["yu%d_%d" % (k, h) for h in hs]
             yk = ["yy%d" % h for h in hs]
-            off = T.yu[:, 16 * k + c0:16 * k + c1]
-            dve(cp(off, src), keys, uk, c1 - c0)
+            c0, c1 = 8 * hs[0], 8 * hs[-1] + 8
+            w = X[:, 16:XW].indirect(T.yu[:, k, c0:c1])
             o = T.yy[:, 16 * c0:16 * c1]
-            if k == 0:
-                dve(lambda: V.tensor_copy(o, X[:, 0:XW].indirect(off)), xks + uk, yk, 16 * (c1 - c0), GA)
-            else:
-                dve(lambda: V.tensor_tensor(o, X[:, 0:XW].indirect(off), o, ALU.max), xks + uk, yk, 16 * (c1 - c0), GA)
+            dve(cp(o, w) if k == 0 else tt(o, w, o, ALU.max), xk + [xn + "z"] + uk, yk, 16 * (c1 - c0), "g")
 
-        def settle(c0, c1, ol, oi, okeys, L=L, I=I, kb=kb):
-            p = "a" if c0 == 0 else "b"
-            uk = ["yu%d_%d" % (k, h) for k in range(c0 // 16, c1 // 16) for h in (0, 1)]
-            dve(ts(T.dead[:, c0:c1], T.yu[:, c0:c1], 0.0, ALU.is_equal), uk, ["dead" + p], c1 - c0)
-            dve(tt(T.tl[:, c0:c1], T.dl[:, c0:c1], T.dead[:, c0:c1], ALU.mult), ["dl", "dead" + p], ["tl" + p], c1 - c0, 2)
-            dve(tt(T.ti[:, c0:c1], T.di[:, c0:c1], T.dead[:, c0:c1], ALU.mult), ["di", "dead" + p], ["ti" + p], c1 - c0, 2)
-            dve(tt(ol, L[:, c0:c1], T.tl[:, c0:c1], ALU.add), kb + ["tl" + p], [okeys[0]], c1 - c0, 2)
-            dve(tt(oi, I[:, c0:c1], T.ti[:, c0:c1], ALU.subtract), kb + ["ti" + p], [okeys[1]], c1 - c0, 2)
+        def settle(k0, k1, ol, oi, okeys, L=L, I=I, kb=kb):
+            p = "a" if k0 == 0 else "b"
+            c0, c1 = 16 * k0, 16 * k1
+            uk = ["yu%d_%d" % (k, h) for k in range(k0, k1) for h in (0, 1)]
+            dve(ts(T.dead[:, c0:c1], T.yu[:, k0:k1, :], 0.0, ALU.is_equal), uk, ["dead" + p], (c1 - c0) / 2)
+            dve(tt(T.tl[:, c0:c1], T.dl[:, c0:c1], T.dead[:, c0:c1], ALU.mult), ["dl", "dead" + p], ["tl" + p], 2 * (c1 - c0))
+            dve(tt(T.ti[:, c0:c1], T.di[:, c0:c1], T.dead[:, c0:c1], ALU.mult), ["di", "dead" + p], ["ti" + p], 2 * (c1 - c0))
+            dve(tt(ol, L[:, c0:c1], T.tl[:, c0:c1], ALU.add), kb + ["tl" + p], [okeys[0]], 2 * (c1 - c0))
+            dve(tt(oi, I[:, c0:c1], T.ti[:, c0:c1], ALU.subtract), kb + ["ti" + p], [okeys[1]], 2 * (c1 - c0))
 
         for k in range(6):
             part = min(k, 1)
-            if k == 1:
-                prep(16, 96, 1, kb)
-                for s in range(6):
-                    k0 = max(s, 1)
-                    dve(ts(T.mm[:, 128 * k0 + s::8], I[:, 16 * k0:96], float(s - 1), ALU.is_equal), kb, ["mm1"], 96 - 16 * k0)
-            if k in (1, 3):
-                xl(k, k + 2)
-            if k == 5:
-                xl(5, 6)
+            if t == 1 and k == 1:
+                prep(16, 96, (1,), kb)
+                masks(kb)
+            if t == 1 and k in (1, 3, 5):
+                xl(k, min(k + 2, 6))
             for h in (0, 1):
+                phase[0] = 12 * t + 2 * k + h
+
                 def B(n, h=h):
                     return T["%s_%d" % (n, h)]
 
                 def K(n, h=h):
                     return "%s_%d" % (n, h)
-                pk = T["pk%d" % h]
-                pkk = "pk%d" % h
-                c0 = 128 * k + 64 * h
-                dve(tt(B("pr")[:], T.mm[:, c0:c0 + 64], T.bz[:, 64 * h:64 * h + 64], ALU.mult),
-                    ["mm%d" % part, "bz%d" % h], [K("pr")], 64, 2)
-                dve(lambda B=B, c0=c0: V.tensor_tensor_scan(B("ss")[:], T.d0[:, c0:c0 + 64], B("pr")[:], 0.0, ALU.mult, ALU.add),
-                    ["d0%d" % part, K("pr")], [K("ss")], 64)
-                dve(cp(B("zi")[:], B("ss")[:, 7::8]), [K("ss")], [K("zi")], 8)
-                dve(ts(B("ni")[:], B("zi")[:], 5, ALU.arith_shift_right, 2047, ALU.bitwise_and), [K("zi")], [K("ni")], 8)
-                dve(cp(B("nu")[:], B("ni")[:]), [K("ni")], [K("nu")], 8)
-                dve(lambda B=B: V.tensor_copy(B("cu")[:], T.fi[:].indirect(B("nu")[:])), ["fi0", "fi1", K("nu")], [K("cu")], 128, GA)
-                dve(ts(B("bu")[:], B("ss")[:, 6::8], 2048.0 + XO, ALU.add, 1.0, ALU.max), [K("ss")], [K("bu")], 8)
+                pk, pkk = T["pk%d" % h], "pk%d" % h
+                pz, pzk = T["pz%d" % h], "pz%d" % h
+                pq = T["pq%d" % h]
+                c0 = NS * (16 * k + 8 * h)
+                n9 = 8 * NS
+                ss = B("ss")
+                cfg = dict(CFG, **CFG["at"].get((t, k, h), {}))
+                mk = ["mk%d" % s for s in range(6)] if (k or not t) else []
+                dve(tt(B("pr")[:], T.mm[:, c0:c0 + n9], pz[:, BZ:BZ + n9], ALU.mult), mmk + mk + ["mw%d" % part, pzk], [K("pr")], n9)
+                dve(scan(ss[:, n9:2 * n9], T.d0[:, c0:c0 + n9], B("pr")[:], ALU.mult, ALU.add), ["d0%d" % part, K("pr")], [K("ss")], n9)
+                dve(tt(ss[:, 5:n9:NS], ss[:, n9 + 6::NS], ss[:, n9 + 8::NS], ALU.subtract), [K("ss")], [K("sr")], 16)
+                dve(ts(B("nb")[:], ss[:, 5::NS], 1.0 / 32, ALU.mult, 1024 - 31.0 / 64, ALU.add), [K("ss"), K("sr")], [K("nb")], 16)
+                dve(cp(B("cu")[:], T.fi[:].indirect(B("nb")[:, 0:8])), ["fi", "fie", K("nb")], [K("cu")], 128, "g")
                 x0 = 256 * k + 128 * h
-                dve(lambda B=B, X=X, x0=x0: V.tensor_tensor(B("q")[:], X[:, 0:XW].indirect(B("bu")[:]), T.xl[:, x0:x0 + 128], ALU.max),
-                    xks + [K("bu"), "xl%d" % k], [K("q")], 128, GA)
-                dve(ts(B("fg")[:], B("cu")[:], T.pf[:, 2:3], ALU.add), [K("cu"), "pf2"], [K("fg")], 128)
-                pe(lambda B=B, pk=pk: P.matmul(pk[:, 0:128], B("fg")[:], T.idf[:], True, False), [K("fg"), "idf"], [pkk], 512)
-                nu, nm = CFG["nu"], CFG["nm"]
-                cw = 128 // nu
-                vk = [[] for u in range(nu)]
-                for i, (eng, a, b) in enumerate(CFG["cutk"].get((k, h), CFG["cuts"])):
-                    key = K("v%d" % i)
-                    for u in range(nu):
-                        if a < cw * u + cw and b > cw * u:
-                            vk[u].append(key)
+                dve(tt(B("q")[:], X[:, 0:XW].indirect(B("nb")[:, 8:16]), T.xl[:, x0:x0 + 128], ALU.max),
+                    xk + [xn + "s", xn + "z", K("nb"), "xl%d" % k], [K("q")], 128, "g")
+                dve(ts(B("fg")[:], B("cu")[:], -MID, ALU.add), [K("cu")], [K("fg")], 64)
+                pe(mat(pk[:, 0:8 * KS], T.onb[0:97, :], T.cr[0:97, :], True, False), ["onb", "cr0", "cr1", "cr2", "cr3"], [pkk], 160)
+                pe(mat(pk[:, 16:8 * KS:KS], T.onb[0:8, :], T.thm[0:8, 8 * k:8 * k + 8], False, False), ["onb", "thm%d" % k], [pkk], 64)
+                pe(mat(pk[:, 0:8 * KS], B("q")[:], T.gq[:], False, False), [K("q"), "gq"], [pkk], 160)
+                for j0, j1, a0 in cfg["relu"]:
+                    gr = "gr%d%d" % (j0, j1)
+                    pe(mat(pk[a0:128, 0:8 * KS], B("q")[:, a0:128], T[gr][:], False, False), [K("q"), gr], [pkk], 160)
+
+                def four(out, lhs, rhs, stop):
+                    for i in range(4):
+                        ins = P.matmul(out(i), lhs, rhs, i == 0, stop and i == 3)
+                    return ins
+                pe(lambda B=B, pq=pq: four(lambda i: pq[:, i::4], T.idb[:], B("q")[:], True), [K("q"), "idb"], [K("pq")], 512, 4)
+                for i, (eng, a, b) in enumerate(cfg["cuts"]):
                     o, w = B("v")[:, 16 * a:16 * b], X[:, XO:XW].indirect(B("cu")[:, a:b])
                     if eng == "dve":
-                        dve(ts(o, w, -1.0, ALU.mult), xk + [K("cu")], [key], 16 * (b - a), GA)
+                        dve(cp(o, w), xk + [K("cu")], [K("v%d" % i)], 16 * (b - a), "g")
                     else:
-                        act(lambda o=o, w=w: S.activation(o, w, ACT.Copy, scale=-1.0), xk + [K("cu")], [key], 16 * (b - a), GA)
-                nb = nm * cw // 512
-                for u in range(nu):
-                    for m0 in range(0, 16, nm):
-                        slot = ring[0] % (6 // nb)
-                        ring[0] += 1
-                        pd = T["pd%d" % (slot * nb // 2)]
-                        p0 = 512 * (slot * nb % 2)
-                        pdk = "pd%d" % slot
+                        act(lambda o=o, w=w: S.activation(o, w, ACT.Copy), xk + [K("cu")], [K("v%d" % i)], 16 * (b - a), "g")
 
-                        def fill(B=B, pd=pd, p0=p0, u=u, m0=m0):
-                            for j in range(nm):
-                                o = pd[:, p0 + cw * j:p0 + cw * j + cw]
-                                P.matmul(o, T.idb[:], B("q")[:, cw * u:cw * u + cw], True, False)
-                                ins = P.matmul(o, T.idb[:], B("v")[:, 16 * cw * u + m0 + j:16 * cw * (u + 1):16], False, True)
-                            return ins
-                        pe(fill, vk[u] + [K("q"), "idb"], [pdk], 2 * cw * nm)
-                        act(lambda B=B, pd=pd, p0=p0, u=u, m0=m0: S.activation(
-                            B("a")[:, m0:m0 + nm, cw * u:cw * u + cw], pd[:, p0:p0 + cw * nm], ACT.Abs),
-                            [], [pdk, K("a%d_%d" % (u, m0))], cw * nm)
-                for m0 in range(0, 16, nm):
-                    def lanes(B=B, pk=pk, m0=m0):
-                        for m in range(m0, m0 + nm):
-                            ins = P.matmul(pk[:, m:128:16], B("a")[:, m, :], T.g8[:], False, m == 15)
+                def vkeys(c, d):
+                    return [K("v%d" % i) for i, (eng, a, b) in enumerate(cfg["cuts"]) if a < d and b > c]
+                ak = [[] for j in range(4)]
+                last = [128] * 4
+                for x, (j0, j1, a0) in enumerate(cfg["relu"]):
+                    n, nj = 4 * (128 - a0), j1 - j0
+                    pd, pdk = T["pd%d" % (ring[0] % 2)], "pd%d" % (ring[0] % 2)
+                    ring[0] += 1
+
+                    def lessq(B=B, pd=pd, n=n, nj=nj, a0=a0):
+                        for i in range(4 * nj):
+                            ins = P.matmul(pd[:, n * (i // 4) + i % 4:n * (i // 4 + 1):4], T.nid[:], B("q")[:, a0:128], i == 0, False)
                         return ins
-                    pe(lanes, [K("a%d_%d" % (u, m0)) for u in range(nu)] + ["g8"], [pkk], 64 * nm)
-                dve(lambda B=B, pk=pk: V.tensor_tensor_scan(B("sc")[:], T.rs[:], pk[:, 0:128], 0.0, ALU.add, ALU.min),
-                    ["rs"], [pkk, K("sc")], 128)
-                dve(lambda B=B: V.tensor_tensor(B("rx")[:], B("sc")[:].indirect(T.eo[:]), T.ma[:], ALU.mult),
-                    [K("sc"), "eo", "ma"], [K("rx")], 128, GA)
-                pe(lambda B=B, pk=pk: P.matmul(pk[:, 128:136], B("rx")[:], T.bm[:], True, True), [K("rx"), "bm"], [pkk], 256)
-                dve(ts(B("kc")[:], pk[:, 128:136], thr[:, k:k + 1], ALU.min), ["thr%d" % t], [pkk, K("kc")], 8)
-                if k < 5:
-                    dve(ts(T.bz[:, 64 * h + k + 1:64 * h + 64:8], B("kc")[:], 8191, ALU.bitwise_and), [K("kc")], ["bz%d" % h], 8)
-                    continue
-                dve(ts(T.b5[:, 8 * h:8 * h + 8], B("kc")[:], 8191, ALU.bitwise_and), [K("kc")], ["b5%d" % h], 8)
-                ymax(5, 8 * h, 8 * h + 8, T.b5[:, 8 * h:8 * h + 8], ["b5%d" % h])
 
-                def wsum(pk=pk, h=h):
-                    for a in range(16):
-                        ins = P.matmul(pk[:, 136:144], T.uw[:, 15 - a:143 - a], T.yy[:, 128 * h + a:128 * h + 128:16], a == 0, a == 15)
+                    def plusv(B=B, pd=pd, n=n, nj=nj, a0=a0, j0=j0):
+                        for i in range(nj):
+                            ins = P.matmul(pd[:, n * i:n * i + n], T.idb[:], B("v")[:, 16 * a0 + j0 + i::4], False, i == nj - 1)
+                        return ins
+                    pe(lessq, [K("q"), "nid"], [K("dq%d" % x), pdk], 4 * nj * max(64, n // 4), 4 * nj)
+                    pe(plusv, vkeys(a0, 128) + ["idb"], [K("dv%d" % x), pdk], n * nj, nj)
+                    act(lambda B=B, pd=pd, n=n, a0=a0, j0=j0, j1=j1: S.activation(B("a")[:, j0:j1, 4 * a0:512], pd[:, 0:n * (j1 - j0)], ACT.Relu),
+                        [pdk], [K("ar%d" % x)], n * nj)
+                    for j in range(j0, j1):
+                        ak[j].append(K("ar%d" % x))
+                        last[j] = a0
+                for i, (a, b) in enumerate(cfg["runs"]):
+                    for j in range(4):
+                        e = min(b, last[j])
+                        if e > a:
+                            dve(tt(B("a")[:, j, 4 * a:4 * e], pq[:, 4 * a:4 * e], B("v")[:, 16 * a + j:16 * e:4], ALU.max),
+                                [K("pq")] + vkeys(a, e), [K("a%d%d" % (j, i))], 4 * (e - a))
+                            ak[j].append(K("a%d%d" % (j, i)))
+
+                def lanes(pk, src, w):
+                    for m, lhs in src:
+                        ins = P.matmul(pk[:, m:8 * KS:KS], lhs, w, False, False)
                     return ins
-                pe(wsum, ["uw", "yy%d" % h], [pkk], 1024)
-                dve(cp(B("s1")[:], pk[:, 136:144]), [], [pkk, K("s1")], 8)
+                sums = []
+                for j in range(4):
+                    sums.append(K("kv%d" % j))
+                    pe(lambda B=B, pk=pk, j=j: lanes(pk, [(m, B("v")[:, m::16]) for m in range(j, 16, 4)], T.gv[:]),
+                       vkeys(0, 128) + ["gv", pkk], sums[-1:], 256, 4)
+                for j in range(4):
+                    sums.append(K("ka%d" % j))
+                    pe(lambda B=B, pk=pk, j=j: lanes(pk, [(j + 4 * i, B("a")[:, j, i::4]) for i in range(4)], T.g8[:]),
+                       ak[j] + ["g8", pkk], sums[-1:], 256, 4)
+                pe(mat(pk[:, 0:8 * KS], B("fg")[:], T.idk[:], False, True), [K("fg"), "idk"] + sums, [pkk], 160)
+                dve(scan(B("sc")[:], T.rs[:], pk[:, 0:8 * KS], ALU.add, ALU.min), ["rs0", "rs1", "rs2", pkk], [K("sc")], 8 * KS)
+                dve(tt(B("lo")[:], B("sc")[:, 16::KS], B("sc")[:, 18::KS], ALU.subtract), [K("sc")], [K("lo")], 16)
+                dve(tt(B("rx")[:], B("lo")[:].indirect(T.eo[:]), T.ma[:], ALU.mult), [K("lo"), "eo", "ma"], [K("rx")], 128, "g")
+                if k < 5:
+                    o = pz[:, BZ + k + 1:BZ + n9:NS]
+                    pe(mat(o, T.onb[0:1, :], T.up8[0:1, :], True, False), ["onb", "up8"], [K("zu"), pzk], 64)
+                    pe(mat(o, B("rx")[:], T.bm32[:], False, True), [K("rx"), "bm32"], [K("zb"), pzk], 64)
+                pe(mat(pz[:, BK + 8 * k:BK + 8 * k + 8], B("rx")[:], T.bm[:], True, True), [K("rx"), "bm"], [K("zk"), pzk], 64)
+                if k in YROWS:
+                    ylist(YROWS[k][0], k + 1, h)
+                if k == 4:
+                    bz, z0 = pz[:, BZ:BZ + n9], n9 * h
+                    dve(ts(T.dx[:, z0:z0 + n9], bz, -32 * (DEAD + LIFT) - 500, ALU.add, -1.0e4, ALU.mult), [pzk], [K("dx")], n9)
+                    dve(ts(T.ds[:, z0:z0 + n9], bz, 32 * (DEAD + LIFT), ALU.is_equal), [pzk], [K("ds")], n9)
+                    dve(scan(T.sb[:, z0:z0 + n9], T.dx[:, z0:z0 + n9], bz, ALU.min, ALU.max), [pzk, K("dx")], [K("sb")], n9)
+                if k < 5:
+                    continue
+                ylist(5, 6, h)
+                ymax(5, [h])
+
+                def wsum(pz=pz, h=h):
+                    for a in range(16):
+                        ins = P.matmul(pz[:, SP:SP + 8], T.uw[:, 15 - a:143 - a], T.yy[:, 128 * h + a:128 * h + 128:16], a == 0, a == 15)
+                    return ins
+                pe(wsum, ["uw", "yy%d" % h], [K("zs"), pzk], 1024, 16)
+                dve(cp(B("s1")[:], pz[:, SP:SP + 8]), [pzk], [K("s1")], 8)
                 dve(ts(B("s2")[:], B("s1")[:], 15, ALU.bitwise_and), [K("s1")], [K("s2")], 8)
-                dve(tt(B("s3")[:], B("s2")[:], T.base[:], ALU.add), [K("s2"), "base"], [K("s3")], 8, 2)
+                dve(tt(B("s3")[:], B("s2")[:], T.base[:], ALU.add), [K("s2"), "base"], [K("s3")], 16)
                 dve(cp(B("pu")[:], B("s3")[:]), [K("s3")], [K("pu")], 8)
                 on = "xa" if (t == 1 and h == 0) else "xb"
                 w0 = XO + 2048 * h
-                dve(lambda B=B, on=on, w0=w0, h=h: V.tensor_copy(T[on][:, w0:w0 + 2048].indirect(B("pu")[:]), T.yy[:, 128 * h:128 * h + 128]),
-                    [K("pu"), "yy%d" % h], ["%s%d" % (on, h)], 128, 3.8)
+                dve(cp(T[on][:, w0:w0 + 2048].indirect(B("pu")[:]), T.yy[:, 128 * h:128 * h + 128]),
+                    [K("pu"), "yy%d" % h], [K("put"), "%s%d" % (on, h)], 128, "s")
                 if t == 1:
-                    if h == 0:
-                        dma("sp", T.yx[:, 0:2048], T.xa[:, w0:w0 + 2048], ["xa0"], ["yx0"], 1600)
-                    else:
-                        dma("sp", T.yx[:, 2048:4096], T.xb[:, w0:w0 + 2048], ["xb1"], ["yx1"], 1600)
-            if k < 5:
-                ymax(k, 0, 16, T.bz[:, k + 1::8], ["bz0", "bz1"])
+                    dma("sp", T.yx[:, 2048 * h:2048 * h + 2048], T[on][:, w0:w0 + 2048], ["%s%d" % (on, h)], ["yx%d" % h], 1600)
+            for j in YROWS.get(k, ()):
+                ymax(j, [0, 1])
             if k == 4:
-                bzk = ["bz0", "bz1"]
-                dve(ts(T.ds[:], T.bz[:], 0.0, ALU.is_equal), bzk, ["ds"], 128)
-                dve(cp(T.bf[:], T.bz[:]), bzk, ["bf"], 128)
-                dve(lambda: V.tensor_tensor_scan(T.sb[:], T.ds[:], T.bf[:], 0.0, ALU.mult, ALU.add), ["ds", "bf"], ["sb"], 128)
-                dve(lambda: V.tensor_tensor_scan(T.sr[:], T.ds[:], T.ds[:], 0.0, ALU.mult, ALU.add), ["ds"], ["sr"], 128)
-                dve(lambda: V.tensor_scalar(T.bp[:], T.sb[:].indirect(T.po[:, 0:6]), -2048.0 - XO, None, ALU.add), ["sb", "po"], ["bp"], 96, GA)
-                dve(tt(T.bp[:], T.bp[:], T.d0[:, 7::8], ALU.mult), ["d00", "d01"], ["bp"], 96, 2)
-                dve(ts(T.w2[:], L[:], 2048.0, ALU.mult), kb, ["w2"], 96)
-                dve(tt(T.w2[:], T.w2[:], T.kt[:], ALU.add), ["kt"], ["w2"], 96, 2)
-                dve(tt(T.zr[:], T.bp[:], T.w2[:], ALU.add), ["bp", "w2"], ["zr"], 96, 2)
+                dve(scan(T.sr[:], T.ds[:], T.ds[:], ALU.mult, ALU.add), ["ds_0", "ds_1"], ["run"], 144)
+                dve(tt(T.bp[:], T.sb[:].indirect(T.po[:, 0:6]), T.d0[:, 6::NS], ALU.mult), ["sb_0", "sb_1", "po", "d00", "d01"], ["bp"], 96, "g")
+                dve(ts(T.w2[:], L[:], 992.0, ALU.mult), kb, ["w1", "w2"], 96)
+                dve(tt(T.w2[:], T.w2[:], T.kt[:], ALU.add), ["kt"], ["w2"], 192)
+                dve(tt(T.zr[:], T.bp[:], T.w2[:], ALU.add), ["bp", "w2"], ["zr"], 192)
                 dve(ts(T.nl[:], T.zr[:], 5, ALU.arith_shift_right, 4095, ALU.bitwise_and), ["zr"], ["nl"], 96)
-                dve(tt(T.dl[:], T.nl[:], L[:], ALU.subtract), kb + ["nl"], ["dl"], 96, 2)
-                dve(tt(T.aa[:], T.ki[:], I[:], ALU.subtract), kb + ["ki"], ["aa"], 96, 2)
-                dve(lambda: V.tensor_tensor(T.di[:], T.sr[:].indirect(T.po[:, 0:6]), T.aa[:], ALU.subtract), ["sr", "po", "aa"], ["di"], 96, GA)
+                dve(tt(T.dl[:], T.nl[:], L[:], ALU.subtract), kb + ["nl"], ["dl"], 192)
+                dve(tt(T.aa[:], T.ki[:], I[:], ALU.subtract), kb + ["ki"], ["aa"], 192)
+                dve(tt(T.di[:], T.sr[:].indirect(T.po[:, 0:6]), T.aa[:], ALU.subtract), ["run", "po", "aa"], ["di"], 96, "g")
                 sl, si = T["sl%d" % t], T["si%d" % t]
-                settle(0, 80, sl[:], si[:], ["sl%d" % t, "si%d" % t])
+                settle(0, 5, sl[:], si[:], ["sl_%d" % t, "si_%d" % t])
                 if t == 0:
-                    send(0, T.cores[(rank + 1) % n_ranks], [(sl[:], T.l1[:, 0:80]), (si[:], T.i1[:, 0:80])], ["sl0", "si0"], ["st1a"])
+                    send(0, T.cores[(rank + 1) % n_ranks], [(sl[:], T.l1[:, 0:80]), (si[:], T.i1[:, 0:80])], ["sl_0", "si_0"], ["st1a"])
                 else:
-                    send(2, T.cores[(rank - 1) % n_ranks], [(sl[:], T.l2[:]), (si[:], T.i2[:])], ["sl1", "si1"], ["st2a"])
+                    send(2, T.cores[(rank - 1) % n_ranks], [(sl[:], T.l2[:]), (si[:], T.i2[:])], ["sl_1", "si_1"], ["st2a"])
         f5 = T["f5%d" % t]
-        settle(80, 96, f5[:, 0:16], f5[:, 16:32], ["f5l%d" % t, "f5i%d" % t])
+        settle(5, 6, f5[:, 0:16], f5[:, 16:32], ["f5l_%d" % t, "f5i_%d" % t])
         if t == 0:
             send(1, T.cores[(rank + 1) % n_ranks], [(f5[:, 0:16], T.l1[:, 80:96]), (f5[:, 16:32], T.i1[:, 80:96])],
-                 ["f5l0", "f5i0"], ["st1b"])
-            pe(lambda: P.matmul(T.pk0[:, 256:352], T.onb[:], T.dead[:], True, True), ["onb", "deada", "deadb"], ["pk0"], 96)
-            dve(lambda: V.tensor_reduce(T.cn[:, 0:1], T.pk0[:, 256:352], AxisListType.X, ALU.add), [], ["pk0", "cn"], 96)
+                 ["f5l_0", "f5i_0"], ["st1b"])
+            pd, pdk = T["pd%d" % (ring[0] % 2)], "pd%d" % (ring[0] % 2)
+            ring[0] += 1
+            pe(mat(pd[:, 0:96], T.onb[:], T.dead[:], True, True), ["onb", "deada", "deadb"], ["cp", pdk], 96)
+            dve(lambda pd=pd: V.tensor_reduce(T.cn[:, 0:1], pd[:, 0:96], AxisListType.X, ALU.add), [pdk], ["cn"], 96)
             dve(cp(T.ci[:, 0:1], T.cn[:, 0:1]), ["cn"], ["ci"], 1)
             dve(ts(T.cj[:, 0:1], T.ci[:, 0:1], 31, ALU.bitwise_and), ["ci"], ["cj"], 1)
             dve(cp(T.cf[:, 0:1], T.cj[:, 0:1]), ["cj"], ["cf"], 1)
-            dve(ts(T.thr1[:, 0:6], T.thf[:, 0:6], T.cf[:, 0:1], ALU.add, DW, ALU.mult), ["cf", "thf"], ["thr1"], 6)
+            dve(ts(T.cr[64:65, 16::KS], T.onb[64:65, 0:8], T.cf[64:65, 0:1], ALU.mult, DW, ALU.mult), ["cf", "onb"], ["cr2"], 8)
         else:
-            send(3, T.cores[(rank - 1) % n_ranks], [(f5[:], T.r5[:])], ["f5l1", "f5i1"], ["st2b"])
+            send(3, T.cores[(rank - 1) % n_ranks], [(f5[:], T.r5[:])], ["f5l_1", "f5i_1"], ["st2b"])
             dma("act", T.yl[:, 0:80], T.l2[:], ["st2a", "sc_0", "sc_1"], ["yla"], 150)
             dma("act", T.yi[:, 0:80], T.i2[:], ["st2a", "sc_0", "sc_1"], ["yia"], 150)
             dma("act", T.yl[:, 80:96], T.r5[:, 0:16], ["st2b"], ["ylb"], 100)
@@ -381,109 +489,138 @@ def depend(ops):
     return deps
 
 
-def tag(o):
-    w = o["w"][-1]
-    if w[:2] in ("pd", "pk", "yu", "xl", "bz"):
-        w = w[:2]
-    elif w[-2:] in ("_0", "_1"):
-        w = w[:-2]
-    return "%s.%s" % (w, o["r"][0][:2] if o["eng"] == "pe" else "")
+def prices(ops, m):
+    cy, ga, sa, fix, hop, pc, po = m
+    out = []
+    for o in ops:
+        f, n = o["form"], o["n"]
+        if f == "e":
+            out.append(fix + max(64.0, n) * cy)
+        elif f == "g" or f == "s":
+            out.append((50.0 if o["eng"] == "dve" else 65.0) + n * cy * (ga if f == "g" else sa))
+        elif f == "pe":
+            out.append(n * pc + o["m"] * po)
+        else:
+            out.append(n)
+    return out
 
 
-def arrange(ops, deps, shift):
+def above(xs, x):
+    lo, hi = 0, len(xs)
+    while lo < hi:
+        mid = (lo + hi) // 2
+        if xs[mid] <= x:
+            lo = mid + 1
+        else:
+            hi = mid
+    return lo
+
+
+def by_rank(pre, post, rank):
+    left = [len(p) for p in pre]
+    ready = sorted((-rank[i], -i) for i in range(len(pre)) if not left[i])
+    out = []
+    while ready:
+        i = -ready.pop()[1]
+        out.append(i)
+        for j in post[i]:
+            left[j] -= 1
+            if not left[j]:
+                x = (-rank[j], -j)
+                ready.insert(above(ready, x), x)
+    return out
+
+
+def arrange(ops, deps):
     n = len(ops)
-    succ = [[] for _ in range(n)]
+    eng = [o["eng"] for o in ops]
+    succ = [[] for _ in ops]
     for i, d in enumerate(deps):
         for j in d:
             succ[j].append(i)
-    level = [0.0] * n
-    for i in range(n - 1, -1, -1):
-        level[i] = ops[i]["cost"] + ops[i]["lat"] + (ops[i]["n"] if ops[i]["kind"] == "dma" else 0.0) + max([level[j] + HOP for j in succ[i]] or [0.0])
-    level = [level[i] + shift[i] if i >= NFIRST else 1.0e9 - i for i in range(n)]
-    bus = 0.0
-    left = [len(d) for d in deps]
-    ready = [i for i in range(n) if left[i] == 0]
-    rt, end, free, order, start = [0.0] * n, [0.0] * n, {}, [], [0.0] * n
-    while ready:
-        st = {i: max(rt[i], free.get(ops[i]["eng"], 0.0)) for i in ready}
-        first = min(ready, key=lambda i: (st[i], -level[i]))
-        near = [i for i in ready if ops[i]["eng"] == ops[first]["eng"] and st[i] <= st[first] + CFG["win"]]
-        best = max(near, key=lambda i: level[i])
-        bs = st[best]
-        ready.remove(best)
-        o = ops[best]
-        start[best] = bs
-        if o["eng"]:
-            free[o["eng"]] = bs + o["cost"]
-        end[best] = bs + o["cost"] + o["lat"]
-        if o["kind"] == "dma" and o["n"]:
-            bus = end[best] = max(end[best], bus) + o["n"]
-        order.append(best)
-        for j in succ[best]:
-            same = o["eng"] == "pe" and ops[j]["eng"] == "pe"
-            rt[j] = max(rt[j], end[best] + (0.0 if same else HOP))
-            left[j] -= 1
-            if left[j] == 0:
-                ready.append(j)
-    return order, start, end
-
-
-def replay(ops, deps, order, ga, fix, hop, pc):
-    end, free = {}, {}
-    for i in order:
-        o = ops[i]
-        e, c = o["eng"], o["cost"]
-        if o["kind"] == "c" and e in ("dve", "act"):
-            c = 60.0 + o["n"] * ga * CY if o["per"] == GA else fix + max(64.0, o["n"] * o["per"]) * CY
-        elif e == "pe":
-            c = o["n"] * pc
-        s = free.get(e, 0.0) if e else 0.0
-        for j in deps[i]:
-            x = end[j] + (0.0 if e == "pe" and ops[j]["eng"] == "pe" else hop)
-            if x > s:
-                s = x
-        free[e] = s + c
-        end[i] = s + c + o["lat"]
-        if o["kind"] == "dma" and o["n"]:
-            free["bus"] = end[i] = max(end[i], free.get("bus", 0.0)) + o["n"]
-    return max(end.values())
-
-
-def search(ops, deps):
+    waited = [[j for j in d if not (eng[i] == "pe" and eng[j] == "pe")] for i, d in enumerate(deps)]
+    costs = [prices(ops, m) for m in COSTS]
+    bus = [o["m"] if o["kind"] == "dma" else 0 for o in ops]
     seed = [CFG["seed"]]
 
-    def rnd(k):
+    def rnd():
         seed[0] = (seed[0] * 1103515245 + 12345) % 2147483648
-        return (seed[0] >> 8) % k
+        return (seed[0] >> 8) / 8388608.0
 
-    def score(p):
-        order = arrange(ops, deps, p)[0]
-        return sum(replay(ops, deps, order, *m) for m in COSTS) / len(COSTS)
-    kinds = {}
-    for i, o in enumerate(ops):
-        kinds.setdefault(tag(o), []).append(i)
-    names = sorted(k for k in kinds if len(kinds[k]) >= 10)
-    steps = [-8000.0, -4000.0, -2000.0, 0.0, 2000.0, 4000.0, 8000.0, 12000.0]
-    p = [0.0] * len(ops)
-    best = score(p)
-    for it in range(CFG["n1"] + CFG["n2"]):
-        q = list(p)
-        for _ in range(1 + rnd(3)):
-            v = steps[rnd(8)]
-            if it < CFG["n1"]:
-                for i in kinds[names[rnd(len(names))]]:
-                    q[i] = v
-            else:
-                q[rnd(len(ops))] = 2 * v
-        s = score(q)
-        if s <= best:
-            best, p = s, q
-    return p, best
+    def replay(order, cost, hop):
+        end, free, wire = [0.0] * n, {}, 0.0
+        for i in order:
+            t = free.get(eng[i], 0.0) - hop if eng[i] else -hop
+            for j in waited[i]:
+                if end[j] > t:
+                    t = end[j]
+            t += hop + cost[i]
+            free[eng[i]] = t
+            t += ops[i]["lat"]
+            if bus[i]:
+                wire = t = max(t, wire) + bus[i]
+            end[i] = t
+        return end
+
+    def length(order):
+        return sum(max(replay(order, c, m[4])) for c, m in zip(costs, COSTS)) / len(COSTS)
+
+    def pack(rank, cost, hop, back):
+        pre, post = (succ, deps) if back else (deps, succ)
+        start, lo, hi = [0.0] * n, {}, {}
+        for i in by_rank(pre, post, rank):
+            e, r, c = eng[i], 0.0, cost[i]
+            for j in pre[i]:
+                x = start[j] + cost[j] + (lat[i] if back else lat[j]) + (0.0 if e == "pe" and eng[j] == "pe" else hop)
+                if x > r:
+                    r = x
+            if e:
+                a, b = lo.setdefault(e, []), hi.setdefault(e, [])
+                k = above(b, r)
+                while k < len(a) and r + c > a[k] + 1e-9:
+                    r = max(r, b[k])
+                    k += 1
+                a.insert(k, r)
+                b.insert(k, r + c)
+            start[i] = r
+        return start
+    loads = [i for i in range(n) if ops[i]["kind"] == "dma" and ops[i]["first"]]
+    lat = [o["lat"] + b for o, b in zip(ops, bus)]
+    wire = 0.0
+    for i in loads:
+        wire += bus[i]
+        lat[i] = ops[i]["lat"] + (wire if bus[i] else 0.0)
+    now = best = list(range(n))
+    tnow = tbest = length(best)
+    for it in range(CFG["rounds"]):
+        w = [rnd() + 0.01 for _ in COSTS]
+        w = [x / sum(w) for x in w]
+        f = {e: 0.86 + 0.28 * rnd() for e in QUEUES}
+        cost = [sum(x * c[i] for x, c in zip(w, costs)) * f[eng[i]] * (0.86 + 0.28 * rnd()) for i in range(n)]
+        hop = sum(x * m[4] for x, m in zip(w, COSTS))
+        at = [0] * n
+        for k, i in enumerate(now):
+            at[i] = k
+        fore = pack(at, cost, hop, False)
+        for rep in range(2):
+            back = pack([-(fore[i] + cost[i] + lat[i]) for i in range(n)], cost, hop, True)
+            rank = [-(back[i] + cost[i]) for i in range(n)]
+            for k, i in enumerate(loads):
+                rank[i] = k - 1.0e12
+            fore = pack(rank, cost, hop, False)
+            order = by_rank(deps, succ, fore)
+            x = length(order)
+            if x < tnow + 300:
+                now, tnow = order, x
+            if x < tbest:
+                best, tbest = order, x
+    return best, tbest
 
 
 def plan(ops):
     deps = depend(ops)
-    order, start, end = arrange(ops, deps, search(ops, deps)[0])
+    order = arrange(ops, deps)[0]
+    at = {i: n for n, i in enumerate(order)}
     pos, cnt = {}, {}
     for i in order:
         o = ops[i]
@@ -500,7 +637,7 @@ def plan(ops):
             continue
         kn = known.setdefault(o["eng"], {})
         ws = []
-        for j in sorted(deps[i], key=lambda j: -end[j]):
+        for j in sorted(deps[i], key=lambda j: -at[j]):
             if o["eng"] == "pe" and ops[j]["eng"] == "pe":
                 continue
             s, v = pos[j]
@@ -523,7 +660,7 @@ def plan(ops):
                 value[i] = (o["eng"], cnt[o["eng"]])
         else:
             value[i] = (o["sem"], o["val"])
-    return order, waits, marked, value, start, end
+    return order, waits, marked, value
 
 
 PLAN = {}
@@ -535,7 +672,7 @@ def rank_program(g, core, T, topo):
     ops = build(g, core, T, topo)
     if "p" not in PLAN:
         PLAN["p"] = plan(ops)
-    order, waits, marked, value = PLAN["p"][:4]
+    order, waits, marked, value = PLAN["p"]
     queue = {"pe": g.tensor, "dve": g.vector, "act": g.scalar, "pool": g, "sp": g.sync}
     for i in order:
         o = ops[i]

@@ -1,11 +1,13 @@
 from concourse.bass import DstId, RemoteDMATransfer
 from concourse.mybir import AluOpType as ALU, AxisListType, ActivationFunctionType as ACT
 
-CFG = {"cuts": [("act", 64, 128), ("act", 0, 32), ("act", 32, 64)], "runs": [(64, 128), (0, 32), (32, 64)],
-       "relu": [(2, 4, 64)], "at": {}, "seed": 1, "rounds": 900}
+CFG = {"cuts": [("act", 0, 64), ("act", 64, 96), ("act", 96, 120), ("dve", 120, 128)], "runs": [(0, 64), (64, 96), (96, 128)],
+       "druns": [(0, 64), (64, 128)], "b2": 64, "b3": 64, "skv": True, "ska": (3,), "fg4": True, "cu": 4, "at": {}, "seed": 1, "rounds": 300,
+       "amp": (0.1, 0.06), "back": 100000, "slack": 200, "moves": 8500}
 for _t in (0, 1):
-    CFG["at"][_t, 0, 0] = {"cuts": [("act", 64, 128), ("dve", 0, 32), ("dve", 32, 64)]}
-    CFG["at"][_t, 5, 0] = CFG["at"][_t, 5, 1] = {"relu": [(2, 4, 64), (0, 2, 64)], "runs": [(0, 32), (32, 64)]}
+    CFG["at"][_t, 0, 0] = {"cuts": [("act", 0, 64), ("act", 64, 80), ("dve", 80, 128)], "cu": 8}
+    for _k, _h in ((4, 1), (5, 0), (5, 1)):
+        CFG["at"][_t, _k, _h] = {"b2": 96, "b3": 96, "cuts": [("act", 0, 64), ("act", 64, 96), ("act", 96, 128)]}
 XO = 32
 XW = XO + 4096
 FW = 2048 + 8
@@ -14,42 +16,46 @@ DW = 131072.0
 MID = 2048.0
 DEAD = -2080.0
 LIFT = 1056.0
-KS, NS = 20, 9
+KS, NS = 20, 10
 RKEY = 1.5 * 2.0 ** 36
 RIDX = 1.5 * 2.0 ** 39
 YROWS = {1: (0, 1), 3: (2, 3), 4: (4,)}
-BZ, BK, SP, Z0, Z1, Z2 = 0, 80, 136, 160, 256, 352
+RSUM = 1.5 * 2.0 ** 27
+BZ, BK, SP = 0, 160, 80
 
 SCRATCH = {
     "xa": ("sbuf", [128, XW], "bfloat16"), "xb": ("sbuf", [128, XW], "bfloat16"),
     "fi": ("sbuf", [128, FW], "int32"),
     "l0": ("sbuf", [128, 96], "int32"), "i0": ("sbuf", [128, 96], "int32"),
     "l1": ("sbuf", [128, 96], "float32"), "i1": ("sbuf", [128, 96], "float32"),
-    "l2": ("sbuf", [128, 80], "float32"), "i2": ("sbuf", [128, 80], "float32"), "r5": ("sbuf", [128, 32], "float32"),
-    "sl0": ("sbuf", [128, 80], "float32"), "si0": ("sbuf", [128, 80], "float32"), "f50": ("sbuf", [128, 32], "float32"),
-    "sl1": ("sbuf", [128, 80], "float32"), "si1": ("sbuf", [128, 80], "float32"), "f51": ("sbuf", [128, 32], "float32"),
+    "l2": ("sbuf", [128, 96], "float32"), "i2": ("sbuf", [128, 96], "float32"),
+    "lf": ("sbuf", [128, 96], "float32"), "if0": ("sbuf", [128, 96], "float32"),
     "exi": ("sbuf", [128, 16], "int32"), "th8": ("sbuf", [128, 8], "int32"), "thf": ("sbuf", [128, 8], "float32"),
-    "thm": ("sbuf", [128, 48], "bfloat16"), "wti": ("sbuf", [128, 4], "int32"), "wtf": ("sbuf", [128, 4], "float32"),
+    "wti": ("sbuf", [128, 4], "int32"), "wtf": ("sbuf", [128, 4], "float32"),
     "mm": ("sbuf", [128, 96 * NS], "float32"), "d0": ("sbuf", [128, 96 * NS], "float32"),
     "yu": ("sbuf", [128, 6, 16], "uint16"), "lu": ("sbuf", [128, 96], "uint16"),
     "xl": ("sbuf", [128, 1536], "bfloat16"), "yy": ("sbuf", [128, 256], "bfloat16"),
     "onb": ("sbuf", [128, 128], "bfloat16"), "idb": ("sbuf", [128, 128], "bfloat16"), "nid": ("sbuf", [128, 128], "bfloat16"),
     "idk": ("sbuf", [128, 8 * KS], "float16"), "iv": ("sbuf", [128, 8 * KS], "float32"), "cr": ("sbuf", [128, 8 * KS], "bfloat16"),
-    "gq": ("sbuf", [128, 8 * KS], "bfloat16"), "gr24": ("sbuf", [128, 8 * KS], "bfloat16"), "gr34": ("sbuf", [128, 8 * KS], "bfloat16"),
-    "gr02": ("sbuf", [128, 8 * KS], "bfloat16"), "gr23": ("sbuf", [128, 8 * KS], "bfloat16"), "gr14": ("sbuf", [128, 8 * KS], "bfloat16"),
+    "thm": ("sbuf", [128, 48], "bfloat16"), "gq4": ("sbuf", [128, 8 * KS], "bfloat16"), "gq2": ("sbuf", [128, 8 * KS], "bfloat16"),
+    "i2x": ("sbuf", [128, 16], "float32"), "wg": ("sbuf", [128, 16], "bfloat16"), "cw": ("sbuf", [128, 48], "bfloat16"),
+    "d6": ("sbuf", [128, 48], "float32"), "p16": ("sbuf", [128, 128], "bfloat16"), "e6": ("sbuf", [128, 8], "uint16"),
     "ig": ("sbuf", [128, 8 * KS], "float32"), "im": ("sbuf", [128, 8 * KS], "float32"),
-    "g8": ("sbuf", [128, 8], "bfloat16"), "gv": ("sbuf", [128, 8], "bfloat16"), "up8": ("sbuf", [128, 8], "bfloat16"),
+    "g8": ("sbuf", [128, 8], "bfloat16"), "gv": ("sbuf", [128, 8], "bfloat16"),
     "bm": ("sbuf", [128, 8], "float16"), "bm32": ("sbuf", [128, 8], "float16"),
     "pi": ("sbuf", [128, 4], "int32"), "pa": ("sbuf", [128, 4], "int32"), "pb": ("sbuf", [128, 4], "int32"),
     "pf": ("sbuf", [128, 12], "float32"), "ia": ("sbuf", [128, 128], "float32"), "ma": ("sbuf", [128, 128], "float32"),
-    "ix": ("sbuf", [128, 144], "float32"), "uw": ("sbuf", [128, 144], "bfloat16"), "rs": ("sbuf", [128, 8 * KS], "float32"),
+    "rs": ("sbuf", [128, 8 * KS], "float32"),
     "ic": ("sbuf", [128, 8], "float32"), "eo": ("sbuf", [128, 8], "uint16"), "po": ("sbuf", [128, 8], "uint16"),
-    "base": ("sbuf", [128, 8], "int32"), "kt": ("sbuf", [128, 96], "float32"), "ki": ("sbuf", [128, 96], "float32"),
+    "kt": ("sbuf", [128, 96], "float32"), "ki": ("sbuf", [128, 96], "float32"),
     "dx": ("sbuf", [128, 16 * NS], "float32"), "ds": ("sbuf", [128, 16 * NS], "float32"), "sb": ("sbuf", [128, 16 * NS], "float32"),
     "sr": ("sbuf", [128, 16 * NS], "float32"), "bp": ("sbuf", [128, 96], "float32"), "w2": ("sbuf", [128, 96], "float32"),
     "zr": ("sbuf", [128, 96], "int32"), "nl": ("sbuf", [128, 96], "int32"), "dl": ("sbuf", [128, 96], "float32"),
     "aa": ("sbuf", [128, 96], "float32"), "di": ("sbuf", [128, 96], "float32"), "dead": ("sbuf", [128, 96], "bfloat16"),
-    "tl": ("sbuf", [128, 96], "float32"), "ti": ("sbuf", [128, 96], "float32"),
+    "ex32": ("sbuf", [128, 16], "float32"), "b0": ("sbuf", [128, 16], "float32"), "z0": ("sbuf", [128, 16], "int32"),
+    "n0": ("sbuf", [128, 16], "int32"), "dl0": ("sbuf", [128, 16], "float32"),
+    "tl0": ("sbuf", [128, 96], "float32"), "ti0": ("sbuf", [128, 96], "float32"),
+    "tl1": ("sbuf", [128, 96], "float32"), "ti1": ("sbuf", [128, 96], "float32"),
     "cn": ("sbuf", [128, 4], "float32"), "ci": ("sbuf", [128, 4], "int32"), "cj": ("sbuf", [128, 4], "int32"),
     "cf": ("sbuf", [128, 4], "float32"),
 }
@@ -57,10 +63,12 @@ for _h in (0, 1):
     for _n in ("pk", "pz", "pq", "pd"):
         SCRATCH["%s%d" % (_n, _h)] = ("psum", [128, 512], "float32")
     for _n, _w, _t in (("pr", 8 * NS, "float32"), ("ss", 16 * NS, "float32"), ("nb", 16, "uint16"), ("cu", 128, "uint16"),
-                       ("fg", 128, "float16"), ("q", 128, "bfloat16"), ("sc", 8 * KS, "float32"), ("lo", 8, "float32"),
-                       ("rx", 128, "float16"), ("s1", 8, "int32"), ("s2", 8, "int32"), ("s3", 8, "int32"), ("pu", 8, "uint16")):
+                       ("fg", 128, "float16"), ("q", 128, "bfloat16"),
+                       ("rx", 128, "float16"), ("sp", 48, "float32"), ("pu", 8, "uint16")):
         SCRATCH["%s_%d" % (_n, _h)] = ("sbuf", [128, _w], _t)
     SCRATCH["a_%d" % _h] = ("sbuf", [128, 4, 512], "bfloat16")
+    SCRATCH["sc_%d" % _h] = ("sbuf", [128, 8 * KS], "float32")
+    SCRATCH["lo_%d" % _h] = ("sbuf", [128, 8], "float32")
     SCRATCH["v_%d" % _h] = ("sbuf", [128, 2048], "bfloat16")
 
 NDMA = 24
@@ -68,8 +76,9 @@ SEMAPHORES = ["pe", "dve", "act", "pool"] + ["m%d" % _i for _i in range(NDMA)] +
              ["arr%d" % _i for _i in range(4)] + ["out%d" % _i for _i in range(4)]
 
 QUEUES = ("pe", "dve", "act", "pool", "sp", None)
-COSTS = [(1.04, 1.56, 3.8, 30.0, 100.0, 0.52, 5.0), (0.9, 1.56, 3.8, 20.0, 160.0, 0.52, 5.0),
-         (0.95, 1.3, 3.8, 20.0, 70.0, 0.75, 0.0), (1.1, 1.9, 4.5, 30.0, 100.0, 0.55, 10.0)]
+COSTS = [(0.88, 1.56, 3.8, 10.0, 30.0, 64, 110.0, 200.0, 250.0, 0.66, 0.0, 0.9), (0.85, 1.5, 3.8, 20.0, 60.0, 64, 150.0, 150.0, 200.0, 0.7, 0.0, 0.65),
+         (0.91, 1.61, 3.8, 18.0, 10.0, 64, 61.0, 81.0, 300.0, 0.67, 0.0, 1.2), (0.88, 1.44, 3.8, 7.0, 138.0, 64, 89.0, 150.0, 128.0, 0.76, 0.5, 0.65),
+         (1.2, 1.9, 4.5, 20.0, 60.0, 64, 120.0, 150.0, 200.0, 0.95, 0.3, 0.9)]
 
 
 def build(g, core, T, topo):
@@ -145,7 +154,7 @@ def build(g, core, T, topo):
             for i, (src, land) in enumerate(pairs):
                 m = sum(1 << e for e in eng[i * share:(i + 1) * share])
                 trs.append(RemoteDMATransfer(dst_ids=[DstId(rid=rid, pnc=pid)], dma_engine_mask=m,
-                                             remote_sem=T.sem["arr%d" % idx], src=src, dst=land))
+                                             remote_sem=T.sem["arr%d" % idx], srcs=src, dsts=[land], alu_op=1))
             return g.remote_dma_fused(trs, local_sem=T.sem["out%d" % idx])
         op("pool", fn, r, ["sent%d" % idx], "ns", 300.0, 0, "send", "out%d" % idx, share * len(pairs), 2500.0)
         op(None, None, ["sent%d" % idx], w, "ns", 0.0, 0, "recv", "arr%d" % idx, share * len(pairs), 500.0)
@@ -159,76 +168,82 @@ def build(g, core, T, topo):
     dma("act", T.th8[0:8, 0:6], T.th[:], [], ["th8"], 0)
     dma("act", T.fi[:, 2048:FW], T.fa[:, 0:8], [], ["fie"], 0)
 
-    mmk, d0k = ["mm7", "mm8"], ["d0z"]
+    mmk, d0k = ["mm6", "mm8", "mm9"], ["d0z"]
     pool(lambda: g.iota(T.pi[:, 0:1], [[1, 1]], 0, 1), [], ["pi"], 1)
     pool(iota(T.ic[:], [[1, 8]], 0), [], ["ic"], 8)
     dve(ms(T.onb[:], 1.0), [], ["onb"], 64)
     pool(iota(T.ig[:], [[1, 8], [0, KS]], 0), [], ["ig"], 160)
-    pool(iota(T.d0[:], [[0, 96 * NS]], 1), [], ["d0z"], 864)
+    dve(ms(T.d0[:], 1.0), [], ["d0z"], 960)
     pool(lambda: g.affine_select(T.idb[:], T.onb[:], [[-1, 128]], ALU.is_equal, 0.0, 0, 1), ["onb"], ["idb"], 128)
     pool(iota(T.im[:], [[0, 8], [1, KS]], 0), [], ["im"], 160)
     pool(iota(T.iv[:], [[32, 8], [1, KS]], 0), [], ["iv"], 160)
     pool(iota(T.ia[:], [[0, 8], [1, 16]], 0), [], ["ia"], 128)
-    dma("pool", T.wti[:, 0:1], T.wt[:], [], ["wti"], 0, slow=True)
-    pool(iota(T.ix[:], [[1, 144]], -15), [], ["ix"], 144)
-    pool(iota(T.kt[:], [[32, 6], [0, 16]], 992 * 1184 - KSUB), [], ["kt"], 96)
+    pool(iota(T.i2x[:], [[1, 8], [0, 2]], 0), [], ["i2x"], 16)
+    pool(iota(T.p16[0:1, :], [[16, 128]], 0), [], ["p16"], 128)
+    pool(iota(T.kt[:], [[32, 6], [0, 16]], 2048 * 1184 - KSUB), [], ["kt"], 96)
     pool(iota(T.ki[:], [[1, 6], [0, 16]], -1), [], ["ki"], 96)
-    dve(ms(T.mm[:, 7::NS], RIDX), [], ["mm7"], 96)
-    dve(ms(T.mm[:, 8::NS], -RIDX), [], ["mm8"], 96)
+    dma("pool", T.wti[:, 0:1], T.wt[:], ["idb", "im", "iv", "ia", "i2x", "p16", "kt", "ki"], ["wti"], 0, slow=True)
+    dve(ms(T.mm[:, 6::NS], 32 * LIFT), [], ["mm6"], 96)
+    dve(ms(T.mm[:, 8::NS], RIDX), [], ["mm8"], 96)
+    dve(ms(T.mm[:, 9::NS], -RIDX), [], ["mm9"], 96)
     for h in (0, 1):
-        dve(ms(T["pz%d" % h][:, BZ:BZ + 8 * NS], 1.0), [], ["pz%d" % h], 72)
+        dve(ms(T["pz%d" % h][:, BZ:BZ + 8 * NS], 1.0), [], ["pz%d" % h], 80)
+    dve(ms(T.cw[0:1, :], 0.0), [], ["cw0", "cw1", "cw2"], 24)
+    dve(ms(T.d6[:], 1.0), [], ["d60", "d63"], 48)
+    for i, c in enumerate((-7.5, RSUM, -RSUM)):
+        dve(ms(T.cw[0:1, i::6], c), [], ["cw%d" % i], 8)
+    dve(ms(T.d6[:, 0::6], 0.0), [], ["d60"], 8)
+    dve(ms(T.d6[:, 3::6], -1.0), [], ["d63"], 8)
     for name in ("xa", "xb"):
         dve(ms(T[name][:, 0:16], 64.0), [], [name + "s"], 8)
         dve(ms(T[name][:, 16:XO], 0.0), [], [name + "z"], 8)
     dve(ms(T.rs[:], 0.0), [], ["rs0", "rs1", "rs2"], 160)
-    dve(ms(T.cr[:], 0.0), [], ["cr0", "cr1", "cr2", "cr3"], 80)
-    dve(ms(T.up8[:], 32 * LIFT), [], ["up8"], 8)
+    crk = ["cm", "cb", "ca"]
+    dve(ms(T.cr[:], 0.0), [], crk, 80)
     dve(ts(T.pa[:, 0:1], T.pi[:, 0:1], 15, ALU.bitwise_and), ["pi"], ["pa"], 1)
     dve(ts(T.pb[:, 0:1], T.pi[:, 0:1], 4, ALU.arith_shift_right), ["pi"], ["pb"], 1)
     dve(ms(T.rs[:, 0::KS], 1.0e9), [], ["rs0"], 8)
     dve(ms(T.rs[:, 17::KS], RKEY), [], ["rs1"], 8)
     dve(ms(T.rs[:, 18::KS], -RKEY), [], ["rs2"], 8)
-    dve(ms(T.cr[32:33, :], -120 * DW), [], ["cr1"], 80)
+    dve(ms(T.cr[64:65, :], -120 * DW), [], ["ca"], 80)
     dve(cp(T.pf[:, 0:1], T.pa[:, 0:1]), ["pa"], ["pf0"], 1)
     dve(cp(T.pf[:, 1:2], T.pb[:, 0:1]), ["pb"], ["pf1"], 1)
     act(lin(T.pf[:, 2:3], T.pf[:, 1:2], 32.0, T.pf[:, 0:1]), ["pf0", "pf1"], ["pf2"], 1)
-    act(lin(T.pf[:, 3:4], T.pf[:, 1:2], 16.0), ["pf1"], ["pf3"], 1)
-    act(lin(T.pf[:, 4:5], T.pf[:, 0:1], 16.0), ["pf0"], ["pf4"], 1)
     act(lin(T.pf[:, 5:6], T.pf[:, 0:1], float(NS)), ["pf0"], ["pf5"], 1)
     phase[0] = -7
     for h in (0, 1):
-        dve(ts(T["pz%d" % h][:, BZ:BZ + 8 * NS:NS], T.exi[:, 8 * h:8 * h + 8], 32.0, ALU.mult, 32 * (LIFT - MID), ALU.add),
+        dve(ts(T["pz%d" % h][:, BZ:BZ + 8 * NS:NS], T.exi[:, 8 * h:8 * h + 8], 32.0, ALU.mult, -32 * MID, ALU.add),
             ["exi"], ["pz%d" % h], 8)
+    dve(ts(T.ex32[:], T.exi[:], 32.0, ALU.mult, -32 * MID, ALU.add), ["exi"], ["ex32"], 16)
+    dve(ms(T.i1[:, 0:16], -1.0), [], ["i1z"], 16)
     dve(ts(T.thf[0:8, 0:6], T.th8[0:8, 0:6], DW, ALU.mult), ["th8"], ["thf"], 6)
     phase[0] = -6
     dve(ms(T.d0[:, 0::NS], 0.0), [], ["d0z"], 96)
     act(lin(T.nid[:], T.idb[:], -1.0), ["idb"], ["nid"], 128)
     for k in range(6):
-        act(lin(T.thm[0:8, 8 * k:8 * k + 8], T.idb[0:8, 0:8], T.thf[0:8, k:k + 1]), ["idb", "thf"], ["thm%d" % k], 8)
+        act(lin(T.thm[0:8, 8 * k:8 * k + 8], T.idb[0:8, 0:8], T.thf[0:8, k:k + 1]), ["idb", "thf"], ["th%d" % k], 8)
+    dve(ts(T.cr[0:1, :], T.im[0:1, :], 8192.0, ALU.mult), ["im"], ["cm"], 160)
+    dve(ts(T.cr[32:33, :], T.im[32:33, :], 16.0, ALU.is_gt, 2.0 ** 40, ALU.mult), ["im"], ["cb"], 160)
+    dve(ms(T.cr[0:1, 16::KS], DEAD), [], ["cm"], 8)
     phase[0] = -8.5
     dve(ts(T.g8[:], T.ic[:], T.pf[:, 1:2], ALU.is_equal, 2 * DW, ALU.mult), ["ic", "pf1"], ["g8"], 8)
     act(lin(T.gv[:], T.g8[:], -0.5), ["g8"], ["gv"], 8)
     dve(ts(T.bm[:], T.ic[:], T.pf[:, 1:2], ALU.is_equal), ["ic", "pf1"], ["bm"], 8)
     dve(ts(T.bm32[:], T.ic[:], T.pf[:, 1:2], ALU.is_equal, 32.0, ALU.mult), ["ic", "pf1"], ["bm32"], 8)
+    dve(ts(T.ma[:], T.ia[:], T.pf[:, 0:1], ALU.is_equal), ["ia", "pf0"], ["ma"], 128)
     dve(cp(T.eo[:], T.ic[:]), ["ic"], ["eo"], 8)
     dve(ts(T.po[:], T.ic[:], T.pf[:, 5:6], ALU.add), ["ic", "pf5"], ["po"], 8)
-    dve(ts(T.base[:], T.ic[:], 256.0, ALU.mult, T.pf[:, 4:5], ALU.add), ["ic", "pf4"], ["base"], 8)
-    dve(ts(T.gq[:], T.ig[:], T.pf[:, 1:2], ALU.is_equal, -DW, ALU.mult), ["ig", "pf1"], ["gq"], 160)
-    dve(ms(T.gq[:, 16::KS], 0.0), [], ["gq"], 8)
-    for j0, j1 in sorted({r[:2] for c in [CFG] + list(CFG["at"].values()) for r in c.get("relu", ())}):
-        gr = T["gr%d%d" % (j0, j1)]
-        dve(ms(gr[:], 0.0), [], ["gr%d%d" % (j0, j1)], 80)
-        for j in range(j0, j1):
-            act(lin(gr[:, j::4], T.gq[:, j::4], -2.0), ["gq"], ["gr%d%d" % (j0, j1)], 40)
+    dve(ts(T.e6[:], T.ic[:], 6.0, ALU.mult, 3.0, ALU.add), ["ic"], ["e6"], 8)
+    dve(ts(T.gq4[:], T.ig[:], T.pf[:, 1:2], ALU.is_equal, -DW, ALU.mult), ["ig", "pf1"], ["gq4"], 160)
+    dve(ms(T.gq4[:, 16::KS], 0.0), [], ["gq4"], 8)
+    dve(ms(T.gq2[:], 0.0), [], ["gq20", "gq21"], 80)
+    for j in (0, 1):
+        dve(cp(T.gq2[:, j::4], T.gq4[:, j::4]), ["gq4"], ["gq2%d" % j], 20)
     phase[0] = -5
-    act(lin(T.cr[0:1, :], T.im[0:1, :], 8192.0), ["im"], ["cr0"], 160)
-    dve(ts(T.cr[96:97, :], T.im[96:97, :], 16.0, ALU.is_gt, 2.0 ** 40, ALU.mult), ["im"], ["cr3"], 160)
-    dve(ms(T.cr[0:1, 16::KS], DEAD), [], ["cr0"], 8)
     dve(ts(T.idk[:], T.iv[:], T.pf[:, 2:3], ALU.is_equal), ["iv", "pf2"], ["idk"], 160)
-    dve(ts(T.ma[:], T.ia[:], T.pf[:, 0:1], ALU.is_equal), ["ia", "pf0"], ["ma"], 128)
     phase[0] = -2
     dve(cp(T.wtf[:, 0:1], T.wti[:, 0:1]), ["wti"], ["wtf"], 1)
-    dve(ts(T.uw[:], T.ix[:], T.pf[:, 3:4], ALU.is_equal, T.wtf[:, 0:1], ALU.mult), ["ix", "pf3", "wtf"], ["uw"], 144)
+    dve(ts(T.wg[:], T.i2x[:], T.pf[:, 1:2], ALU.is_equal, T.wtf[:, 0:1], ALU.mult), ["i2x", "pf1", "wtf"], ["wg"], 16)
     dma("sp", T.xb[:, XO:XW], T.xs[:], ["fi"], ["xb0", "xb1"], 3200)
 
     ring = [0]
@@ -236,19 +251,15 @@ def build(g, core, T, topo):
         X = T.xa if t == 0 else T.xb
         xn = "xa" if t == 0 else "xb"
         xk = [xn + "0", xn + "1"]
-        L, I = (T.l0, T.i0) if t == 0 else (T.l1, T.i1)
-        ka, kb = (["l0"], ["l0", "i0"]) if t == 0 else (["st1a"], ["st1a", "st1b"])
+        L, I = (T.lf, T.if0) if t == 0 else (T.l1, T.i1)
+        ka, kb = (["lf"], ["lf", "if0"]) if t == 0 else (["st1a"], ["st1a", "st1b", "i1z"])
         wadd = float(992 * 1184 + 32 * 77 * t - 32768 - KSUB)
 
         def prep(c0, c1, part, keys, t=t, L=L):
-            a, b = T.d0[:, NS * c0 + 6:NS * c1:NS], T.mm[:, NS * c0 + 6:NS * c1:NS]
+            a, b = T.d0[:, NS * c0 + 7:NS * c1:NS], T.mm[:, NS * c0 + 7:NS * c1:NS]
             dve(cp(T.lu[:, c0:c1], L[:, c0:c1]), keys, ["lu%d" % p for p in part], c1 - c0)
-            if t == 0:
-                dve(ts(a, L[:, c0:c1], 1184.0, ALU.add, 1.0 / 32, ALU.mult), keys + d0k, ["d0%d" % p for p in part], c1 - c0)
-                dve(ts(b, L[:, c0:c1], 1024.0, ALU.mult, wadd, ALU.add), keys, ["mw%d" % p for p in part], c1 - c0)
-            else:
-                act(lin(a, L[:, c0:c1], 1.0 / 32, 37.0), keys, ["d0%d" % p for p in part], c1 - c0)
-                act(lin(b, L[:, c0:c1], 1024.0, wadd), keys, ["mw%d" % p for p in part] + ["mk5"] * part[0], c1 - c0)
+            act(lin(a, L[:, c0:c1], 1.0 / 32, 37.0), keys + d0k, ["d0%d" % p for p in part], c1 - c0)
+            act(lin(b, L[:, c0:c1], 1024.0, wadd), keys, ["mw%d" % p for p in part], c1 - c0)
 
         def masks(keys, t=t, I=I):
             for s in range(6):
@@ -257,10 +268,12 @@ def build(g, core, T, topo):
 
         def xl(k0, k1, X=X, xk=xk):
             act(lambda: S.activation(T.xl[:, 256 * k0:256 * k1], X[:, XO:XW].indirect(T.lu[:, 16 * k0:16 * k1]), ACT.Copy),
-                xk + ["lu%d" % min(k0, 1)], ["xl%d" % k for k in range(k0, k1)], 256 * (k1 - k0), "g")
+                xk + ["lu%d" % min(k0, 1)], ["xl%d_%d" % (k, h) for k in range(k0, k1) for h in (0, 1)], 256 * (k1 - k0), "g")
 
         if t == 0:
             phase[0] = -8
+            dve(cp(T.lf[:], T.l0[:]), ["l0"], ["lf"], 96)
+            dve(cp(T.if0[:], T.i0[:]), ["i0"], ["if0"], 96)
             prep(0, 96, (0, 1), ka)
             masks(kb)
             phase[0] = -4
@@ -270,12 +283,14 @@ def build(g, core, T, topo):
         else:
             phase[0] = 12
             prep(0, 16, (0,), ka)
-            xl(0, 1)
+            for h in (0, 1):
+                act(lambda h=h, X=X: S.activation(T.xl[:, 128 * h:128 * h + 128], X[:, XO:XW].indirect(T.lu[:, 8 * h:8 * h + 8]), ACT.Copy),
+                    xk + ["lu0"], ["xl0_%d" % h], 128, "g")
             dma("sp", T.xa[:, XO:XO + 2048], T.xb[:, XO:XO + 2048], ["xb0", "sent1"], ["xa0"], 1600)
 
         def ylist(k0, k1, h):
-            dve(ts(T.yu[:, k0:k1, 8 * h:8 * h + 8], T["pz%d" % h][:, BK + 8 * k0:BK + 8 * k1], MID + 16, ALU.add, 0.0, ALU.max),
-                ["pz%d" % h], ["yu%d_%d" % (k, h) for k in range(k0, k1)], 8 * (k1 - k0))
+            dve(ts(T.yu[:, k0:k1, 8 * h:8 * h + 8], T["pk%d" % h][:, BK + 8 * k0:BK + 8 * k1], MID + 16, ALU.add, 0.0, ALU.max),
+                ["pk%d" % h], ["yu%d_%d" % (k, h) for k in range(k0, k1)], 8 * (k1 - k0))
 
         def ymax(k, hs, X=X, xk=xk, xn=xn):
             uk = ["yu%d_%d" % (k, h) for h in hs]
@@ -285,21 +300,31 @@ def build(g, core, T, topo):
             o = T.yy[:, 16 * c0:16 * c1]
             dve(cp(o, w) if k == 0 else tt(o, w, o, ALU.max), xk + [xn + "z"] + uk, yk, 16 * (c1 - c0), "g")
 
-        def settle(k0, k1, ol, oi, okeys, L=L, I=I, kb=kb):
+        def settle(k0, k1, t=t, kb=kb):
             p = "a" if k0 == 0 else "b"
             c0, c1 = 16 * k0, 16 * k1
             uk = ["yu%d_%d" % (k, h) for k in range(k0, k1) for h in (0, 1)]
+            tl, ti = T["tl%d" % t], T["ti%d" % t]
             dve(ts(T.dead[:, c0:c1], T.yu[:, k0:k1, :], 0.0, ALU.is_equal), uk, ["dead" + p], (c1 - c0) / 2)
-            dve(tt(T.tl[:, c0:c1], T.dl[:, c0:c1], T.dead[:, c0:c1], ALU.mult), ["dl", "dead" + p], ["tl" + p], 2 * (c1 - c0))
-            dve(tt(T.ti[:, c0:c1], T.di[:, c0:c1], T.dead[:, c0:c1], ALU.mult), ["di", "dead" + p], ["ti" + p], 2 * (c1 - c0))
-            dve(tt(ol, L[:, c0:c1], T.tl[:, c0:c1], ALU.add), kb + ["tl" + p], [okeys[0]], 2 * (c1 - c0))
-            dve(tt(oi, I[:, c0:c1], T.ti[:, c0:c1], ALU.subtract), kb + ["ti" + p], [okeys[1]], 2 * (c1 - c0))
+            n = 1 if k1 == 1 else 2
+            dl, dlk = (T.dl0, "dl0") if k1 == 1 else (T.dl, "dl")
+            dve(tt(tl[:, c0:c1], dl[:, c0:c1], T.dead[:, c0:c1], ALU.mult), [dlk, "dead" + p], ["tl%s_%d" % (p, t)], 2 * (c1 - c0))
+            if n == 2:
+                dve(tt(ti[:, c0:c1], T.di[:, c0:c1], T.dead[:, c0:c1], ALU.mult), ["di", "dead" + p], ["ti%s_%d" % (p, t)], 2 * (c1 - c0))
+            old = (T.lf, T.if0) if t == 0 else (T.l1, T.i1)
+            land = (T.l1, T.i1) if t == 0 else (T.l2, T.i2)
+            send(2 * t + (k0 > 0), T.cores[(rank + 1 - 2 * t) % n_ranks],
+                 [([a[:, c0:c1], b[:, c0:c1]], c[:, c0:c1]) for a, b, c in zip(old, (tl, ti), land)][:n],
+                 kb + ["tl%s_%d" % (p, t), "ti%s_%d" % (p, t)][:n], ["st%d%s" % (t + 1, p)])
 
         for k in range(6):
             part = min(k, 1)
             if t == 1 and k == 1:
                 prep(16, 96, (1,), kb)
                 masks(kb)
+            if k == 1:
+                act(lin(T.w2[:], L[:], 2048.0), kb, ["w1", "w2"], 96)
+                dve(tt(T.w2[:], T.w2[:], T.kt[:], ALU.add), ["kt"], ["w2"], 192)
             if t == 1 and k in (1, 3, 5):
                 xl(k, min(k + 2, 6))
             for h in (0, 1):
@@ -320,151 +345,155 @@ def build(g, core, T, topo):
                 mk = ["mk%d" % s for s in range(6)] if (k or not t) else []
                 dve(tt(B("pr")[:], T.mm[:, c0:c0 + n9], pz[:, BZ:BZ + n9], ALU.mult), mmk + mk + ["mw%d" % part, pzk], [K("pr")], n9)
                 dve(scan(ss[:, n9:2 * n9], T.d0[:, c0:c0 + n9], B("pr")[:], ALU.mult, ALU.add), ["d0%d" % part, K("pr")], [K("ss")], n9)
-                dve(tt(ss[:, 5:n9:NS], ss[:, n9 + 6::NS], ss[:, n9 + 8::NS], ALU.subtract), [K("ss")], [K("sr")], 16)
-                dve(ts(B("nb")[:], ss[:, 5::NS], 1.0 / 32, ALU.mult, 1024 - 31.0 / 64, ALU.add), [K("ss"), K("sr")], [K("nb")], 16)
-                dve(cp(B("cu")[:], T.fi[:].indirect(B("nb")[:, 0:8])), ["fi", "fie", K("nb")], [K("cu")], 128, "g")
+                dve(tt(ss[:, 6:n9:NS], ss[:, n9 + 7::NS], ss[:, n9 + 9::NS], ALU.subtract), [K("ss")], [K("sr")], 16)
+                dve(ts(B("nb")[:], ss[:, 6::NS], 1.0 / 32, ALU.mult, 1024 - 31.0 / 64, ALU.add), [K("ss"), K("sr")], [K("nb")], 16)
+                c1 = cfg["cu"]
+                dve(cp(B("cu")[:, 0:16 * c1], T.fi[:].indirect(B("nb")[:, 0:c1])), ["fi", "fie", K("nb")], [K("cu")] + [K("cw")] * (c1 == 8), 16 * c1, "g")
+                if c1 < 8:
+                    dve(cp(B("cu")[:, 16 * c1:128], T.fi[:].indirect(B("nb")[:, c1:8])), ["fi", "fie", K("nb")], [K("cw")], 128 - 16 * c1, "g")
                 x0 = 256 * k + 128 * h
                 dve(tt(B("q")[:], X[:, 0:XW].indirect(B("nb")[:, 8:16]), T.xl[:, x0:x0 + 128], ALU.max),
-                    xk + [xn + "s", xn + "z", K("nb"), "xl%d" % k], [K("q")], 128, "g")
-                dve(ts(B("fg")[:], B("cu")[:], -MID, ALU.add), [K("cu")], [K("fg")], 64)
-                pe(mat(pk[:, 0:8 * KS], T.onb[0:97, :], T.cr[0:97, :], True, False), ["onb", "cr0", "cr1", "cr2", "cr3"], [pkk], 160)
-                pe(mat(pk[:, 16:8 * KS:KS], T.onb[0:8, :], T.thm[0:8, 8 * k:8 * k + 8], False, False), ["onb", "thm%d" % k], [pkk], 64)
-                pe(mat(pk[:, 0:8 * KS], B("q")[:], T.gq[:], False, False), [K("q"), "gq"], [pkk], 160)
-                for j0, j1, a0 in cfg["relu"]:
-                    gr = "gr%d%d" % (j0, j1)
-                    pe(mat(pk[a0:128, 0:8 * KS], B("q")[:, a0:128], T[gr][:], False, False), [K("q"), gr], [pkk], 160)
+                    xk + [xn + "s", xn + "z", K("nb"), "xl%d_%d" % (k, h)], [K("q")], 128, "g")
+                dve(ts(B("fg")[:], B("cu")[:], -MID, ALU.add), [K("cu"), K("cw")], [K("fg")], 64)
+                pe(mat(pk[:, 0:8 * KS], T.onb[0:65, :], T.cr[0:65, :], True, False), ["onb"] + crk, [pkk], 160)
+                b2, b3 = cfg["b2"], cfg["b3"]
+                low = [0, 0, b2, b3]
 
-                def four(out, lhs, rhs, stop):
-                    for i in range(4):
-                        ins = P.matmul(out(i), lhs, rhs, i == 0, stop and i == 3)
-                    return ins
-                pe(lambda B=B, pq=pq: four(lambda i: pq[:, i::4], T.idb[:], B("q")[:], True), [K("q"), "idb"], [K("pq")], 512, 4)
+                def parts(a, split):
+                    cut = [a] + [c for c in (64, 96) if a < c and (a == 32 if c == 64 else split)] + [128]
+                    return list(zip(cut, cut[1:])) if a < 128 else []
+                sums = [K("kt"), K("kq")]
+                pe(mat(pk[:, 16:8 * KS:KS], T.onb[0:8, :], T.thm[0:8, 8 * k:8 * k + 8], False, False), ["onb", "th%d" % k, pkk], [K("kt")], 64)
+                pe(mat(pk[:, 0:8 * KS], B("q")[:], T.gq2[:], False, False), [K("q"), "gq20", "gq21", pkk], [K("kq")], 160)
+                for j in (2, 3):
+                    for a, b in parts(low[j], False) if low[j] else []:
+                        sums.append(K("kr%d%d" % (j, a)))
+                        pe(mat(pk[a:b, j:8 * KS:4], B("q")[:, a:b], T.gq4[:, j::4], False, False), [K("q"), "gq4", pkk], sums[-1:], max(40, min(64, b - a)))
+                pd = T["pd%d" % h]
+                if b2 == b3 <= 64:
+                    banks = [(pq, K("pq"), 0, (), 128), (pd, K("pd"), 0, (2, 3), b2)]
+                else:
+                    banks = [(pq, K("pq"), 0, (), 128), (pd, K("pd"), 0, (3,), b3), (pz, pzk, 128, (2,), b2)][:3 if b2 else 2]
+                for bank, key, p0, js, b in banks:
+                    def four(B=B, bank=bank, p0=p0, b=b, n=4 * max(1, len(js)), stop=not js):
+                        for i in range(n):
+                            p = p0 + 4 * b * (i // 4)
+                            ins = P.matmul(bank[:, p + i % 4:p + 4 * b:4], T.idb[:], B("q")[:, 0:b], i == 0, stop and i == n - 1)
+                        return ins
+                    pe(four, [K("q"), "idb"], [K("fq%d" % sum(js)), key], 4 * max(64, b) * max(1, len(js)), 4)
                 for i, (eng, a, b) in enumerate(cfg["cuts"]):
                     o, w = B("v")[:, 16 * a:16 * b], X[:, XO:XW].indirect(B("cu")[:, a:b])
+                    ck = [K("cu")] * (a < 16 * c1) + [K("cw")] * (b > 16 * c1)
                     if eng == "dve":
-                        dve(cp(o, w), xk + [K("cu")], [K("v%d" % i)], 16 * (b - a), "g")
+                        dve(cp(o, w), xk + ck, [K("v%d" % i)], 16 * (b - a), "g")
                     else:
-                        act(lambda o=o, w=w: S.activation(o, w, ACT.Copy), xk + [K("cu")], [K("v%d" % i)], 16 * (b - a), "g")
+                        act(lambda o=o, w=w: S.activation(o, w, ACT.Copy), xk + ck, [K("v%d" % i)], 16 * (b - a), "g")
 
                 def vkeys(c, d):
                     return [K("v%d" % i) for i, (eng, a, b) in enumerate(cfg["cuts"]) if a < d and b > c]
                 ak = [[] for j in range(4)]
-                last = [128] * 4
-                for x, (j0, j1, a0) in enumerate(cfg["relu"]):
-                    n, nj = 4 * (128 - a0), j1 - j0
-                    pd, pdk = T["pd%d" % (ring[0] % 2)], "pd%d" % (ring[0] % 2)
-                    ring[0] += 1
-
-                    def lessq(B=B, pd=pd, n=n, nj=nj, a0=a0):
-                        for i in range(4 * nj):
-                            ins = P.matmul(pd[:, n * (i // 4) + i % 4:n * (i // 4 + 1):4], T.nid[:], B("q")[:, a0:128], i == 0, False)
-                        return ins
-
-                    def plusv(B=B, pd=pd, n=n, nj=nj, a0=a0, j0=j0):
-                        for i in range(nj):
-                            ins = P.matmul(pd[:, n * i:n * i + n], T.idb[:], B("v")[:, 16 * a0 + j0 + i::4], False, i == nj - 1)
-                        return ins
-                    pe(lessq, [K("q"), "nid"], [K("dq%d" % x), pdk], 4 * nj * max(64, n // 4), 4 * nj)
-                    pe(plusv, vkeys(a0, 128) + ["idb"], [K("dv%d" % x), pdk], n * nj, nj)
-                    act(lambda B=B, pd=pd, n=n, a0=a0, j0=j0, j1=j1: S.activation(B("a")[:, j0:j1, 4 * a0:512], pd[:, 0:n * (j1 - j0)], ACT.Relu),
-                        [pdk], [K("ar%d" % x)], n * nj)
-                    for j in range(j0, j1):
-                        ak[j].append(K("ar%d" % x))
-                        last[j] = a0
                 for i, (a, b) in enumerate(cfg["runs"]):
                     for j in range(4):
-                        e = min(b, last[j])
-                        if e > a:
-                            dve(tt(B("a")[:, j, 4 * a:4 * e], pq[:, 4 * a:4 * e], B("v")[:, 16 * a + j:16 * e:4], ALU.max),
-                                [K("pq")] + vkeys(a, e), [K("a%d%d" % (j, i))], 4 * (e - a))
-                            ak[j].append(K("a%d%d" % (j, i)))
+                        e = max(a, low[j])
+                        if e < b:
+                            dve(tt(B("a")[:, j, 4 * e:4 * b], pq[:, 4 * e:4 * b], B("v")[:, 16 * e + j:16 * b:4], ALU.max),
+                                [K("pq")] + vkeys(e, b), [K("a%d%d" % (j, i))], 4 * (b - e))
+                            ak[j].append((K("a%d%d" % (j, i)), e, b))
+                for bank, key, p0, js, top in banks[1:]:
+                    runs = [(x, a, min(b, top)) for a, b in cfg["druns"] if a < top for x in range(len(js))]
+                    for x, a, b in runs:
+                        p = p0 + 4 * top * x
+                        pe(mat(bank[:, p + 4 * a:p + 4 * b], T.nid[:], B("v")[:, 16 * a + js[x]:16 * b:4], False, (x, a, b) == runs[-1]),
+                           vkeys(a, b) + ["nid"], [K("dv%d" % js[x]), key], max(64, 4 * (b - a)))
+                    act(lambda B=B, bank=bank, p0=p0, js=js, top=top: S.activation(
+                        B("a")[:, js[0]:js[-1] + 1, 0:4 * top], bank[:, p0:p0 + 4 * top * len(js)], ACT.Abs, scale=0.5),
+                        [key], [K("ab%d" % js[0])], 4 * top * len(js))
+                    for j in js:
+                        ak[j].append((K("ab%d" % js[0]), 0, top))
 
-                def lanes(pk, src, w):
+                def lanes(pk, a, b, src, w):
                     for m, lhs in src:
-                        ins = P.matmul(pk[:, m:8 * KS:KS], lhs, w, False, False)
+                        ins = P.matmul(pk[a:b, m:8 * KS:KS], lhs, w, False, False)
                     return ins
-                sums = []
                 for j in range(4):
-                    sums.append(K("kv%d" % j))
-                    pe(lambda B=B, pk=pk, j=j: lanes(pk, [(m, B("v")[:, m::16]) for m in range(j, 16, 4)], T.gv[:]),
-                       vkeys(0, 128) + ["gv", pkk], sums[-1:], 256, 4)
+                    for a, b in parts(low[j], cfg["skv"]):
+                        sums.append(K("kv%d%d" % (j, a)))
+                        pe(lambda B=B, pk=pk, j=j, a=a, b=b: lanes(pk, a, b, [(m, B("v")[:, 16 * a + m:16 * b:16]) for m in range(j, 16, 4)], T.gv[:]),
+                           vkeys(a, b) + ["gv", pkk], sums[-1:], 4 * min(64, b - a), 4)
                 for j in range(4):
-                    sums.append(K("ka%d" % j))
-                    pe(lambda B=B, pk=pk, j=j: lanes(pk, [(j + 4 * i, B("a")[:, j, i::4]) for i in range(4)], T.g8[:]),
-                       ak[j] + ["g8", pkk], sums[-1:], 256, 4)
-                pe(mat(pk[:, 0:8 * KS], B("fg")[:], T.idk[:], False, True), [K("fg"), "idk"] + sums, [pkk], 160)
+                    for a, b in parts(0, j in cfg["ska"]):
+                        sums.append(K("ka%d%d" % (j, a)))
+                        pe(lambda B=B, pk=pk, j=j, a=a, b=b: lanes(pk, a, b, [(j + 4 * i, B("a")[:, j, 4 * a + i:4 * b:4]) for i in range(4)], T.g8[:]),
+                           [key for key, c, d in ak[j] if c < b and d > a] + ["g8", pkk], sums[-1:], 4 * min(64, b - a), 4)
+                if cfg["fg4"]:
+                    for j in range(3):
+                        pe(mat(pk[:, j:8 * KS:4], B("fg")[:], T.idk[:, j::4], False, False),
+                           [K("fg"), "idk", pkk] + [x for x in sums if x[1] == "q" or x[2] == str(j)], [K("kf%d" % j)], 64)
+                    pe(mat(pk[:, 3:8 * KS:4], B("fg")[:], T.idk[:, 3::4], False, True),
+                       [K("fg"), "idk"] + sums + [K("kf%d" % j) for j in range(3)], [pkk], 64)
+                else:
+                    pe(mat(pk[:, 0:8 * KS], B("fg")[:], T.idk[:], False, True), [K("fg"), "idk"] + sums, [pkk], 160)
                 dve(scan(B("sc")[:], T.rs[:], pk[:, 0:8 * KS], ALU.add, ALU.min), ["rs0", "rs1", "rs2", pkk], [K("sc")], 8 * KS)
                 dve(tt(B("lo")[:], B("sc")[:, 16::KS], B("sc")[:, 18::KS], ALU.subtract), [K("sc")], [K("lo")], 16)
                 dve(tt(B("rx")[:], B("lo")[:].indirect(T.eo[:]), T.ma[:], ALU.mult), [K("lo"), "eo", "ma"], [K("rx")], 128, "g")
                 if k < 5:
-                    o = pz[:, BZ + k + 1:BZ + n9:NS]
-                    pe(mat(o, T.onb[0:1, :], T.up8[0:1, :], True, False), ["onb", "up8"], [K("zu"), pzk], 64)
-                    pe(mat(o, B("rx")[:], T.bm32[:], False, True), [K("rx"), "bm32"], [K("zb"), pzk], 64)
-                pe(mat(pz[:, BK + 8 * k:BK + 8 * k + 8], B("rx")[:], T.bm[:], True, True), [K("rx"), "bm"], [K("zk"), pzk], 64)
+                    pe(mat(pz[:, BZ + k + 1:BZ + n9:NS], B("rx")[:], T.bm32[:], True, True), [K("rx"), "bm32"], [K("zb"), pzk], 64)
+                pe(mat(pk[:, BK + 8 * k:BK + 8 * k + 8], B("rx")[:], T.bm[:], True, True), [K("rx"), "bm"], [K("zk"), pkk], 64)
                 if k in YROWS:
                     ylist(YROWS[k][0], k + 1, h)
                 if k == 4:
                     bz, z0 = pz[:, BZ:BZ + n9], n9 * h
-                    dve(ts(T.dx[:, z0:z0 + n9], bz, -32 * (DEAD + LIFT) - 500, ALU.add, -1.0e4, ALU.mult), [pzk], [K("dx")], n9)
-                    dve(ts(T.ds[:, z0:z0 + n9], bz, 32 * (DEAD + LIFT), ALU.is_equal), [pzk], [K("ds")], n9)
+                    dve(ts(T.dx[:, z0:z0 + n9], bz, -32 * DEAD - 500, ALU.add, -1.0e4, ALU.mult), [pzk], [K("dx")], n9)
+                    dve(ts(T.ds[:, z0:z0 + n9], bz, 32 * DEAD, ALU.is_equal), [pzk], [K("ds")], n9)
                     dve(scan(T.sb[:, z0:z0 + n9], T.dx[:, z0:z0 + n9], bz, ALU.min, ALU.max), [pzk, K("dx")], [K("sb")], n9)
                 if k < 5:
                     continue
                 ylist(5, 6, h)
                 ymax(5, [h])
 
-                def wsum(pz=pz, h=h):
-                    for a in range(16):
-                        ins = P.matmul(pz[:, SP:SP + 8], T.uw[:, 15 - a:143 - a], T.yy[:, 128 * h + a:128 * h + 128:16], a == 0, a == 15)
-                    return ins
-                pe(wsum, ["uw", "yy%d" % h], [K("zs"), pzk], 1024, 16)
-                dve(cp(B("s1")[:], pz[:, SP:SP + 8]), [pzk], [K("s1")], 8)
-                dve(ts(B("s2")[:], B("s1")[:], 15, ALU.bitwise_and), [K("s1")], [K("s2")], 8)
-                dve(tt(B("s3")[:], B("s2")[:], T.base[:], ALU.add), [K("s2"), "base"], [K("s3")], 16)
-                dve(cp(B("pu")[:], B("s3")[:]), [K("s3")], [K("pu")], 8)
+                pe(mat(pk[:, 0:48], T.onb[0:1, :], T.cw[0:1, :], True, False), ["onb", "cw0", "cw1", "cw2"], [K("s0"), pkk], 64)
+                pe(mat(pk[:, 3:48:6], T.p16[0:1, :], T.onb[0:1, 0:8], False, False), ["onb", "p16"], [K("s1"), pkk], 64)
+                pe(mat(pk[:, 0:48:3], T.yy[:, 128 * h:128 * h + 128], T.wg[:], False, True), ["yy%d" % h, "wg"], [K("s2"), pkk], 64)
+                dve(scan(B("sp")[:], T.d6[:], pk[:, 0:48], ALU.mult, ALU.add), ["d60", "d63", pkk], [K("sp")], 48)
+                dve(tt(B("rx")[:], B("sp")[:].indirect(T.e6[:]), T.ma[:], ALU.mult), [K("sp"), "e6", "ma"], [K("ry"), K("rx")], 128, "g")
+                pe(mat(pz[:, SP:SP + 8], B("rx")[:], T.bm[:], True, True), [K("rx"), "bm"], [K("zs"), pzk], 64)
+                dve(cp(B("pu")[:], pz[:, SP:SP + 8]), [pzk], [K("pu")], 8)
                 on = "xa" if (t == 1 and h == 0) else "xb"
                 w0 = XO + 2048 * h
                 dve(cp(T[on][:, w0:w0 + 2048].indirect(B("pu")[:]), T.yy[:, 128 * h:128 * h + 128]),
                     [K("pu"), "yy%d" % h], [K("put"), "%s%d" % (on, h)], 128, "s")
                 if t == 1:
-                    dma("sp", T.yx[:, 2048 * h:2048 * h + 2048], T[on][:, w0:w0 + 2048], ["%s%d" % (on, h)], ["yx%d" % h], 1600)
+                    dma("sp", T.yx[:, 2048 * h:2048 * h + 2048], T[on][:, w0:w0 + 2048], ["%s%d" % (on, h)], ["yx%d" % h], 2000)
             for j in YROWS.get(k, ()):
                 ymax(j, [0, 1])
             if k == 4:
-                dve(scan(T.sr[:], T.ds[:], T.ds[:], ALU.mult, ALU.add), ["ds_0", "ds_1"], ["run"], 144)
-                dve(tt(T.bp[:], T.sb[:].indirect(T.po[:, 0:6]), T.d0[:, 6::NS], ALU.mult), ["sb_0", "sb_1", "po", "d00", "d01"], ["bp"], 96, "g")
-                dve(ts(T.w2[:], L[:], 992.0, ALU.mult), kb, ["w1", "w2"], 96)
-                dve(tt(T.w2[:], T.w2[:], T.kt[:], ALU.add), ["kt"], ["w2"], 192)
+                dve(scan(T.sr[:], T.ds[:], T.ds[:], ALU.mult, ALU.subtract), ["ds_0", "ds_1"], ["run"], 160)
+                dve(tt(T.bp[:], T.sb[:].indirect(T.po[:, 0:6]), T.d0[:, 7::NS], ALU.mult), ["sb_0", "sb_1", "po", "d00", "d01"], ["bp"], 96, "g")
                 dve(tt(T.zr[:], T.bp[:], T.w2[:], ALU.add), ["bp", "w2"], ["zr"], 192)
                 dve(ts(T.nl[:], T.zr[:], 5, ALU.arith_shift_right, 4095, ALU.bitwise_and), ["zr"], ["nl"], 96)
                 dve(tt(T.dl[:], T.nl[:], L[:], ALU.subtract), kb + ["nl"], ["dl"], 192)
                 dve(tt(T.aa[:], T.ki[:], I[:], ALU.subtract), kb + ["ki"], ["aa"], 192)
-                dve(tt(T.di[:], T.sr[:].indirect(T.po[:, 0:6]), T.aa[:], ALU.subtract), ["run", "po", "aa"], ["di"], 96, "g")
-                sl, si = T["sl%d" % t], T["si%d" % t]
-                settle(0, 5, sl[:], si[:], ["sl_%d" % t, "si_%d" % t])
-                if t == 0:
-                    send(0, T.cores[(rank + 1) % n_ranks], [(sl[:], T.l1[:, 0:80]), (si[:], T.i1[:, 0:80])], ["sl_0", "si_0"], ["st1a"])
-                else:
-                    send(2, T.cores[(rank - 1) % n_ranks], [(sl[:], T.l2[:]), (si[:], T.i2[:])], ["sl_1", "si_1"], ["st2a"])
-        f5 = T["f5%d" % t]
-        settle(5, 6, f5[:, 0:16], f5[:, 16:32], ["f5l_%d" % t, "f5i_%d" % t])
+                dve(tt(T.di[:], T.sr[:].indirect(T.po[:, 0:6]), T.aa[:], ALU.add), ["run", "po", "aa"], ["di"], 96, "g")
+                if t == 1:
+                    settle(0, 5)
+            if t == 0 and 0 in YROWS.get(k, ()):
+                dve(tt(T.b0[:], T.d0[:, 7:16 * NS:NS], T.ex32[:], ALU.mult), ["d00", "ex32"], ["b0"], 32)
+                dve(tt(T.z0[:], T.b0[:], T.w2[:, 0:16], ALU.add), ["b0", "w2"], ["z0"], 32)
+                dve(ts(T.n0[:], T.z0[:], 5, ALU.arith_shift_right, 4095, ALU.bitwise_and), ["z0"], ["n0"], 16)
+                dve(tt(T.dl0[:], T.n0[:], L[:, 0:16], ALU.subtract), kb + ["n0"], ["dl0"], 32)
+                settle(0, 1)
+        settle(5 if t else 1, 6)
         if t == 0:
-            send(1, T.cores[(rank + 1) % n_ranks], [(f5[:, 0:16], T.l1[:, 80:96]), (f5[:, 16:32], T.i1[:, 80:96])],
-                 ["f5l_0", "f5i_0"], ["st1b"])
-            pd, pdk = T["pd%d" % (ring[0] % 2)], "pd%d" % (ring[0] % 2)
-            ring[0] += 1
+            pd, pdk = T.pd1, "pd_1"
             pe(mat(pd[:, 0:96], T.onb[:], T.dead[:], True, True), ["onb", "deada", "deadb"], ["cp", pdk], 96)
             dve(lambda pd=pd: V.tensor_reduce(T.cn[:, 0:1], pd[:, 0:96], AxisListType.X, ALU.add), [pdk], ["cn"], 96)
             dve(cp(T.ci[:, 0:1], T.cn[:, 0:1]), ["cn"], ["ci"], 1)
             dve(ts(T.cj[:, 0:1], T.ci[:, 0:1], 31, ALU.bitwise_and), ["ci"], ["cj"], 1)
-            dve(cp(T.cf[:, 0:1], T.cj[:, 0:1]), ["cj"], ["cf"], 1)
-            dve(ts(T.cr[64:65, 16::KS], T.onb[64:65, 0:8], T.cf[64:65, 0:1], ALU.mult, DW, ALU.mult), ["cf", "onb"], ["cr2"], 8)
+            dve(ts(T.cf[:, 0:1], T.cj[:, 0:1], -120.0, ALU.add), ["cj"], ["cf"], 1)
+            dve(ts(T.cr[64:65, 16::KS], T.onb[64:65, 0:8], T.cf[64:65, 0:1], ALU.mult, DW, ALU.mult), ["cf", "onb"], ["ca"], 8)
         else:
-            send(3, T.cores[(rank - 1) % n_ranks], [(f5[:], T.r5[:])], ["f5l_1", "f5i_1"], ["st2b"])
-            dma("act", T.yl[:, 0:80], T.l2[:], ["st2a", "sc_0", "sc_1"], ["yla"], 150)
-            dma("act", T.yi[:, 0:80], T.i2[:], ["st2a", "sc_0", "sc_1"], ["yia"], 150)
-            dma("act", T.yl[:, 80:96], T.r5[:, 0:16], ["st2b"], ["ylb"], 100)
-            dma("act", T.yi[:, 80:96], T.r5[:, 16:32], ["st2b"], ["yib"], 100)
+            dma("act", T.yl[:], T.l2[:], ["st2a", "st2b"], ["yl"], 150)
+            dma("act", T.yi[:], T.i2[:], ["st2a", "st2b"], ["yi"], 150)
     return ops
 
 
@@ -489,20 +518,42 @@ def depend(ops):
     return deps
 
 
-def prices(ops, m):
-    cy, ga, sa, fix, hop, pc, po = m
+def prices(ops, deps, m):
+    cy, ga, sa, fixv, fixs, least, own, other, tensor, pc, second, slow = m
     out = []
     for o in ops:
         f, n = o["form"], o["n"]
         if f == "e":
-            out.append(fix + max(64.0, n) * cy)
+            out.append((fixv if o["eng"] == "dve" else fixs) + max(least, n) * cy)
         elif f == "g" or f == "s":
-            out.append((50.0 if o["eng"] == "dve" else 65.0) + n * cy * (ga if f == "g" else sa))
+            two = second if o["w"][0][:2] in ("yy", "q_", "rx", "ry", "bp", "di") else 0.0
+            out.append((50.0 if o["eng"] == "dve" else 65.0) + n * cy * (ga + two if f == "g" else sa))
         elif f == "pe":
-            out.append(n * pc + o["m"] * po)
+            out.append(n * pc)
         else:
             out.append(n)
-    return out
+    waits = []
+    for o, d in zip(ops, deps):
+        e = o["eng"]
+        waits.append([(j, (0.0 if e == "pe" else own) if ops[j]["eng"] == e else tensor if ops[j]["eng"] == "pe" else other) for j in d])
+    return out, waits, slow
+
+
+def replay(ops, order, cost, waits, slow):
+    end, free, wire = [0.0] * len(ops), {}, 0.0
+    for i in order:
+        o = ops[i]
+        t = free.get(o["eng"], 0.0) if o["eng"] else 0.0
+        for j, w in waits[i]:
+            if end[j] + w > t:
+                t = end[j] + w
+        t += cost[i]
+        free[o["eng"]] = t
+        t += o["lat"]
+        if o["kind"] == "dma" and o["m"]:
+            wire = t = max(t, wire) + o["m"] * slow
+        end[i] = t
+    return end
 
 
 def above(xs, x):
@@ -538,8 +589,7 @@ def arrange(ops, deps):
     for i, d in enumerate(deps):
         for j in d:
             succ[j].append(i)
-    waited = [[j for j in d if not (eng[i] == "pe" and eng[j] == "pe")] for i, d in enumerate(deps)]
-    costs = [prices(ops, m) for m in COSTS]
+    costs = [prices(ops, deps, m) for m in COSTS]
     bus = [o["m"] if o["kind"] == "dma" else 0 for o in ops]
     seed = [CFG["seed"]]
 
@@ -547,23 +597,8 @@ def arrange(ops, deps):
         seed[0] = (seed[0] * 1103515245 + 12345) % 2147483648
         return (seed[0] >> 8) / 8388608.0
 
-    def replay(order, cost, hop):
-        end, free, wire = [0.0] * n, {}, 0.0
-        for i in order:
-            t = free.get(eng[i], 0.0) - hop if eng[i] else -hop
-            for j in waited[i]:
-                if end[j] > t:
-                    t = end[j]
-            t += hop + cost[i]
-            free[eng[i]] = t
-            t += ops[i]["lat"]
-            if bus[i]:
-                wire = t = max(t, wire) + bus[i]
-            end[i] = t
-        return end
-
     def length(order):
-        return sum(max(replay(order, c, m[4])) for c, m in zip(costs, COSTS)) / len(COSTS)
+        return sum(max(replay(ops, order, *c)) / m[0] for c, m in zip(costs, COSTS)) / len(COSTS)
 
     def pack(rank, cost, hop, back):
         pre, post = (succ, deps) if back else (deps, succ)
@@ -571,7 +606,9 @@ def arrange(ops, deps):
         for i in by_rank(pre, post, rank):
             e, r, c = eng[i], 0.0, cost[i]
             for j in pre[i]:
-                x = start[j] + cost[j] + (lat[i] if back else lat[j]) + (0.0 if e == "pe" and eng[j] == "pe" else hop)
+                a = e if back else eng[j]
+                x = start[j] + cost[j] + (lat[i] if back else lat[j]) + \
+                    ((0.0 if e == "pe" else hop[0]) if e == eng[j] else hop[2] if a == "pe" else hop[1])
                 if x > r:
                     r = x
             if e:
@@ -588,16 +625,19 @@ def arrange(ops, deps):
     lat = [o["lat"] + b for o, b in zip(ops, bus)]
     wire = 0.0
     for i in loads:
-        wire += bus[i]
+        wire += 0.65 * bus[i]
         lat[i] = ops[i]["lat"] + (wire if bus[i] else 0.0)
     now = best = list(range(n))
     tnow = tbest = length(best)
     for it in range(CFG["rounds"]):
         w = [rnd() + 0.01 for _ in COSTS]
         w = [x / sum(w) for x in w]
-        f = {e: 0.86 + 0.28 * rnd() for e in QUEUES}
-        cost = [sum(x * c[i] for x, c in zip(w, costs)) * f[eng[i]] * (0.86 + 0.28 * rnd()) for i in range(n)]
-        hop = sum(x * m[4] for x, m in zip(w, COSTS))
+        amp = CFG["amp"][0] + (CFG["amp"][1] - CFG["amp"][0]) * it / CFG["rounds"]
+        f = {e: 1 + amp * (2 * rnd() - 1) for e in QUEUES}
+        cost = [sum(x * c[0][i] for x, c in zip(w, costs)) * f[eng[i]] * (1 + amp * (2 * rnd() - 1)) for i in range(n)]
+        if it % CFG["back"] == 0:
+            now, tnow = best, tbest
+        hop = [sum(x * m[j] for x, m in zip(w, COSTS)) for j in (6, 7, 8)]
         at = [0] * n
         for k, i in enumerate(now):
             at[i] = k
@@ -610,10 +650,39 @@ def arrange(ops, deps):
             fore = pack(rank, cost, hop, False)
             order = by_rank(deps, succ, fore)
             x = length(order)
-            if x < tnow + 300:
+            if x < tnow + CFG["slack"]:
                 now, tnow = order, x
             if x < tbest:
                 best, tbest = order, x
+
+    def starts(order):
+        end = replay(ops, order, *costs[0])
+        out = [end[i] - costs[0][0][i] - ops[i]["lat"] - bus[i] for i in range(n)]
+        for k, i in enumerate(loads):
+            out[i] = k - 1.0e12
+        return out
+
+    def pick(xs):
+        return xs[int(rnd() * len(xs))]
+    kinds = {}
+    for i, o in enumerate(ops):
+        kinds.setdefault(o["w"][0].rsplit("_", 1)[0], []).append(i)
+    names = sorted(k for k in kinds if len(kinds[k]) >= 12)
+    at = starts(best)
+    for it in range(CFG["moves"]):
+        rank = list(at)
+        if rnd() < 0.5:
+            d, lo, span = pick((-600, -300, -150, -60, 60, 150, 300, 600)), int(24 * rnd()), pick((1, 2, 4, 99))
+            for i in kinds[pick(names)]:
+                if span == 99 or lo <= ops[i]["ph"] < lo + span:
+                    rank[i] += d
+        else:
+            for _ in range(pick((1, 2))):
+                rank[int(n * rnd())] += pick((-3000, -1000, -300, -100, 100, 300, 1000, 3000))
+        order = by_rank(deps, succ, rank)
+        x = length(order)
+        if x <= tbest:
+            best, tbest, at = order, x, starts(order)
     return best, tbest
 
 

from concourse.bass import DstId, RemoteDMATransfer
from concourse.mybir import AluOpType as ALU, AxisListType, ActivationFunctionType as ACT

CFG = {"cuts": [("act", 0, 64), ("act", 64, 96), ("act", 96, 120), ("dve", 120, 128)], "runs": [(0, 64), (64, 96), (96, 128)],
       "druns": [(0, 64), (64, 128)], "b2": 64, "b3": 64, "skv": True, "ska": (3,), "fg4": True, "cu": 4, "at": {}, "seed": 1, "rounds": 300,
       "amp": (0.1, 0.06), "back": 100000, "slack": 200, "moves": 8500}
for _t in (0, 1):
    CFG["at"][_t, 0, 0] = {"cuts": [("act", 0, 64), ("act", 64, 80), ("dve", 80, 128)], "cu": 8}
    for _k, _h in ((4, 1), (5, 0), (5, 1)):
        CFG["at"][_t, _k, _h] = {"b2": 96, "b3": 96, "cuts": [("act", 0, 64), ("act", 64, 96), ("act", 96, 128)]}
XO = 32
XW = XO + 4096
FW = 2048 + 8
KSUB = 65536 * 166
DW = 131072.0
MID = 2048.0
DEAD = -2080.0
LIFT = 1056.0
KS, NS = 20, 10
RKEY = 1.5 * 2.0 ** 36
RIDX = 1.5 * 2.0 ** 39
YROWS = {1: (0, 1), 3: (2, 3), 4: (4,)}
RSUM = 1.5 * 2.0 ** 27
BZ, BK, SP = 0, 160, 80

SCRATCH = {
    "xa": ("sbuf", [128, XW], "bfloat16"), "xb": ("sbuf", [128, XW], "bfloat16"),
    "fi": ("sbuf", [128, FW], "int32"),
    "l0": ("sbuf", [128, 96], "int32"), "i0": ("sbuf", [128, 96], "int32"),
    "l1": ("sbuf", [128, 96], "float32"), "i1": ("sbuf", [128, 96], "float32"),
    "l2": ("sbuf", [128, 96], "float32"), "i2": ("sbuf", [128, 96], "float32"),
    "lf": ("sbuf", [128, 96], "float32"), "if0": ("sbuf", [128, 96], "float32"),
    "exi": ("sbuf", [128, 16], "int32"), "th8": ("sbuf", [128, 8], "int32"), "thf": ("sbuf", [128, 8], "float32"),
    "wti": ("sbuf", [128, 4], "int32"), "wtf": ("sbuf", [128, 4], "float32"),
    "mm": ("sbuf", [128, 96 * NS], "float32"), "d0": ("sbuf", [128, 96 * NS], "float32"),
    "yu": ("sbuf", [128, 6, 16], "uint16"), "lu": ("sbuf", [128, 96], "uint16"),
    "xl": ("sbuf", [128, 1536], "bfloat16"), "yy": ("sbuf", [128, 256], "bfloat16"),
    "onb": ("sbuf", [128, 128], "bfloat16"), "idb": ("sbuf", [128, 128], "bfloat16"), "nid": ("sbuf", [128, 128], "bfloat16"),
    "idk": ("sbuf", [128, 8 * KS], "float16"), "iv": ("sbuf", [128, 8 * KS], "float32"), "cr": ("sbuf", [128, 8 * KS], "bfloat16"),
    "thm": ("sbuf", [128, 48], "bfloat16"), "gq4": ("sbuf", [128, 8 * KS], "bfloat16"), "gq2": ("sbuf", [128, 8 * KS], "bfloat16"),
    "i2x": ("sbuf", [128, 16], "float32"), "wg": ("sbuf", [128, 16], "bfloat16"), "cw": ("sbuf", [128, 48], "bfloat16"),
    "d6": ("sbuf", [128, 48], "float32"), "p16": ("sbuf", [128, 128], "bfloat16"), "e6": ("sbuf", [128, 8], "uint16"),
    "ig": ("sbuf", [128, 8 * KS], "float32"), "im": ("sbuf", [128, 8 * KS], "float32"),
    "g8": ("sbuf", [128, 8], "bfloat16"), "gv": ("sbuf", [128, 8], "bfloat16"),
    "bm": ("sbuf", [128, 8], "float16"), "bm32": ("sbuf", [128, 8], "float16"),
    "pi": ("sbuf", [128, 4], "int32"), "pa": ("sbuf", [128, 4], "int32"), "pb": ("sbuf", [128, 4], "int32"),
    "pf": ("sbuf", [128, 12], "float32"), "ia": ("sbuf", [128, 128], "float32"), "ma": ("sbuf", [128, 128], "float32"),
    "rs": ("sbuf", [128, 8 * KS], "float32"),
    "ic": ("sbuf", [128, 8], "float32"), "eo": ("sbuf", [128, 8], "uint16"), "po": ("sbuf", [128, 8], "uint16"),
    "kt": ("sbuf", [128, 96], "float32"), "ki": ("sbuf", [128, 96], "float32"),
    "dx": ("sbuf", [128, 16 * NS], "float32"), "ds": ("sbuf", [128, 16 * NS], "float32"), "sb": ("sbuf", [128, 16 * NS], "float32"),
    "sr": ("sbuf", [128, 16 * NS], "float32"), "bp": ("sbuf", [128, 96], "float32"), "w2": ("sbuf", [128, 96], "float32"),
    "zr": ("sbuf", [128, 96], "int32"), "nl": ("sbuf", [128, 96], "int32"), "dl": ("sbuf", [128, 96], "float32"),
    "aa": ("sbuf", [128, 96], "float32"), "di": ("sbuf", [128, 96], "float32"), "dead": ("sbuf", [128, 96], "bfloat16"),
    "ex32": ("sbuf", [128, 16], "float32"), "b0": ("sbuf", [128, 16], "float32"), "z0": ("sbuf", [128, 16], "int32"),
    "n0": ("sbuf", [128, 16], "int32"), "dl0": ("sbuf", [128, 16], "float32"),
    "tl0": ("sbuf", [128, 96], "float32"), "ti0": ("sbuf", [128, 96], "float32"),
    "tl1": ("sbuf", [128, 96], "float32"), "ti1": ("sbuf", [128, 96], "float32"),
    "cn": ("sbuf", [128, 4], "float32"), "ci": ("sbuf", [128, 4], "int32"), "cj": ("sbuf", [128, 4], "int32"),
    "cf": ("sbuf", [128, 4], "float32"),
}
for _h in (0, 1):
    for _n in ("pk", "pz", "pq", "pd"):
        SCRATCH["%s%d" % (_n, _h)] = ("psum", [128, 512], "float32")
    for _n, _w, _t in (("pr", 8 * NS, "float32"), ("ss", 16 * NS, "float32"), ("nb", 16, "uint16"), ("cu", 128, "uint16"),
                       ("fg", 128, "float16"), ("q", 128, "bfloat16"),
                       ("rx", 128, "float16"), ("sp", 48, "float32"), ("pu", 8, "uint16")):
        SCRATCH["%s_%d" % (_n, _h)] = ("sbuf", [128, _w], _t)
    SCRATCH["a_%d" % _h] = ("sbuf", [128, 4, 512], "bfloat16")
    SCRATCH["sc_%d" % _h] = ("sbuf", [128, 8 * KS], "float32")
    SCRATCH["lo_%d" % _h] = ("sbuf", [128, 8], "float32")
    SCRATCH["v_%d" % _h] = ("sbuf", [128, 2048], "bfloat16")

NDMA = 24
SEMAPHORES = ["pe", "dve", "act", "pool"] + ["m%d" % _i for _i in range(NDMA)] + \
             ["arr%d" % _i for _i in range(4)] + ["out%d" % _i for _i in range(4)]

QUEUES = ("pe", "dve", "act", "pool", "sp", None)
COSTS = [(0.88, 1.56, 3.8, 10.0, 30.0, 64, 110.0, 200.0, 250.0, 0.66, 0.0, 0.9), (0.85, 1.5, 3.8, 20.0, 60.0, 64, 150.0, 150.0, 200.0, 0.7, 0.0, 0.65),
         (0.91, 1.61, 3.8, 18.0, 10.0, 64, 61.0, 81.0, 300.0, 0.67, 0.0, 1.2), (0.88, 1.44, 3.8, 7.0, 138.0, 64, 89.0, 150.0, 128.0, 0.76, 0.5, 0.65),
         (1.2, 1.9, 4.5, 20.0, 60.0, 64, 120.0, 150.0, 200.0, 0.95, 0.3, 0.9)]


def build(g, core, T, topo):
    rank = T.rank_of(core)
    n_ranks = len(T.cores)
    ops = []
    ndma = [0]
    phase = [-1]

    def op(eng, fn, r, w, form, n, m=0, kind="c", sem=None, val=0, lat=0.0):
        ops.append({"eng": eng, "fn": fn, "r": r, "w": w, "form": form, "n": n, "m": m, "kind": kind, "sem": sem,
                    "val": val, "lat": lat, "ph": phase[0], "first": not r})

    V, S, P = g.vector, g.scalar, g.tensor

    def dve(fn, r, w, n, form="e"):
        op("dve", fn, r, w, form, n)

    def act(fn, r, w, n, form="e"):
        op("act", fn, r, w, form, n)

    def pool(fn, r, w, n):
        op("pool", fn, r, w, "ns", 150 + 2.1 * n)

    def pe(fn, r, w, cyc, calls=1):
        op("pe", fn, r, w, "pe", cyc, calls)

    def dma(eng, out, in_, r, w, bus, slow=False):
        name = "m%d" % ndma[0]
        ndma[0] += 1
        q = {"sp": g.sync, "act": g.scalar, "pool": g}[eng]
        if slow:
            fn = lambda: q.dma_start(out, in_, allow_slow_non_contiguous=True)
        else:
            fn = lambda: q.dma_start(out, in_)
        op(eng, fn, r, w, "ns", 60.0, bus, "dma", name, 16, 1500.0)

    def ts(out, in0, s1, o1, s2=None, o2=None):
        if o2 is None:
            return lambda: V.tensor_scalar(out, in0, s1, None, o1)
        return lambda: V.tensor_scalar(out, in0, s1, s2, o1, o2)

    def tt(out, a, b, o):
        return lambda: V.tensor_tensor(out, a, b, o)

    def cp(out, a):
        return lambda: V.tensor_copy(out, a)

    def ms(out, c):
        return lambda: V.memset(out, c)

    def scan(out, a, b, o0, o1):
        return lambda: V.tensor_tensor_scan(out, a, b, 0.0, o0, o1)

    def lin(out, in_, scale, bias=None):
        if bias is None:
            return lambda: S.activation(out, in_, ACT.Copy, scale=scale)
        return lambda: S.activation(out, in_, ACT.Identity, bias=bias, scale=scale)

    def mat(out, lhs, rhs, start, stop):
        return lambda: P.matmul(out, lhs, rhs, start, stop)

    def iota(out, pattern, base, cm=0):
        return lambda: g.iota(out, pattern, base, cm, allow_small_or_imprecise_dtypes=True)

    def send(idx, dst, pairs, r, w):
        eng = topo.engines(core, dst)[:8]
        rid, pid = topo.addr(dst)[:2]
        share = len(eng) // len(pairs)

        def fn():
            trs = []
            for i, (src, land) in enumerate(pairs):
                m = sum(1 << e for e in eng[i * share:(i + 1) * share])
                trs.append(RemoteDMATransfer(dst_ids=[DstId(rid=rid, pnc=pid)], dma_engine_mask=m,
                                             remote_sem=T.sem["arr%d" % idx], srcs=src, dsts=[land], alu_op=1))
            return g.remote_dma_fused(trs, local_sem=T.sem["out%d" % idx])
        op("pool", fn, r, ["sent%d" % idx], "ns", 300.0, 0, "send", "out%d" % idx, share * len(pairs), 2500.0)
        op(None, None, ["sent%d" % idx], w, "ns", 0.0, 0, "recv", "arr%d" % idx, share * len(pairs), 500.0)

    phase[0] = -9
    dma("sp", T.l0[:], T.lc[:], [], ["l0"], 150)
    dma("act", T.i0[:], T.up[:], [], ["i0"], 150)
    dma("act", T.exi[:], T.ex[:], [], ["exi"], 100)
    dma("sp", T.xa[:, XO:XW], T.xs[:], [], ["xa0", "xa1"], 3200)
    dma("sp", T.fi[:, 0:2048], T.fa[:], [], ["fi"], 3200)
    dma("act", T.th8[0:8, 0:6], T.th[:], [], ["th8"], 0)
    dma("act", T.fi[:, 2048:FW], T.fa[:, 0:8], [], ["fie"], 0)

    mmk, d0k = ["mm6", "mm8", "mm9"], ["d0z"]
    pool(lambda: g.iota(T.pi[:, 0:1], [[1, 1]], 0, 1), [], ["pi"], 1)
    pool(iota(T.ic[:], [[1, 8]], 0), [], ["ic"], 8)
    dve(ms(T.onb[:], 1.0), [], ["onb"], 64)
    pool(iota(T.ig[:], [[1, 8], [0, KS]], 0), [], ["ig"], 160)
    dve(ms(T.d0[:], 1.0), [], ["d0z"], 960)
    pool(lambda: g.affine_select(T.idb[:], T.onb[:], [[-1, 128]], ALU.is_equal, 0.0, 0, 1), ["onb"], ["idb"], 128)
    pool(iota(T.im[:], [[0, 8], [1, KS]], 0), [], ["im"], 160)
    pool(iota(T.iv[:], [[32, 8], [1, KS]], 0), [], ["iv"], 160)
    pool(iota(T.ia[:], [[0, 8], [1, 16]], 0), [], ["ia"], 128)
    pool(iota(T.i2x[:], [[1, 8], [0, 2]], 0), [], ["i2x"], 16)
    pool(iota(T.p16[0:1, :], [[16, 128]], 0), [], ["p16"], 128)
    pool(iota(T.kt[:], [[32, 6], [0, 16]], 2048 * 1184 - KSUB), [], ["kt"], 96)
    pool(iota(T.ki[:], [[1, 6], [0, 16]], -1), [], ["ki"], 96)
    dma("pool", T.wti[:, 0:1], T.wt[:], ["idb", "im", "iv", "ia", "i2x", "p16", "kt", "ki"], ["wti"], 0, slow=True)
    dve(ms(T.mm[:, 6::NS], 32 * LIFT), [], ["mm6"], 96)
    dve(ms(T.mm[:, 8::NS], RIDX), [], ["mm8"], 96)
    dve(ms(T.mm[:, 9::NS], -RIDX), [], ["mm9"], 96)
    for h in (0, 1):
        dve(ms(T["pz%d" % h][:, BZ:BZ + 8 * NS], 1.0), [], ["pz%d" % h], 80)
    dve(ms(T.cw[0:1, :], 0.0), [], ["cw0", "cw1", "cw2"], 24)
    dve(ms(T.d6[:], 1.0), [], ["d60", "d63"], 48)
    for i, c in enumerate((-7.5, RSUM, -RSUM)):
        dve(ms(T.cw[0:1, i::6], c), [], ["cw%d" % i], 8)
    dve(ms(T.d6[:, 0::6], 0.0), [], ["d60"], 8)
    dve(ms(T.d6[:, 3::6], -1.0), [], ["d63"], 8)
    for name in ("xa", "xb"):
        dve(ms(T[name][:, 0:16], 64.0), [], [name + "s"], 8)
        dve(ms(T[name][:, 16:XO], 0.0), [], [name + "z"], 8)
    dve(ms(T.rs[:], 0.0), [], ["rs0", "rs1", "rs2"], 160)
    crk = ["cm", "cb", "ca"]
    dve(ms(T.cr[:], 0.0), [], crk, 80)
    dve(ts(T.pa[:, 0:1], T.pi[:, 0:1], 15, ALU.bitwise_and), ["pi"], ["pa"], 1)
    dve(ts(T.pb[:, 0:1], T.pi[:, 0:1], 4, ALU.arith_shift_right), ["pi"], ["pb"], 1)
    dve(ms(T.rs[:, 0::KS], 1.0e9), [], ["rs0"], 8)
    dve(ms(T.rs[:, 17::KS], RKEY), [], ["rs1"], 8)
    dve(ms(T.rs[:, 18::KS], -RKEY), [], ["rs2"], 8)
    dve(ms(T.cr[64:65, :], -120 * DW), [], ["ca"], 80)
    dve(cp(T.pf[:, 0:1], T.pa[:, 0:1]), ["pa"], ["pf0"], 1)
    dve(cp(T.pf[:, 1:2], T.pb[:, 0:1]), ["pb"], ["pf1"], 1)
    act(lin(T.pf[:, 2:3], T.pf[:, 1:2], 32.0, T.pf[:, 0:1]), ["pf0", "pf1"], ["pf2"], 1)
    act(lin(T.pf[:, 5:6], T.pf[:, 0:1], float(NS)), ["pf0"], ["pf5"], 1)
    phase[0] = -7
    for h in (0, 1):
        dve(ts(T["pz%d" % h][:, BZ:BZ + 8 * NS:NS], T.exi[:, 8 * h:8 * h + 8], 32.0, ALU.mult, -32 * MID, ALU.add),
            ["exi"], ["pz%d" % h], 8)
    dve(ts(T.ex32[:], T.exi[:], 32.0, ALU.mult, -32 * MID, ALU.add), ["exi"], ["ex32"], 16)
    dve(ms(T.i1[:, 0:16], -1.0), [], ["i1z"], 16)
    dve(ts(T.thf[0:8, 0:6], T.th8[0:8, 0:6], DW, ALU.mult), ["th8"], ["thf"], 6)
    phase[0] = -6
    dve(ms(T.d0[:, 0::NS], 0.0), [], ["d0z"], 96)
    act(lin(T.nid[:], T.idb[:], -1.0), ["idb"], ["nid"], 128)
    for k in range(6):
        act(lin(T.thm[0:8, 8 * k:8 * k + 8], T.idb[0:8, 0:8], T.thf[0:8, k:k + 1]), ["idb", "thf"], ["th%d" % k], 8)
    dve(ts(T.cr[0:1, :], T.im[0:1, :], 8192.0, ALU.mult), ["im"], ["cm"], 160)
    dve(ts(T.cr[32:33, :], T.im[32:33, :], 16.0, ALU.is_gt, 2.0 ** 40, ALU.mult), ["im"], ["cb"], 160)
    dve(ms(T.cr[0:1, 16::KS], DEAD), [], ["cm"], 8)
    phase[0] = -8.5
    dve(ts(T.g8[:], T.ic[:], T.pf[:, 1:2], ALU.is_equal, 2 * DW, ALU.mult), ["ic", "pf1"], ["g8"], 8)
    act(lin(T.gv[:], T.g8[:], -0.5), ["g8"], ["gv"], 8)
    dve(ts(T.bm[:], T.ic[:], T.pf[:, 1:2], ALU.is_equal), ["ic", "pf1"], ["bm"], 8)
    dve(ts(T.bm32[:], T.ic[:], T.pf[:, 1:2], ALU.is_equal, 32.0, ALU.mult), ["ic", "pf1"], ["bm32"], 8)
    dve(ts(T.ma[:], T.ia[:], T.pf[:, 0:1], ALU.is_equal), ["ia", "pf0"], ["ma"], 128)
    dve(cp(T.eo[:], T.ic[:]), ["ic"], ["eo"], 8)
    dve(ts(T.po[:], T.ic[:], T.pf[:, 5:6], ALU.add), ["ic", "pf5"], ["po"], 8)
    dve(ts(T.e6[:], T.ic[:], 6.0, ALU.mult, 3.0, ALU.add), ["ic"], ["e6"], 8)
    dve(ts(T.gq4[:], T.ig[:], T.pf[:, 1:2], ALU.is_equal, -DW, ALU.mult), ["ig", "pf1"], ["gq4"], 160)
    dve(ms(T.gq4[:, 16::KS], 0.0), [], ["gq4"], 8)
    dve(ms(T.gq2[:], 0.0), [], ["gq20", "gq21"], 80)
    for j in (0, 1):
        dve(cp(T.gq2[:, j::4], T.gq4[:, j::4]), ["gq4"], ["gq2%d" % j], 20)
    phase[0] = -5
    dve(ts(T.idk[:], T.iv[:], T.pf[:, 2:3], ALU.is_equal), ["iv", "pf2"], ["idk"], 160)
    phase[0] = -2
    dve(cp(T.wtf[:, 0:1], T.wti[:, 0:1]), ["wti"], ["wtf"], 1)
    dve(ts(T.wg[:], T.i2x[:], T.pf[:, 1:2], ALU.is_equal, T.wtf[:, 0:1], ALU.mult), ["i2x", "pf1", "wtf"], ["wg"], 16)
    dma("sp", T.xb[:, XO:XW], T.xs[:], ["fi"], ["xb0", "xb1"], 3200)

    ring = [0]
    for t in (0, 1):
        X = T.xa if t == 0 else T.xb
        xn = "xa" if t == 0 else "xb"
        xk = [xn + "0", xn + "1"]
        L, I = (T.lf, T.if0) if t == 0 else (T.l1, T.i1)
        ka, kb = (["lf"], ["lf", "if0"]) if t == 0 else (["st1a"], ["st1a", "st1b", "i1z"])
        wadd = float(992 * 1184 + 32 * 77 * t - 32768 - KSUB)

        def prep(c0, c1, part, keys, t=t, L=L):
            a, b = T.d0[:, NS * c0 + 7:NS * c1:NS], T.mm[:, NS * c0 + 7:NS * c1:NS]
            dve(cp(T.lu[:, c0:c1], L[:, c0:c1]), keys, ["lu%d" % p for p in part], c1 - c0)
            act(lin(a, L[:, c0:c1], 1.0 / 32, 37.0), keys + d0k, ["d0%d" % p for p in part], c1 - c0)
            act(lin(b, L[:, c0:c1], 1024.0, wadd), keys, ["mw%d" % p for p in part], c1 - c0)

        def masks(keys, t=t, I=I):
            for s in range(6):
                k0 = max(s, 1) if t else 0
                dve(ts(T.mm[:, 16 * NS * k0 + s::NS], I[:, 16 * k0:96], float(s - 1), ALU.is_equal), keys, ["mk%d" % s], 96 - 16 * k0)

        def xl(k0, k1, X=X, xk=xk):
            act(lambda: S.activation(T.xl[:, 256 * k0:256 * k1], X[:, XO:XW].indirect(T.lu[:, 16 * k0:16 * k1]), ACT.Copy),
                xk + ["lu%d" % min(k0, 1)], ["xl%d_%d" % (k, h) for k in range(k0, k1) for h in (0, 1)], 256 * (k1 - k0), "g")

        if t == 0:
            phase[0] = -8
            dve(cp(T.lf[:], T.l0[:]), ["l0"], ["lf"], 96)
            dve(cp(T.if0[:], T.i0[:]), ["i0"], ["if0"], 96)
            prep(0, 96, (0, 1), ka)
            masks(kb)
            phase[0] = -4
            xl(0, 1)
            xl(1, 6)
            phase[0] = 0
        else:
            phase[0] = 12
            prep(0, 16, (0,), ka)
            for h in (0, 1):
                act(lambda h=h, X=X: S.activation(T.xl[:, 128 * h:128 * h + 128], X[:, XO:XW].indirect(T.lu[:, 8 * h:8 * h + 8]), ACT.Copy),
                    xk + ["lu0"], ["xl0_%d" % h], 128, "g")
            dma("sp", T.xa[:, XO:XO + 2048], T.xb[:, XO:XO + 2048], ["xb0", "sent1"], ["xa0"], 1600)

        def ylist(k0, k1, h):
            dve(ts(T.yu[:, k0:k1, 8 * h:8 * h + 8], T["pk%d" % h][:, BK + 8 * k0:BK + 8 * k1], MID + 16, ALU.add, 0.0, ALU.max),
                ["pk%d" % h], ["yu%d_%d" % (k, h) for k in range(k0, k1)], 8 * (k1 - k0))

        def ymax(k, hs, X=X, xk=xk, xn=xn):
            uk = ["yu%d_%d" % (k, h) for h in hs]
            yk = ["yy%d" % h for h in hs]
            c0, c1 = 8 * hs[0], 8 * hs[-1] + 8
            w = X[:, 16:XW].indirect(T.yu[:, k, c0:c1])
            o = T.yy[:, 16 * c0:16 * c1]
            dve(cp(o, w) if k == 0 else tt(o, w, o, ALU.max), xk + [xn + "z"] + uk, yk, 16 * (c1 - c0), "g")

        def settle(k0, k1, t=t, kb=kb):
            p = "a" if k0 == 0 else "b"
            c0, c1 = 16 * k0, 16 * k1
            uk = ["yu%d_%d" % (k, h) for k in range(k0, k1) for h in (0, 1)]
            tl, ti = T["tl%d" % t], T["ti%d" % t]
            dve(ts(T.dead[:, c0:c1], T.yu[:, k0:k1, :], 0.0, ALU.is_equal), uk, ["dead" + p], (c1 - c0) / 2)
            n = 1 if k1 == 1 else 2
            dl, dlk = (T.dl0, "dl0") if k1 == 1 else (T.dl, "dl")
            dve(tt(tl[:, c0:c1], dl[:, c0:c1], T.dead[:, c0:c1], ALU.mult), [dlk, "dead" + p], ["tl%s_%d" % (p, t)], 2 * (c1 - c0))
            if n == 2:
                dve(tt(ti[:, c0:c1], T.di[:, c0:c1], T.dead[:, c0:c1], ALU.mult), ["di", "dead" + p], ["ti%s_%d" % (p, t)], 2 * (c1 - c0))
            old = (T.lf, T.if0) if t == 0 else (T.l1, T.i1)
            land = (T.l1, T.i1) if t == 0 else (T.l2, T.i2)
            send(2 * t + (k0 > 0), T.cores[(rank + 1 - 2 * t) % n_ranks],
                 [([a[:, c0:c1], b[:, c0:c1]], c[:, c0:c1]) for a, b, c in zip(old, (tl, ti), land)][:n],
                 kb + ["tl%s_%d" % (p, t), "ti%s_%d" % (p, t)][:n], ["st%d%s" % (t + 1, p)])

        for k in range(6):
            part = min(k, 1)
            if t == 1 and k == 1:
                prep(16, 96, (1,), kb)
                masks(kb)
            if k == 1:
                act(lin(T.w2[:], L[:], 2048.0), kb, ["w1", "w2"], 96)
                dve(tt(T.w2[:], T.w2[:], T.kt[:], ALU.add), ["kt"], ["w2"], 192)
            if t == 1 and k in (1, 3, 5):
                xl(k, min(k + 2, 6))
            for h in (0, 1):
                phase[0] = 12 * t + 2 * k + h

                def B(n, h=h):
                    return T["%s_%d" % (n, h)]

                def K(n, h=h):
                    return "%s_%d" % (n, h)
                pk, pkk = T["pk%d" % h], "pk%d" % h
                pz, pzk = T["pz%d" % h], "pz%d" % h
                pq = T["pq%d" % h]
                c0 = NS * (16 * k + 8 * h)
                n9 = 8 * NS
                ss = B("ss")
                cfg = dict(CFG, **CFG["at"].get((t, k, h), {}))
                mk = ["mk%d" % s for s in range(6)] if (k or not t) else []
                dve(tt(B("pr")[:], T.mm[:, c0:c0 + n9], pz[:, BZ:BZ + n9], ALU.mult), mmk + mk + ["mw%d" % part, pzk], [K("pr")], n9)
                dve(scan(ss[:, n9:2 * n9], T.d0[:, c0:c0 + n9], B("pr")[:], ALU.mult, ALU.add), ["d0%d" % part, K("pr")], [K("ss")], n9)
                dve(tt(ss[:, 6:n9:NS], ss[:, n9 + 7::NS], ss[:, n9 + 9::NS], ALU.subtract), [K("ss")], [K("sr")], 16)
                dve(ts(B("nb")[:], ss[:, 6::NS], 1.0 / 32, ALU.mult, 1024 - 31.0 / 64, ALU.add), [K("ss"), K("sr")], [K("nb")], 16)
                c1 = cfg["cu"]
                dve(cp(B("cu")[:, 0:16 * c1], T.fi[:].indirect(B("nb")[:, 0:c1])), ["fi", "fie", K("nb")], [K("cu")] + [K("cw")] * (c1 == 8), 16 * c1, "g")
                if c1 < 8:
                    dve(cp(B("cu")[:, 16 * c1:128], T.fi[:].indirect(B("nb")[:, c1:8])), ["fi", "fie", K("nb")], [K("cw")], 128 - 16 * c1, "g")
                x0 = 256 * k + 128 * h
                dve(tt(B("q")[:], X[:, 0:XW].indirect(B("nb")[:, 8:16]), T.xl[:, x0:x0 + 128], ALU.max),
                    xk + [xn + "s", xn + "z", K("nb"), "xl%d_%d" % (k, h)], [K("q")], 128, "g")
                dve(ts(B("fg")[:], B("cu")[:], -MID, ALU.add), [K("cu"), K("cw")], [K("fg")], 64)
                pe(mat(pk[:, 0:8 * KS], T.onb[0:65, :], T.cr[0:65, :], True, False), ["onb"] + crk, [pkk], 160)
                b2, b3 = cfg["b2"], cfg["b3"]
                low = [0, 0, b2, b3]

                def parts(a, split):
                    cut = [a] + [c for c in (64, 96) if a < c and (a == 32 if c == 64 else split)] + [128]
                    return list(zip(cut, cut[1:])) if a < 128 else []
                sums = [K("kt"), K("kq")]
                pe(mat(pk[:, 16:8 * KS:KS], T.onb[0:8, :], T.thm[0:8, 8 * k:8 * k + 8], False, False), ["onb", "th%d" % k, pkk], [K("kt")], 64)
                pe(mat(pk[:, 0:8 * KS], B("q")[:], T.gq2[:], False, False), [K("q"), "gq20", "gq21", pkk], [K("kq")], 160)
                for j in (2, 3):
                    for a, b in parts(low[j], False) if low[j] else []:
                        sums.append(K("kr%d%d" % (j, a)))
                        pe(mat(pk[a:b, j:8 * KS:4], B("q")[:, a:b], T.gq4[:, j::4], False, False), [K("q"), "gq4", pkk], sums[-1:], max(40, min(64, b - a)))
                pd = T["pd%d" % h]
                if b2 == b3 <= 64:
                    banks = [(pq, K("pq"), 0, (), 128), (pd, K("pd"), 0, (2, 3), b2)]
                else:
                    banks = [(pq, K("pq"), 0, (), 128), (pd, K("pd"), 0, (3,), b3), (pz, pzk, 128, (2,), b2)][:3 if b2 else 2]
                for bank, key, p0, js, b in banks:
                    def four(B=B, bank=bank, p0=p0, b=b, n=4 * max(1, len(js)), stop=not js):
                        for i in range(n):
                            p = p0 + 4 * b * (i // 4)
                            ins = P.matmul(bank[:, p + i % 4:p + 4 * b:4], T.idb[:], B("q")[:, 0:b], i == 0, stop and i == n - 1)
                        return ins
                    pe(four, [K("q"), "idb"], [K("fq%d" % sum(js)), key], 4 * max(64, b) * max(1, len(js)), 4)
                for i, (eng, a, b) in enumerate(cfg["cuts"]):
                    o, w = B("v")[:, 16 * a:16 * b], X[:, XO:XW].indirect(B("cu")[:, a:b])
                    ck = [K("cu")] * (a < 16 * c1) + [K("cw")] * (b > 16 * c1)
                    if eng == "dve":
                        dve(cp(o, w), xk + ck, [K("v%d" % i)], 16 * (b - a), "g")
                    else:
                        act(lambda o=o, w=w: S.activation(o, w, ACT.Copy), xk + ck, [K("v%d" % i)], 16 * (b - a), "g")

                def vkeys(c, d):
                    return [K("v%d" % i) for i, (eng, a, b) in enumerate(cfg["cuts"]) if a < d and b > c]
                ak = [[] for j in range(4)]
                for i, (a, b) in enumerate(cfg["runs"]):
                    for j in range(4):
                        e = max(a, low[j])
                        if e < b:
                            dve(tt(B("a")[:, j, 4 * e:4 * b], pq[:, 4 * e:4 * b], B("v")[:, 16 * e + j:16 * b:4], ALU.max),
                                [K("pq")] + vkeys(e, b), [K("a%d%d" % (j, i))], 4 * (b - e))
                            ak[j].append((K("a%d%d" % (j, i)), e, b))
                for bank, key, p0, js, top in banks[1:]:
                    runs = [(x, a, min(b, top)) for a, b in cfg["druns"] if a < top for x in range(len(js))]
                    for x, a, b in runs:
                        p = p0 + 4 * top * x
                        pe(mat(bank[:, p + 4 * a:p + 4 * b], T.nid[:], B("v")[:, 16 * a + js[x]:16 * b:4], False, (x, a, b) == runs[-1]),
                           vkeys(a, b) + ["nid"], [K("dv%d" % js[x]), key], max(64, 4 * (b - a)))
                    act(lambda B=B, bank=bank, p0=p0, js=js, top=top: S.activation(
                        B("a")[:, js[0]:js[-1] + 1, 0:4 * top], bank[:, p0:p0 + 4 * top * len(js)], ACT.Abs, scale=0.5),
                        [key], [K("ab%d" % js[0])], 4 * top * len(js))
                    for j in js:
                        ak[j].append((K("ab%d" % js[0]), 0, top))

                def lanes(pk, a, b, src, w):
                    for m, lhs in src:
                        ins = P.matmul(pk[a:b, m:8 * KS:KS], lhs, w, False, False)
                    return ins
                for j in range(4):
                    for a, b in parts(low[j], cfg["skv"]):
                        sums.append(K("kv%d%d" % (j, a)))
                        pe(lambda B=B, pk=pk, j=j, a=a, b=b: lanes(pk, a, b, [(m, B("v")[:, 16 * a + m:16 * b:16]) for m in range(j, 16, 4)], T.gv[:]),
                           vkeys(a, b) + ["gv", pkk], sums[-1:], 4 * min(64, b - a), 4)
                for j in range(4):
                    for a, b in parts(0, j in cfg["ska"]):
                        sums.append(K("ka%d%d" % (j, a)))
                        pe(lambda B=B, pk=pk, j=j, a=a, b=b: lanes(pk, a, b, [(j + 4 * i, B("a")[:, j, 4 * a + i:4 * b:4]) for i in range(4)], T.g8[:]),
                           [key for key, c, d in ak[j] if c < b and d > a] + ["g8", pkk], sums[-1:], 4 * min(64, b - a), 4)
                if cfg["fg4"]:
                    for j in range(3):
                        pe(mat(pk[:, j:8 * KS:4], B("fg")[:], T.idk[:, j::4], False, False),
                           [K("fg"), "idk", pkk] + [x for x in sums if x[1] == "q" or x[2] == str(j)], [K("kf%d" % j)], 64)
                    pe(mat(pk[:, 3:8 * KS:4], B("fg")[:], T.idk[:, 3::4], False, True),
                       [K("fg"), "idk"] + sums + [K("kf%d" % j) for j in range(3)], [pkk], 64)
                else:
                    pe(mat(pk[:, 0:8 * KS], B("fg")[:], T.idk[:], False, True), [K("fg"), "idk"] + sums, [pkk], 160)
                dve(scan(B("sc")[:], T.rs[:], pk[:, 0:8 * KS], ALU.add, ALU.min), ["rs0", "rs1", "rs2", pkk], [K("sc")], 8 * KS)
                dve(tt(B("lo")[:], B("sc")[:, 16::KS], B("sc")[:, 18::KS], ALU.subtract), [K("sc")], [K("lo")], 16)
                dve(tt(B("rx")[:], B("lo")[:].indirect(T.eo[:]), T.ma[:], ALU.mult), [K("lo"), "eo", "ma"], [K("rx")], 128, "g")
                if k < 5:
                    pe(mat(pz[:, BZ + k + 1:BZ + n9:NS], B("rx")[:], T.bm32[:], True, True), [K("rx"), "bm32"], [K("zb"), pzk], 64)
                pe(mat(pk[:, BK + 8 * k:BK + 8 * k + 8], B("rx")[:], T.bm[:], True, True), [K("rx"), "bm"], [K("zk"), pkk], 64)
                if k in YROWS:
                    ylist(YROWS[k][0], k + 1, h)
                if k == 4:
                    bz, z0 = pz[:, BZ:BZ + n9], n9 * h
                    dve(ts(T.dx[:, z0:z0 + n9], bz, -32 * DEAD - 500, ALU.add, -1.0e4, ALU.mult), [pzk], [K("dx")], n9)
                    dve(ts(T.ds[:, z0:z0 + n9], bz, 32 * DEAD, ALU.is_equal), [pzk], [K("ds")], n9)
                    dve(scan(T.sb[:, z0:z0 + n9], T.dx[:, z0:z0 + n9], bz, ALU.min, ALU.max), [pzk, K("dx")], [K("sb")], n9)
                if k < 5:
                    continue
                ylist(5, 6, h)
                ymax(5, [h])

                pe(mat(pk[:, 0:48], T.onb[0:1, :], T.cw[0:1, :], True, False), ["onb", "cw0", "cw1", "cw2"], [K("s0"), pkk], 64)
                pe(mat(pk[:, 3:48:6], T.p16[0:1, :], T.onb[0:1, 0:8], False, False), ["onb", "p16"], [K("s1"), pkk], 64)
                pe(mat(pk[:, 0:48:3], T.yy[:, 128 * h:128 * h + 128], T.wg[:], False, True), ["yy%d" % h, "wg"], [K("s2"), pkk], 64)
                dve(scan(B("sp")[:], T.d6[:], pk[:, 0:48], ALU.mult, ALU.add), ["d60", "d63", pkk], [K("sp")], 48)
                dve(tt(B("rx")[:], B("sp")[:].indirect(T.e6[:]), T.ma[:], ALU.mult), [K("sp"), "e6", "ma"], [K("ry"), K("rx")], 128, "g")
                pe(mat(pz[:, SP:SP + 8], B("rx")[:], T.bm[:], True, True), [K("rx"), "bm"], [K("zs"), pzk], 64)
                dve(cp(B("pu")[:], pz[:, SP:SP + 8]), [pzk], [K("pu")], 8)
                on = "xa" if (t == 1 and h == 0) else "xb"
                w0 = XO + 2048 * h
                dve(cp(T[on][:, w0:w0 + 2048].indirect(B("pu")[:]), T.yy[:, 128 * h:128 * h + 128]),
                    [K("pu"), "yy%d" % h], [K("put"), "%s%d" % (on, h)], 128, "s")
                if t == 1:
                    dma("sp", T.yx[:, 2048 * h:2048 * h + 2048], T[on][:, w0:w0 + 2048], ["%s%d" % (on, h)], ["yx%d" % h], 2000)
            for j in YROWS.get(k, ()):
                ymax(j, [0, 1])
            if k == 4:
                dve(scan(T.sr[:], T.ds[:], T.ds[:], ALU.mult, ALU.subtract), ["ds_0", "ds_1"], ["run"], 160)
                dve(tt(T.bp[:], T.sb[:].indirect(T.po[:, 0:6]), T.d0[:, 7::NS], ALU.mult), ["sb_0", "sb_1", "po", "d00", "d01"], ["bp"], 96, "g")
                dve(tt(T.zr[:], T.bp[:], T.w2[:], ALU.add), ["bp", "w2"], ["zr"], 192)
                dve(ts(T.nl[:], T.zr[:], 5, ALU.arith_shift_right, 4095, ALU.bitwise_and), ["zr"], ["nl"], 96)
                dve(tt(T.dl[:], T.nl[:], L[:], ALU.subtract), kb + ["nl"], ["dl"], 192)
                dve(tt(T.aa[:], T.ki[:], I[:], ALU.subtract), kb + ["ki"], ["aa"], 192)
                dve(tt(T.di[:], T.sr[:].indirect(T.po[:, 0:6]), T.aa[:], ALU.add), ["run", "po", "aa"], ["di"], 96, "g")
                if t == 1:
                    settle(0, 5)
            if t == 0 and 0 in YROWS.get(k, ()):
                dve(tt(T.b0[:], T.d0[:, 7:16 * NS:NS], T.ex32[:], ALU.mult), ["d00", "ex32"], ["b0"], 32)
                dve(tt(T.z0[:], T.b0[:], T.w2[:, 0:16], ALU.add), ["b0", "w2"], ["z0"], 32)
                dve(ts(T.n0[:], T.z0[:], 5, ALU.arith_shift_right, 4095, ALU.bitwise_and), ["z0"], ["n0"], 16)
                dve(tt(T.dl0[:], T.n0[:], L[:, 0:16], ALU.subtract), kb + ["n0"], ["dl0"], 32)
                settle(0, 1)
        settle(5 if t else 1, 6)
        if t == 0:
            pd, pdk = T.pd1, "pd_1"
            pe(mat(pd[:, 0:96], T.onb[:], T.dead[:], True, True), ["onb", "deada", "deadb"], ["cp", pdk], 96)
            dve(lambda pd=pd: V.tensor_reduce(T.cn[:, 0:1], pd[:, 0:96], AxisListType.X, ALU.add), [pdk], ["cn"], 96)
            dve(cp(T.ci[:, 0:1], T.cn[:, 0:1]), ["cn"], ["ci"], 1)
            dve(ts(T.cj[:, 0:1], T.ci[:, 0:1], 31, ALU.bitwise_and), ["ci"], ["cj"], 1)
            dve(ts(T.cf[:, 0:1], T.cj[:, 0:1], -120.0, ALU.add), ["cj"], ["cf"], 1)
            dve(ts(T.cr[64:65, 16::KS], T.onb[64:65, 0:8], T.cf[64:65, 0:1], ALU.mult, DW, ALU.mult), ["cf", "onb"], ["ca"], 8)
        else:
            dma("act", T.yl[:], T.l2[:], ["st2a", "st2b"], ["yl"], 150)
            dma("act", T.yi[:], T.i2[:], ["st2a", "st2b"], ["yi"], 150)
    return ops


def depend(ops):
    last_w, readers, deps = {}, {}, []
    for i, o in enumerate(ops):
        d = set()
        for k in o["r"]:
            if k in last_w:
                d.add(last_w[k])
        for k in o["w"]:
            if k in last_w:
                d.add(last_w[k])
            d.update(readers.get(k, []))
        for k in o["r"]:
            readers.setdefault(k, []).append(i)
        for k in o["w"]:
            last_w[k] = i
            readers[k] = []
        d.discard(i)
        deps.append(sorted(d))
    return deps


def prices(ops, deps, m):
    cy, ga, sa, fixv, fixs, least, own, other, tensor, pc, second, slow = m
    out = []
    for o in ops:
        f, n = o["form"], o["n"]
        if f == "e":
            out.append((fixv if o["eng"] == "dve" else fixs) + max(least, n) * cy)
        elif f == "g" or f == "s":
            two = second if o["w"][0][:2] in ("yy", "q_", "rx", "ry", "bp", "di") else 0.0
            out.append((50.0 if o["eng"] == "dve" else 65.0) + n * cy * (ga + two if f == "g" else sa))
        elif f == "pe":
            out.append(n * pc)
        else:
            out.append(n)
    waits = []
    for o, d in zip(ops, deps):
        e = o["eng"]
        waits.append([(j, (0.0 if e == "pe" else own) if ops[j]["eng"] == e else tensor if ops[j]["eng"] == "pe" else other) for j in d])
    return out, waits, slow


def replay(ops, order, cost, waits, slow):
    end, free, wire = [0.0] * len(ops), {}, 0.0
    for i in order:
        o = ops[i]
        t = free.get(o["eng"], 0.0) if o["eng"] else 0.0
        for j, w in waits[i]:
            if end[j] + w > t:
                t = end[j] + w
        t += cost[i]
        free[o["eng"]] = t
        t += o["lat"]
        if o["kind"] == "dma" and o["m"]:
            wire = t = max(t, wire) + o["m"] * slow
        end[i] = t
    return end


def above(xs, x):
    lo, hi = 0, len(xs)
    while lo < hi:
        mid = (lo + hi) // 2
        if xs[mid] <= x:
            lo = mid + 1
        else:
            hi = mid
    return lo


def by_rank(pre, post, rank):
    left = [len(p) for p in pre]
    ready = sorted((-rank[i], -i) for i in range(len(pre)) if not left[i])
    out = []
    while ready:
        i = -ready.pop()[1]
        out.append(i)
        for j in post[i]:
            left[j] -= 1
            if not left[j]:
                x = (-rank[j], -j)
                ready.insert(above(ready, x), x)
    return out


def arrange(ops, deps):
    n = len(ops)
    eng = [o["eng"] for o in ops]
    succ = [[] for _ in ops]
    for i, d in enumerate(deps):
        for j in d:
            succ[j].append(i)
    costs = [prices(ops, deps, m) for m in COSTS]
    bus = [o["m"] if o["kind"] == "dma" else 0 for o in ops]
    seed = [CFG["seed"]]

    def rnd():
        seed[0] = (seed[0] * 1103515245 + 12345) % 2147483648
        return (seed[0] >> 8) / 8388608.0

    def length(order):
        return sum(max(replay(ops, order, *c)) / m[0] for c, m in zip(costs, COSTS)) / len(COSTS)

    def pack(rank, cost, hop, back):
        pre, post = (succ, deps) if back else (deps, succ)
        start, lo, hi = [0.0] * n, {}, {}
        for i in by_rank(pre, post, rank):
            e, r, c = eng[i], 0.0, cost[i]
            for j in pre[i]:
                a = e if back else eng[j]
                x = start[j] + cost[j] + (lat[i] if back else lat[j]) + \
                    ((0.0 if e == "pe" else hop[0]) if e == eng[j] else hop[2] if a == "pe" else hop[1])
                if x > r:
                    r = x
            if e:
                a, b = lo.setdefault(e, []), hi.setdefault(e, [])
                k = above(b, r)
                while k < len(a) and r + c > a[k] + 1e-9:
                    r = max(r, b[k])
                    k += 1
                a.insert(k, r)
                b.insert(k, r + c)
            start[i] = r
        return start
    loads = [i for i in range(n) if ops[i]["kind"] == "dma" and ops[i]["first"]]
    lat = [o["lat"] + b for o, b in zip(ops, bus)]
    wire = 0.0
    for i in loads:
        wire += 0.65 * bus[i]
        lat[i] = ops[i]["lat"] + (wire if bus[i] else 0.0)
    now = best = list(range(n))
    tnow = tbest = length(best)
    for it in range(CFG["rounds"]):
        w = [rnd() + 0.01 for _ in COSTS]
        w = [x / sum(w) for x in w]
        amp = CFG["amp"][0] + (CFG["amp"][1] - CFG["amp"][0]) * it / CFG["rounds"]
        f = {e: 1 + amp * (2 * rnd() - 1) for e in QUEUES}
        cost = [sum(x * c[0][i] for x, c in zip(w, costs)) * f[eng[i]] * (1 + amp * (2 * rnd() - 1)) for i in range(n)]
        if it % CFG["back"] == 0:
            now, tnow = best, tbest
        hop = [sum(x * m[j] for x, m in zip(w, COSTS)) for j in (6, 7, 8)]
        at = [0] * n
        for k, i in enumerate(now):
            at[i] = k
        fore = pack(at, cost, hop, False)
        for rep in range(2):
            back = pack([-(fore[i] + cost[i] + lat[i]) for i in range(n)], cost, hop, True)
            rank = [-(back[i] + cost[i]) for i in range(n)]
            for k, i in enumerate(loads):
                rank[i] = k - 1.0e12
            fore = pack(rank, cost, hop, False)
            order = by_rank(deps, succ, fore)
            x = length(order)
            if x < tnow + CFG["slack"]:
                now, tnow = order, x
            if x < tbest:
                best, tbest = order, x

    def starts(order):
        end = replay(ops, order, *costs[0])
        out = [end[i] - costs[0][0][i] - ops[i]["lat"] - bus[i] for i in range(n)]
        for k, i in enumerate(loads):
            out[i] = k - 1.0e12
        return out

    def pick(xs):
        return xs[int(rnd() * len(xs))]
    kinds = {}
    for i, o in enumerate(ops):
        kinds.setdefault(o["w"][0].rsplit("_", 1)[0], []).append(i)
    names = sorted(k for k in kinds if len(kinds[k]) >= 12)
    at = starts(best)
    for it in range(CFG["moves"]):
        rank = list(at)
        if rnd() < 0.5:
            d, lo, span = pick((-600, -300, -150, -60, 60, 150, 300, 600)), int(24 * rnd()), pick((1, 2, 4, 99))
            for i in kinds[pick(names)]:
                if span == 99 or lo <= ops[i]["ph"] < lo + span:
                    rank[i] += d
        else:
            for _ in range(pick((1, 2))):
                rank[int(n * rnd())] += pick((-3000, -1000, -300, -100, 100, 300, 1000, 3000))
        order = by_rank(deps, succ, rank)
        x = length(order)
        if x <= tbest:
            best, tbest, at = order, x, starts(order)
    return best, tbest


def plan(ops):
    deps = depend(ops)
    order = arrange(ops, deps)[0]
    at = {i: n for n, i in enumerate(order)}
    pos, cnt = {}, {}
    for i in order:
        o = ops[i]
        if o["kind"] == "c":
            cnt[o["eng"]] = cnt.get(o["eng"], 0) + 1
            pos[i] = (o["eng"], cnt[o["eng"]])
        else:
            pos[i] = (o["sem"], o["val"])
    known, clock, waits, marked = {}, {}, {}, set()
    for i in order:
        o = ops[i]
        if o["kind"] == "recv":
            clock[i] = {}
            continue
        kn = known.setdefault(o["eng"], {})
        ws = []
        for j in sorted(deps[i], key=lambda j: -at[j]):
            if o["eng"] == "pe" and ops[j]["eng"] == "pe":
                continue
            s, v = pos[j]
            if kn.get(s, 0) >= v:
                continue
            ws.append(j)
            marked.add(j)
            kn[s] = v
            for a, b in clock[j].items():
                if kn.get(a, 0) < b:
                    kn[a] = b
        waits[i] = ws
        clock[i] = dict(kn)
    value, cnt = {}, {}
    for i in order:
        o = ops[i]
        if o["kind"] == "c":
            if i in marked:
                cnt[o["eng"]] = cnt.get(o["eng"], 0) + 1
                value[i] = (o["eng"], cnt[o["eng"]])
        else:
            value[i] = (o["sem"], o["val"])
    return order, waits, marked, value


PLAN = {}


def rank_program(g, core, T, topo):
    if T.rank_of(core) is None:
        return
    ops = build(g, core, T, topo)
    if "p" not in PLAN:
        PLAN["p"] = plan(ops)
    order, waits, marked, value = PLAN["p"]
    queue = {"pe": g.tensor, "dve": g.vector, "act": g.scalar, "pool": g, "sp": g.sync}
    for i in order:
        o = ops[i]
        if o["kind"] == "recv":
            continue
        q = queue[o["eng"]]
        for j in waits[i]:
            s, v = value[j]
            q.wait_ge(T.sem[s], v)
        ins = o["fn"]()
        if o["kind"] == "dma":
            ins.then_inc(T.sem[o["sem"]], 16)
        elif o["kind"] == "c" and i in marked:
            ins.then_inc(T.sem[o["eng"]], 1)
    for i in order:
        o = ops[i]
        if o["kind"] != "c" and i not in marked:
            g.wait_ge(T.sem[o["sem"]], o["val"])
